import numpy as np, ml_dtypes
CORES = [2,6,10,14,18,22,26,30]
N = 8
BF = ml_dtypes.bfloat16
W, S, M, CAP, RO, DX = 8192, 512, 16, 64, 4, 4
def places(g, w, k):
    u = np.add.reduce(w[..., :, None] * g, axis=-2) & 4095
    return ((u * u >> 5)[..., None, :] + k[..., :, None] * u[..., None, :]) & (W - 1)
def parts(rng):
    return (rng.integers(0, 256, (N, 8, 16, W), dtype=np.int32), rng.integers(0, 256, (N, 8, 16, S)), rng.integers(0, 256, (N, 8, 16, RO)),
            rng.integers(0, 3969, (N, 8, M)), rng.integers(620, 1000, (N, 8)))
def pack(x, g, w, k, t):
    return {"xs": x.reshape(N, 128, W).astype(np.float32).astype(BF), "gd": g.reshape(N, 128, S).astype(np.float32).astype(BF), "wt": w.reshape(N, 128, RO).astype(np.int32),
            "km": np.repeat(k, 16, axis=1).astype(np.int32), "th": np.repeat(t, 16, axis=1)[:, :, None].astype(np.int32)}
def plant(x, g, j, c, i, d):
    v = 255 - g[:, j]; n = np.arange(len(j)); a = v[i, n]
    v[i, n] = np.where(a < 128, a + d, a - d); x[:, c] = v
def lone(rng, x, g, w, k, s0, s1, lo, hi):
    c = places(g, w, k)[:, s0:s1]; m, j = np.nonzero((c >= lo) & (c < hi))
    if len(m):
        i = int(rng.integers(0, len(m))); x[:, c[m[i], j[i]]] = 255 - g[:, s0 + j[i]]
def setup_inputs(rng):
    x, g, w, k, t = parts(rng); h = rng.integers(0, 8)
    t[0, h] = 995; t[1, h] = 620; t[DX, h] = 620
    return pack(x, g, w, k, t)
def setup_inputs_room(rng):
    x, g, w, k, t = parts(rng); t = rng.integers(60, 129, (N, 8)); k = np.minimum(k | 1, 3967)
    for q in range(N):
        room = rng.permutation(np.array([0, 1, CAP - 1, CAP, CAP + 1, 2 * CAP, 0, CAP]))
        for h in range(8):
            c = places(g[q, h], w[q, h, :, 0], k[q, h])[rng.integers(0, M, S), np.arange(S)]
            o = rng.permutation(S); o = o[c[o] < W - 96]; first = np.unique(c[o], return_index=True)[1]
            o = o[np.sort(first)][:int(room[h])]; n = len(o)
            plant(x[q, h], g[q, h], o, c[o], rng.integers(0, 16, n), rng.integers(0, t[q, h], n))
    return pack(x, g, w, k, t)
def setup_inputs_ties(rng):
    x, g, w, k, t = parts(rng)
    w[:, :, 2, 0] = w[:, :, 1, 0]; g[:, :, 1] = np.minimum(g[:, :, 1], 254); g[:, :, 2] = np.maximum(g[:, :, 2], 1)
    for q in range(N):
        for h in (0, 2, 4, 6):
            n = int(rng.choice(np.array([CAP // 4, CAP // 2, CAP]))); t[q, h] = 3 if h == 2 * (q % 4) else rng.integers(1, 4)
            o = rng.permutation(S); a = np.minimum(o[:n], o[n:2 * n]); b = np.maximum(o[:n], o[n:2 * n]); e = o[2 * n:3 * n]
            kd = rng.integers(0, 4, n); kd[:4] = np.arange(4); s = (kd > 0).astype(np.int64)
            v = g[q, h][:, a].copy(); v[1] += s; v[2] -= s; g[q, h][:, b] = v
            c = places(g[q, h], w[q, h, :, 0], k[q, h])
            ca = c[rng.integers(0, M, n), a]; m = rng.integers(0, M, n); c1 = c[m, e]; c2 = c[(m + rng.integers(1, M, n)) % M, e]
            al = np.concatenate([ca, c1, c2]); one = np.bincount(al, minlength=W)[al] == 1
            pa = one[:n] & (ca < W - 96); pe = one[n:2 * n] & one[2 * n:]
            v = 255 - g[q, h][:, a]; v[1] -= ((kd == 1) | (kd == 2)).astype(np.int64); v[2] += (kd == 1).astype(np.int64); x[q, h][:, ca[pa]] = v[:, pa]
            i = rng.integers(0, 16, n); d = rng.integers(0, t[q, h], n)
            plant(x[q, h], g[q, h], e[pe], c1[pe], i[pe], d[pe]); plant(x[q, h], g[q, h], e[pe], c2[pe], i[pe], d[pe])
    a = int(rng.integers(0, S // 4)); b = a + int(rng.integers(1, S // 4))
    w[:, 1, :, 0] = 0; w[:, 1, 0, 0] = 1; k[:, 1, 0] = 0; k[:, 1, 1] = 3; t[:, 1] = 20
    g[:, 1, :, b] = g[:, 1, :, a].copy(); g[:, 1, 0, a] = 32; g[:, 1, 0, b] = 64
    x[:, 1, :, 128] = 255 - g[:, 1, :, a]; x[:, 1, 0, 128] = 207
    return pack(x, g, w, k, t)
def setup_inputs_ends(rng):
    x, g, w, k, t = parts(rng); o = rng.permutation(8); w[:, :, 0, 0] |= 1
    low = rng.integers(0, 192, (N, 4, W)); few = rng.integers(0, 64, (N, W)) == 0
    x[:, o[0], 0] = low[:, 0]; x[:, o[1], 0] = rng.integers(192, 256, (N, W))
    x[:, o[2], 0] = low[:, 1]; x[:, o[2], 0, 0] = 192; x[::2, o[2], 0, W - 1] = 255
    x[1::2, o[2], 0, W - 40] = 192; x[1::2, o[2], 0, W - 20] = 192
    x[:, o[3], 0, W // 2:] = low[:, 2, W // 2:]; x[:, o[4], 0] = np.where(few, 192, low[:, 3])
    x[:, o[6], 0, W - 81:] = low[:, 0, W - 81:]; x[:, o[7], 0, W - 81:] = low[:, 1, W - 81:]; x[:, o[7], 0, W - 4] = 192
    t[::2, o[0]] = 4080; t[1::2, o[0]] = 4; t[1::2, o[2]] = 4
    for q in range(1, N, 2):
        lone(rng, x[q, o[0]], g[q, o[0]], w[q, o[0], :, 0], k[q, o[0]], 0, S // 4, W // 2, W - 96)
        lone(rng, x[q, o[0]], g[q, o[0]], w[q, o[0], :, 1], k[q, o[0]], S // 4, S - 3 * CAP, 0, W // 4)
        lone(rng, x[q, o[2]], g[q, o[2]], w[q, o[2], :, 0], k[q, o[2]], 0, S, 0, W // 4)
    for q in range(N):
        for h in o[5:]:
            u = np.add.reduce(w[q, h, :, 0][:, None] * g[q, h], axis=0) & 4095; used = []
            for m, c in enumerate((W - 97, W - 96, 0)):
                for j in range(S):
                    if u[j] & 1 and j not in used:
                        v = int(u[j]); kk = (c - (v * v >> 5)) * pow(v, -1, W) % W
                        if kk <= 3968:
                            k[q, h, m] = kk; used.append(j)
                            plant(x[q, h], g[q, h], np.array([j]), np.array([c]), np.array([3 + m]), np.array([m])); break
    return pack(x, g, w, k, t)
def setup_inputs_alike(rng):
    x, g, w, k, t = parts(rng); o = rng.permutation(8)
    g[:, o[0]] = g[:, o[0], :, :1].copy()
    for q in range(N):
        c = places(g[q, o[0]], w[q, o[0], :, 0], k[q, o[0]])[:, 0]; m = np.flatnonzero(c < W - 96)[:1]
        plant(x[q, o[0]], g[q, o[0]], np.zeros(len(m), np.int64), c[m], m, np.full(len(m), 3))
    w[:, o[1]] = 0
    for q in range(N):
        e = np.arange(1, CAP + 1); d = np.append(e[::-1] if q % 2 == 0 else e, 0); n = np.arange(CAP + 1); i = rng.integers(0, 16, CAP + 1)
        v = np.repeat(255 - x[q, o[1], :, :1], CAP + 1, axis=1); a = v[i, n]
        v[i, n] = np.where(a < 128, a + d, a - d); g[q, o[1], :, :CAP + 1] = v
    k[:, o[2]] = k[:, o[2], :1].copy()
    g[:, o[3]] = g[:, o[3]][:, :, rng.integers(0, 4, S)]
    b = x[:, o[4], :, :8].copy(); b[:, 0, 0] = 200
    x[:, o[4]] = b[:, :, rng.integers(0, 8, W)]; g[:, o[4]] = 255 - b[:, :, rng.integers(0, 8, S)]
    k[:, o[5]] = rng.choice(np.array([0, 1, 3968]), (N, M))
    x[:, o[6]] = 255 * rng.integers(0, 2, (N, 16, W)); g[:, o[6]] = 255 * rng.integers(0, 2, (N, 16, S))
    w[:, o[7], :, 0] = 0; w[:, o[7], 0, 0] = 1; k[:, o[7]] = rng.integers(0, 8, (N, M)); t[:, o[7]] = 4080
    g[:, o[7], 0] = np.minimum(g[:, o[7], 0], 254); g[:, o[7], 0, S - 1] = 255
    for q in range(N):
        c = int(places(g[q, o[7]], w[q, o[7], :, 0], k[q, o[7]])[0, S - 1]); x[q, o[7], :, c] = 255 - g[q, o[7], :, S - 1]
    return pack(x, g, w, k, t)
def setup_inputs_spread(rng):
    x, g, w, k, t = parts(rng)
    def uneven(n):
        v = np.minimum((np.exp2(8 * rng.random((N, 8, 1, n))) * rng.random((N, 8, 16, n))).astype(np.int64), 255)
        return np.where(rng.random((N, 8, 1, n)) < 0.5, v, 255 - v)
    x = uneven(W); g = uneven(S)
    w = np.minimum(np.exp2(8 * rng.random(w.shape)).astype(np.int64), 255); k = np.minimum(np.exp2(12 * rng.random(k.shape)).astype(np.int64), 3968)
    t = np.minimum(np.maximum(np.exp2(12 * rng.random((N, 8))).astype(np.int64), 1), 4080); t[:, rng.integers(0, 8)] = rng.integers(1500, 2500, N)
    return pack(x, g, w, k, t)
def check_inputs(d):
    bad = []
    for n, lo, hi in (("xs", 0, 255), ("gd", 0, 255), ("wt", 0, 255), ("km", 0, 3968), ("th", 1, 4080)):
        a = np.asarray(d[n]).astype(np.float64)
        if not np.all((a >= lo) & (a <= hi) & (np.floor(a) == a)): bad.append("range of " + n)
    for n in ("km", "th"):
        a = np.asarray(d[n]).reshape(N, 8, 16, -1)
        if np.any(a != a[:, :, :1]): bad.append("rows of a group alike in " + n)
    return bad
def reference(xs, gd, wt, km, th):
    x = xs.astype(np.float32).astype(np.int32).reshape(N, 8, 16, W); g = gd.astype(np.float32).astype(np.int32).reshape(N, 8, 16, S)
    w = wt.astype(np.int64).reshape(N, 8, 16, RO); k = km.astype(np.int64).reshape(N, 8, 16, M)[:, :, 0]; t = th.astype(np.int64).reshape(N, 8, 16)[:, :, 0]
    log = np.zeros((N, 8, W), np.int64); place = np.arange(W); slot = np.arange(S); rows = np.arange(8)[:, None]
    for rnd in range(RO):
        cuts = []; gives = []; nx = []
        for a in range(N):
            c = places(g[a], w[a, :, :, rnd], k[a])
            v = np.take_along_axis(x[a], c.reshape(8, 1, M * S), 2).reshape(8, 16, M, S)
            D = np.add.reduce(np.abs(g[a][:, :, None, :] + v - 255), axis=1)
            m = np.argmin(D, axis=1)[:, None]
            D = np.take_along_axis(D, m, 1)[:, 0].astype(np.int64); c = np.take_along_axis(c, m, 1)[:, 0]
            fit = (D < t[a][:, None]) & (c < W - 96)
            cand = fit & (np.add.accumulate(fit.astype(np.int64), axis=1) <= CAP)
            key = D * S + slot; low = np.full((8, W), 2 ** 40, np.int64)
            np.minimum.at(low, (rows, c), np.where(cand, key, 2 ** 40))
            cut = cand & (np.take_along_axis(low, c, 1) == key)
            ok = (x[a][:, 0] >= 192) & (x[a][:, 0] <= 255)
            U = np.minimum.accumulate(np.where(ok, place, W - 1)[:, ::-1], axis=1)[:, ::-1]
            e1 = np.take_along_axis(U, np.minimum(c + 16, W - 1), 1); e2 = np.take_along_axis(U, np.minimum(e1 + 8, W - 1), 1)
            gives.append([np.maximum(255 - np.take_along_axis(x[a], e[:, None, :], 2), 0) for e in (np.minimum(c + 10, W - 1), e1, e2)])
            reach = np.full((8, W), -1, np.int64); np.maximum.at(reach, (rows, c), np.where(cut, e2, -1))
            gone = np.maximum.accumulate(reach, axis=1) >= place
            log[a] = np.where(gone & (log[a] == 0), rnd + 1, log[a])
            nx.append(np.where(gone[:, None, :], np.int32(512), x[a])); cuts.append(cut)
        ng = []
        for a in range(N):
            p, q = a ^ 1, a ^ DX
            every = np.concatenate([gives[p][0], gives[q][1], gives[q][2], g[a], g[a]], axis=2)
            there = np.concatenate([cuts[p], cuts[q], cuts[q], ~cuts[a], cuts[a]], axis=1)
            o = np.argsort(~there, axis=1, kind="stable")[:, :S]
            ng.append(np.take_along_axis(every, o[:, None, :], 2))
        x = np.stack(nx); g = np.stack(ng)
    return {"yg": g.reshape(N, 128, S).astype(np.float32).astype(BF), "yc": log.astype(np.float32)}

@@ -1,0 +1,626 @@
+from concourse.mybir import AluOpType as O, AxisListType, ActivationFunctionType as F
+
+RO = 4
+QW = 784
+QG = 208
+DW = 976
+BIG = 1.0e9
+
+_f = "x0c:512b okl:512 oks:512 Ut:512 RV1:512b SG:2560b Yt:512 Yu:512 idf:128 idb:128b BM:128b BMgf:8 tri:128b oneb:512b onef:512 O16:16b"
+_f += " tri2:128 BO2:128 id2:64 maskJ:512 i64b:64b i64f:64 mW:64 t32:32 z16:128 rs16:512 rs64:256 Kpat:512b Mpat:512b c16:128b c16f:128 thr:1 thS:32"
+_f += " Bpat:128b TriB:128b cm:128 Pm:128b Jm:128b pi:1i pj:1i rcol:1 b512:1 acol:1 iW:32 dW:4 aW:8 i512:512 rself:128 rselb:128b kA:16i kB:16i kAf:16 kBf:16"
+_f += " iM:16 slS:32i slL:32i tA:128 tB:128 X:8192b Urep:8256 A0:8192 Ab:8192b Gr0:1024b Gr1:1024b xs2:1024b wti:4i kmi:16i thi:1i wf:4 kf:16 Lw:2048b Lsel:2048b"
+_f += " Wf:8b Wff:8 ui:64i U:64i sq:64i Fi:64i UF:64 FF:64 UU:64 T0:256i T1:256i T1f:256 OT0:256u OT1:256u KS0:512 KS1:512 Ki:64i kp:64i pr:64 tt:32i tf:32 tc:32i CD:64i CDl:64i"
+_f += " VL:192b f1:32 f2:32 fit:32b rsel:32 OH:2048b Ls:24 cds:12 Vp:4 DG:512 EQ:256 SC:256 vm:4 win:4 E5:4 OE:264 rid:4 tmA:128 tmB:128 EW:8i cW:4i s1:8i tW:8 isl:4 q1:4 q2:4 q3:4"
+_f += " OFF:24u OFC:4u OFD:4u UG:128 xg:192b yv:192b mk:192b mP:72b mT:136b PL:8i hiI:8i loI:8i hiF:8 loF:8 HH:1024b sgn:4096b c511:1b bs:1 bA:1 bB:1 Dw:976b DS:512b sN:2b A1:1 mi:192 MI:32u"
+_f += " tot:1 dg:128 cmx:128 cry:1 Gn:512b"
+_dt = {"b": "bfloat16", "i": "int32", "u": "uint16"}
+_pool, _where, SCRATCH = {}, {}, {}
+for _x in _f.split():
+    _n, _c = _x.split(":")
+    _d = _dt.get(_c[-1], "float32")
+    _c = int(_c if _d == "float32" else _c[:-1])
+    if _c <= 264 and _n not in ("mP", "mT"):
+        _p = "pool_" + _d
+        _where[_n] = (_p, _pool.get(_p, 0), _c)
+        _pool[_p] = _pool.get(_p, 0) + (_c + 15) // 16 * 16
+        SCRATCH[_p] = ("sbuf", [128, _pool[_p]], _d)
+    else:
+        _where[_n] = (_n, 0, _c)
+        SCRATCH[_n] = ("sbuf", [128, _c], _d)
+for _t in range(RO):
+    SCRATCH["Q%d" % _t] = ("sbuf", [128, QW], "bfloat16")
+    _where["Q%d" % _t] = ("Q%d" % _t, 0, QW)
+for _t in range(8):
+    SCRATCH["B%d" % _t] = ("psum", [128, 512], "float32")
+    _where["B%d" % _t] = ("B%d" % _t, 0, 512)
+NDMA = 48
+SEMAPHORES = ["sv", "ss", "st", "sg"] + ["d%d" % _t for _t in range(NDMA)]
+for _t in range(RO):
+    SEMAPHORES += ["aP%d" % _t, "aT%d" % _t, "lP%d" % _t, "lT%d" % _t]
+
+
+def rank_program(g, core, T, topo):
+    rank = T.rank_of(core)
+    if rank is None:
+        return
+    queues = {"v": g.vector, "s": g.scalar, "t": g.tensor, "g": g, "y": g.sync}
+    own = {"v": "sv", "s": "ss", "t": "st", "g": "sg"}
+    count, log = {}, {}
+    known = {q: {} for q in queues}
+
+    def A(n, lo=0, hi=None, st=1, p0=0, p1=128, pst=1):
+        p, o, c = _where[n]
+        hi = c if hi is None else hi
+        hi = min(hi, lo + (hi - lo - 1) // st * st + 1)
+        ap = T[p][p0:p1:pst, o + lo:o + hi:st] if (pst != 1 or st != 1) else T[p][p0:p1, o + lo:o + hi]
+        return (ap, [(p, o + lo, o + hi, st, p0, p1)])
+
+    def IX(win, off):
+        return (win[0].indirect(off[0]), win[1] + off[1])
+
+    def hit(a, b):
+        if a[1] >= b[2] or b[1] >= a[2] or a[4] >= b[5] or b[4] >= a[5]:
+            return False
+        return not (a[3] == b[3] and a[3] > 1 and (a[1] - b[1]) % a[3])
+
+    def need(q, reads, writes):
+        w = {}
+        for regs, isw in ((reads, False), (writes, True)):
+            for r in regs:
+                bank = r[0][0] == "B" and r[0][1:].isdigit()
+                for (r2, w2, q2, sem, n, snap) in log.get(r[0], []):
+                    if q2 == q and q2 in own:
+                        if not (isw or w2) or not hit(r, r2) or (isw and q == "t"):
+                            continue
+                    elif not bank and (not (isw or w2) or not hit(r, r2)):
+                        continue
+                    if known[q].get(sem, 0) < n and w.get(sem, (0,))[0] < n:
+                        w[sem] = (n, snap)
+        for sem in sorted(w, key=lambda s: -len(w[s][1])):
+            n, snap = w[sem]
+            if known[q].get(sem, 0) >= n:
+                continue
+            queues[q].wait_ge(T.sem[sem], n)
+            for k in snap:
+                known[q][k] = max(snap[k], known[q].get(k, 0))
+            known[q][sem] = n
+
+    def note(q, reads, writes, sem, n, snap):
+        for regs, isw in ((reads, False), (writes, True)):
+            for r in regs:
+                L = log.setdefault(r[0], [])
+                if isw:
+                    L[:] = [e for e in L if not (e[0][1] >= r[1] and e[0][2] <= r[2] and r[3] == 1 and e[0][4] >= r[4] and e[0][5] <= r[5])]
+                else:
+                    L[:] = [e for e in L if not (e[2] == q and not e[1] and e[0] == r and q in own)]
+                L.append((r, isw, q, sem, n, snap))
+
+    def rg(xs):
+        return [r for x in xs if isinstance(x, tuple) for r in x[1]]
+
+    def ap(x):
+        return x[0] if isinstance(x, tuple) else x
+
+    def run(q, outs, ins, f):
+        r, w, s = rg(ins), rg(outs), own[q]
+        need(q, r, w)
+        count[s] = count.get(s, 0) + 1
+        f().then_inc(T.sem[s], 1)
+        note(q, r, w, s, count[s], dict(known[q]))
+
+    V, SE, PE = g.vector, g.scalar, g.tensor
+
+    def cp(o, i):
+        run("v", [o], [i], lambda: V.tensor_copy(ap(o), ap(i)))
+
+    def sct(win, off, i):
+        run("v", [win], [off, i], lambda: V.tensor_copy(win[0].indirect(off[0]), ap(i)))
+
+    def tt(o, a, b, op):
+        run("v", [o], [a, b], lambda: V.tensor_tensor(ap(o), ap(a), ap(b), op))
+
+    def ts(o, a, s1, op0, s2=None, op1=None):
+        if op1 is None:
+            run("v", [o], [a, s1], lambda: V.tensor_scalar(ap(o), ap(a), ap(s1), None, op0))
+        else:
+            run("v", [o], [a, s1, s2], lambda: V.tensor_scalar(ap(o), ap(a), ap(s1), ap(s2), op0, op1))
+
+    def scan(o, a, b, init, op0, op1):
+        run("v", [o], [a, b, init], lambda: V.tensor_tensor_scan(ap(o), ap(a), ap(b), ap(init), op0, op1))
+
+    def ms(o, c):
+        run("v", [o], [], lambda: V.memset(ap(o), c))
+
+    def act(o, i, f, bias=None, scale=None):
+        kw = {}
+        if bias is not None:
+            kw["bias"] = ap(bias)
+        if scale is not None:
+            kw["scale"] = ap(scale)
+        run("s", [o], [i, bias, scale], lambda: SE.activation(ap(o), ap(i), f, **kw))
+
+    def mm(o, l, r, start=True, stop=True):
+        run("t", [o], [l, r], lambda: PE.matmul(ap(o), ap(l), ap(r), start, stop))
+
+    def iota(o, pat, base, ch, small=True):
+        kw = {"allow_small_or_imprecise_dtypes": True} if small else {}
+        run("g", [o], [], lambda: g.iota(ap(o), pat, base, ch, **kw))
+
+    def sel(o, i, pat, op, base, ch):
+        run("g", [o], [i], lambda: g.affine_select(ap(o), ap(i), pat, op, 0.0, base, ch))
+
+    nd = [0]
+
+    def dma(q, o, i):
+        r, w = rg([i]), rg([o])
+        need(q, r, w)
+        s = "d%d" % nd[0]
+        nd[0] += 1
+        queues[q].dma_start(ap(o), ap(i)).then_inc(T.sem[s], 16)
+        count[s] = 16
+        note("d" + s, r, w, s, 16, dict(known[q]))
+
+    dma("y", A("Q0", QG, QG + 512), (T.gd[:, :], []))
+    dma("y", A("wti"), (T.wt[:, :], []))
+    dma("y", A("kmi"), (T.km[:, :], []))
+    dma("y", A("x0c"), (T.xs[0:128:16, :], []))
+    dma("y", A("thi"), (T.th[:, :], []))
+    dma("y", A("X"), (T.xs[:, :], []))
+    o128 = A("oneb", 0, 128)
+
+    def weights(t):
+        act(A("Wff"), A("BMgf"), F.Copy, None, A("wf", t, t + 1))
+        act(A("Wf"), A("BMgf"), F.Copy, None, A("wf", t, t + 1))
+        for q in range(8):
+            act(A("Lw", 16 * q, 16 * q + 1936, 129), A("oneb", 0, 16), F.Copy, None, A("Wff", q, q + 1))
+
+    def consts0():
+        ms(A("oneb"), 1.0)
+        sel(A("BM"), o128, [[-16, 8], [0, 16]], O.is_ge, 0, 1)
+        sel(A("BM"), A("BM"), [[16, 8], [0, 16]], O.is_ge, 15, -1)
+        iota(A("pi"), [[0, 1]], 0, 1, False)
+        iota(A("iM"), [[64, 16]], 0, 0)
+        ms(A("Lw"), 0.0)
+        ms(A("onef"), 1.0)
+        cp(A("wf"), A("wti"))
+        cp(A("BMgf"), A("BM", 0, 128, 16))
+        weights(0)
+        cp(A("kf"), A("kmi"))
+
+    def consts1():
+        ms(A("c16"), 0.0625)
+        ms(A("rs16"), 0.0)
+        ms(A("rs16", 0, 512, 16), BIG)
+        ts(A("O16", 0, 16, 2), A("BMgf"), 1024.0, O.mult)
+        ts(A("O16", 1, 16, 2), A("BMgf"), 1024.0, O.mult)
+        ts(A("kA"), A("kmi"), 6, O.logical_shift_right)
+        ts(A("kB"), A("kmi"), 63, O.bitwise_and)
+        cp(A("kAf"), A("kA"))
+        cp(A("kBf"), A("kB"))
+        for q in range(8):
+            m = A("BMgf", q, q + 1)
+            act(A("Kpat", q * 32, q * 32 + 16), A("kAf"), F.Copy, None, m)
+            act(A("Kpat", q * 32 + 16, q * 32 + 32), A("kBf"), F.Copy, None, m)
+            act(A("Mpat", q * 32, q * 32 + 16), A("iM"), F.Copy, None, m)
+            act(A("Mpat", q * 32 + 16, q * 32 + 32), A("iM"), F.Copy, None, m)
+        act(A("Kpat", 256, 512), A("Kpat", 0, 256), F.Copy)
+        act(A("Mpat", 256, 512), A("Mpat", 0, 256), F.Copy)
+
+    def consts2():
+        sel(A("idf"), A("onef", 0, 128), [[-1, 128]], O.is_equal, 0, 1)
+        sel(A("Pm"), o128, [[-16, 8], [1, 16]], O.is_equal, -15, 1)
+        sel(A("Jm"), o128, [[1, 128]], O.is_equal, -127, 1)
+        iota(A("i512"), [[1, 512]], 0, 0)
+        sel(A("cm"), A("onef", 0, 128), [[-1, 128]], O.is_gt, 0, 1)
+        sel(A("tri"), o128, [[1, 128]], O.is_ge, 0, -1)
+        sel(A("tB"), A("onef", 0, 128), [[1, 128]], O.is_gt, 0, -1)
+        iota(A("i64f"), [[1, 64]], 1, 0)
+        iota(A("tA"), [[0, 8], [1, 16]], 5, 0)
+        iota(A("iW"), [[16, 32]], 0, 0)
+        iota(A("dW"), [[16, 4]], 706, 0)
+        iota(A("aW"), [[1, 2], [16, 4]], 0, 0)
+        iota(A("slS"), [[128, 4], [0, 8]], 1, 1, False)
+        iota(A("Urep"), [[0, 8256]], 0, 0)
+        iota(A("Dw"), [[0, DW]], 0, 0)
+        ms(A("bA"), 191.5)
+        ms(A("bB"), -256.0)
+        act(A("SG", 2048, 2560), A("x0c"), F.Sign, A("bA"), -1.0)
+        act(A("idb"), A("idf"), F.Copy)
+        act(A("Jm"), A("Jm"), F.Copy, None, -16384.0)
+        ts(A("pj"), A("pi"), 15, O.bitwise_and)
+        cp(A("rcol"), A("pj"))
+        ts(A("b512"), A("rcol"), 512.0, O.mult)
+        ts(A("pj"), A("pi"), 63, O.bitwise_and)
+        ts(A("acol"), A("pj"), -262144.0, O.add)
+        tt(A("cm"), A("cm"), A("BM"), O.mult)
+
+    def consts3():
+        act(A("Lsel"), A("Lw"), F.Copy, None, 0.0)
+        for q in range(8):
+            act(A("Lsel", 16 * q, 16 * q + 1936, 129), A("c16", 0, 16), F.Copy, None, A("BMgf", q, q + 1))
+        act(A("i64b"), A("i64f"), F.Copy)
+        tt(A("id2"), A("idf", 0, 64), A("idf", 64, 128), O.add)
+        tt(A("t32"), A("id2", 0, 32), A("id2", 32, 64), O.add)
+        for k in range(4):
+            tt(A("mW", 16 * k, 16 * k + 16), A("t32", 0, 16), A("t32", 16, 32), O.add)
+        ms(A("c16f"), 0.0625)
+        ms(A("z16"), 1.0)
+        ms(A("z16", 0, 128, 16), 0.0)
+        ms(A("rs64"), -BIG)
+        ms(A("rs64", 0, 256, 64), BIG)
+        cp(A("tri2"), A("tri"))
+        ms(A("tri2", 64, 128, 1, 0, 64), 0.0)
+        ms(A("BO2"), 0.0)
+        ms(A("BO2", 0, 64, 1, 0, 64), 1.0)
+        ms(A("BO2", 64, 128, 1, 64, 128), 1.0)
+        ms(A("maskJ"), 0.0)
+        for j in range(4):
+            for h in range(2):
+                c = j * 128 + (2 * j + h) * 16
+                ms(A("maskJ", c, c + 16, 1, 64 * h, 64 * h + 64), 1.0)
+        ts(A("bs"), A("rcol"), 0.0, O.is_equal)
+        ts(A("rself"), A("BM"), A("bs"), O.mult)
+        cp(A("rselb"), A("rself"))
+        tt(A("tA"), A("tA"), A("BM"), O.mult)
+        ts(A("Bpat"), A("tA"), -5.0, O.add)
+        tt(A("tA"), A("tB"), A("tri"), O.add)
+        tt(A("TriB"), A("tA"), A("BM"), O.mult)
+        ts(A("iW"), A("iW"), A("rcol"), O.add)
+        ts(A("dW"), A("dW"), A("rcol"), O.add)
+        ts(A("aW"), A("aW"), A("rcol"), O.add)
+        ts(A("slL"), A("slS"), 63, O.bitwise_and)
+        cp(A("VL", 160, 192), A("slL"))
+        tt(A("VL", 64, 96), A("slS"), A("slL"), O.subtract)
+        ms(A("mP"), 0.0)
+        ms(A("mT"), 0.0)
+        ms(A("OE"), 0.0)
+        cp(A("thr"), A("thi"))
+        ts(A("tA", 0, 8), A("BMgf"), A("thr"), O.mult)
+        mm(A("B6", 0, 8), A("c16f"), A("tA", 0, 8))
+        for b in range(4):
+            cp(A("thS", 8 * b, 8 * b + 8), A("B6", 0, 8))
+
+    def p1a(t, ch):
+        bank, Q, o = "B2" if ch == 0 else "B4", "Q%d" % t, QG + 256 * ch
+        w, s = (0, 16) if ch == 0 else (16, 0)
+        for r in range(16):
+            mm(A(bank, w, w + 16), A("Lw", r * 128, r * 128 + 128), A(Q, o + r, o + 256, 16), r == 0, r == 15)
+        for b in range(2):
+            mm(A(bank, s + 8 * b, s + 8 * b + 8), A(Q, o + 128 * b, o + 128 * b + 128), A("Wf"))
+
+    def p1b(ch):
+        a, b = 32 * ch, 32 * ch + 32
+        cp(A("ui", a, b), A("B2" if ch == 0 else "B4", 0, 32))
+        ts(A("U", a, b), A("ui", a, b), 4095, O.bitwise_and)
+        tt(A("sq", a, b), A("U", a, b), A("U", a, b), O.mult)
+        cp(A("UF", a, b), A("U", a, b))
+        ts(A("Fi", a, b), A("sq", a, b), 5, O.logical_shift_right)
+        cp(A("FF", a, b), A("Fi", a, b))
+
+    def lists(ch):
+        for b in range(16):
+            k = b + 48 * ch
+            u, f = A("UF", k, k + 1), A("FF", k, k + 1)
+            if ch:
+                act(A("T1f", b, 256, 16), A("kf"), F.Identity, f, u)
+            else:
+                ts(A("T0", b, 256, 16), A("kf"), u, O.mult, f, O.add)
+
+    def lists2(ch):
+        n = "T%d" % ch
+        if ch:
+            cp(A("T1"), A("T1f"))
+        ts(A(n), A(n), 8191, O.bitwise_and)
+        cp(A("O" + n), A(n))
+
+    def reps0(t):
+        for k in range(4):
+            act(A("Gr0", 256 * k, 256 * k + 256), A("Q%d" % t, QG, QG + 256), F.Copy)
+
+    def reps1(t):
+        for k in range(4):
+            dma("y", A("Gr1", 256 * k, 256 * k + 256), A("Q%d" % t, QG + 256, QG + 512))
+
+    def patterns(ch):
+        mm(A("B%d" % ch), A("c16"), A("Kpat"), True, False)
+        mm(A("B%d" % ch), A("c16"), A("Mpat"), False, False)
+
+    def sums(ch, m0, m1, last):
+        for m in range(m0, m1):
+            for b in range(2):
+                a = ch * 4096 + m * 256 + b * 128
+                mm(A("B%d" % ch, b * 256 + m, b * 256 + m + 241, 16), A("Ab", a, a + 128), A("O16"), False, last and m == m1 - 1 and b == 1)
+
+    def gather(ch, m0, m1, last=False):
+        n, o = (m1 - m0) * 256, ch * 4096 + m0 * 256
+        tt(A("A0", o, o + n), IX(A("X"), A("OT%d" % ch, m0 * 16, m1 * 16)), A("Gr%d" % ch, 0, n), O.add)
+        act(A("Ab", o, o + n), A("A0", o, o + n), F.Abs, -255.0)
+        sums(ch, m0, m1, last)
+
+    def sgather(m0, bank, k):
+        act(A("xs2", 512 * k, 512 * k + 512), IX(A("X"), A("OT1", m0 * 16, m0 * 16 + 32)), F.Copy)
+        mm(A(bank), A("idb"), A("xs2", 512 * k, 512 * k + 512), True, False)
+        mm(A(bank), A("idb"), A("Gr1", 0, 512), False, True)
+
+    def sgather2(m0, bank):
+        o = 4096 + m0 * 256
+        act(A("Ab", o, o + 512), A(bank), F.Abs, -255.0)
+        sums(1, m0, m0 + 2, False)
+
+    def lowest(ch):
+        scan(A("KS%d" % ch), A("rs16"), A("B%d" % ch), 0.0, O.max, O.min)
+        cp(A("Ki", 32 * ch, 32 * ch + 32), A("KS%d" % ch, 15, 512, 16))
+
+    def decode():
+        ts(A("kp"), A("Ki"), 63, O.bitwise_and)
+        ts(A("CD", 32, 64), A("Ki", 0, 64, 2), 10, O.logical_shift_right)
+        tt(A("pr"), A("kp"), A("UU"), O.mult)
+        tt(A("f1"), A("CD", 32, 64), A("thS"), O.is_lt)
+        tt(A("tf"), A("pr", 0, 64, 2), A("pr", 1, 64, 2), O.add)
+        tt(A("tc"), A("tf"), A("FF", 16, 48), O.add)
+        ts(A("tt"), A("tc"), 8191, O.bitwise_and)
+        ts(A("CD", 0, 32), A("tt"), 64.0, O.add)
+        ts(A("f2"), A("tt"), 8096.0, O.is_lt)
+        tt(A("fit"), A("f1"), A("f2"), O.mult)
+
+    def choose():
+        mm(A("B2", 0, 32), A("tri"), A("fit"), True, False)
+        mm(A("B2", 8, 32), o128, A("fit", 0, 24), False, False)
+        mm(A("B2", 16, 32), o128, A("fit", 0, 16), False, False)
+        mm(A("B2", 24, 32), o128, A("fit", 0, 8), False, True)
+        ts(A("CDl"), A("CD"), 63, O.bitwise_and)
+        tt(A("VL", 0, 64), A("CD"), A("CDl"), O.subtract)
+        cp(A("VL", 96, 160), A("CDl"))
+        tt(A("rsel"), A("B2", 0, 32), A("fit"), O.mult)
+        for q in range(8):
+            for b in range(4):
+                c = b * 8 + q
+                ts(A("OH", c * 64, c * 64 + 64), A("i64b"), A("rsel", c, c + 1), O.is_equal)
+                h, j = q % 2, q // 2
+                mm(A("B3", j, j + 21, 4, 64 * h, 64 * h + 64), A("OH", c * 64, c * 64 + 64), A("VL", c, c + 161, 32), b == 0, b == 3)
+
+    def resolve():
+        cp(A("Ls"), A("B3", 0, 24))
+        tt(A("cds"), A("Ls", 0, 12), A("Ls", 12, 24), O.add)
+
+        def diag(to, col):
+            for j in (2, 3):
+                act(A("DG", to + 64 * j, to + 64 * j + 64), A("id2"), F.Copy, None, A(col, j, j + 1))
+            for j in (0, 1):
+                ts(A("DG", to + 64 * j, to + 64 * j + 64), A("id2"), A(col, j, j + 1), O.mult)
+
+        diag(0, "cds")
+        mm(A("B4", 0, 256), A("BO2"), A("DG", 0, 256))
+        ts(A("Vp"), A("cds", 4, 8), 64.0, O.mult, A("acol"), O.add)
+        diag(256, "Vp")
+        mm(A("B5", 0, 256), A("BO2"), A("DG", 256, 512))
+        ts(A("E5"), A("cds", 0, 4), 1024.0, O.mult)
+        tt(A("E5"), A("E5"), A("cds", 8, 12), O.add)
+        ts(A("vm"), A("cds", 0, 4), 64.0, O.is_ge)
+        for j in range(4):
+            ts(A("EQ", 64 * j, 64 * j + 64), A("B4", 64 * j, 64 * j + 64), A("cds", j, j + 1), O.is_equal)
+        tt(A("EQ"), A("EQ"), A("B5", 0, 256), O.mult)
+        scan(A("SC"), A("rs64"), A("EQ"), 0.0, O.max, O.min)
+        tt(A("win"), A("SC", 63, 256, 64), A("Vp"), O.is_equal)
+        tt(A("OE", 65, 264, 66), A("win"), A("vm"), O.mult)
+        mm(A("B3", 32, 36), A("tri2"), A("OE", 65, 264, 66))
+        tt(A("rid"), A("B3", 32, 36), A("OE", 65, 264, 66), O.mult)
+        for j in range(4):
+            ts(A("OE", 66 * j, 66 * j + 64), A("i64f"), A("rid", j, j + 1), O.is_equal, A("E5", j, j + 1), O.mult)
+            mm(A("B6", 0, 66), A("maskJ", 128 * j, 128 * j + 128), A("OE", 66 * j, 66 * j + 66), j == 0, j == 3)
+
+    def wrap(src, src2=None):
+        tt(A("tmA", 0, 64), src, A("mW"), O.mult)
+        if src2 is not None:
+            tt(A("tmA", 64, 128), src2, A("mW"), O.mult)
+        n = 64 if src2 is None else 128
+        scan(A("tmB", 0, n), A("z16", 0, n), A("tmA", 0, n), 0.0, O.mult, O.add)
+        return A("tmB", 15, n, 16)
+
+    def send(t, what):
+        dst = T.cores[rank ^ (1 if what == "P" else 4)]
+        e = topo.engines(core, dst)
+        e = e[8:16] if what == "P" else e[:8]
+        rid, pid, _ = topo.addr(dst)
+        src = A("m" + what)
+        land = A("Q%d" % t, 0, 72) if what == "P" else A("Q%d" % t, 72, QG)
+        need("g", src[1], [])
+        la, aa = "l%s%d" % (what, t), "a%s%d" % (what, t)
+        g.remote_dma(out_ap=land[0], in_ap=src[0], remote_sem=T.sem[aa], local_sem=T.sem[la], pid=pid, routing_id=rid, dma_engine_mask=sum(1 << x for x in e))
+        count[la] = count[aa] = len(e)
+        note("r", src[1], [], la, len(e), dict(known["g"]))
+        note("r", [], land[1], aa, len(e), {})
+
+    def marks(k):
+        ts(A("hiI", k, k + 4), A("PL", k, k + 4), 9, O.arith_shift_right)
+        ts(A("loI", k, k + 4), A("PL", k, k + 4), 511, O.bitwise_and)
+        ts(A("loF", k, k + 4), A("loI", k, k + 4), -1.0, O.mult, 0.5, O.add)
+        cp(A("hiF", k, k + 4), A("hiI", k, k + 4))
+        for i in range(k, k + 4):
+            act(A("sgn", 512 * i, 512 * i + 512), A("i512"), F.Sign, A("loF", i, i + 1))
+
+    def blocks(k):
+        for i in range(k, k + 4):
+            ts(A("HH", 128 * i, 128 * i + 128), A("Bpat"), A("hiF", i, i + 1), O.is_equal, 4096.0 if k == 0 else -4096.0, O.mult)
+
+    def cover(k):
+        for i in range(k, k + 4):
+            mm(A("B5"), A("HH", 128 * i, 128 * i + 128), A("sgn", 512 * i, 512 * i + 512), i == 0, i == 7)
+
+    def give(t):
+        n = A("B6", 65, 66)
+        cp(A("EW"), wrap(A("B6", 0, 64), A("B6", 1, 65)))
+        ts(A("cW"), A("EW", 0, 4), 10, O.logical_shift_right)
+        ts(A("OFF", 4, 8), A("cW"), -1.0, O.mult, 8239.0, O.add)
+        cp(A("UG", 0, 64), IX(A("Urep"), A("OFF", 4, 8)))
+        mm(A("B0", 0, 64), A("rself"), A("UG", 0, 64))
+        act(A("mP", 64, 65), n, F.Copy)
+        act(A("mP", 65, 66), n, F.Copy, 72.0, -1.0)
+        act(A("mT", 128, 129), n, F.Copy)
+        act(A("mT", 129, 130), n, F.Copy, 64.0, -1.0)
+        act(A("mT", 130, 131), n, F.Copy, 72.0, -1.0)
+        ts(A("OFF", 0, 4), A("cW"), -54.0, O.add, 0.0, O.max)
+        cp(A("xg", 0, 64), IX(A("X"), A("OFF", 0, 4)))
+        mm(A("B7", 0, 64), A("rselb"), A("xg", 0, 64))
+        ts(A("yv", 0, 64), A("xg", 0, 64), -1.0, O.mult, 255.0, O.add)
+        ts(A("PL", 0, 4), A("cW"), -64.0, O.add)
+        marks(0)
+        e1 = wrap(A("B0", 0, 64))
+        ts(A("OFF", 16, 20), e1, -8.0, O.add, 0.0, O.max)
+        cp(A("UG", 64, 128), IX(A("Urep"), A("OFF", 16, 20)))
+        mm(A("B1", 0, 64), A("rself"), A("UG", 64, 128))
+        ts(A("OFF", 8, 12), e1, -1.0, O.mult, 8191.0, O.add)
+        ts(A("mk", 0, 64), A("B7", 0, 64), 256.0, O.is_lt)
+        tt(A("mP", 0, 64), A("mk", 0, 64), A("yv", 0, 64), O.mult)
+        send(t, "P")
+        e2 = wrap(A("B1", 0, 64))
+        ts(A("OFF", 12, 16), e2, -1.0, O.mult, 8191.0, O.add)
+        cp(A("xg", 64, 192), IX(A("X"), A("OFF", 8, 16)))
+        mm(A("B7", 64, 192), A("rselb"), A("xg", 64, 192))
+        ts(A("yv", 64, 192), A("xg", 64, 192), -1.0, O.mult, 255.0, O.add)
+        ts(A("PL", 4, 8), e2, -1.0, O.mult, 8192.0, O.add)
+        ts(A("mk", 64, 192), A("B7", 64, 192), 256.0, O.is_lt)
+        tt(A("mT", 0, 128), A("mk", 64, 192), A("yv", 64, 192), O.mult)
+        send(t, "T")
+        marks(4)
+        blocks(0)
+        cover(0)
+        blocks(4)
+        cover(4)
+
+    def order(t):
+        ts(A("s1"), A("EW"), 1023, O.bitwise_and)
+        tt(A("tW"), A("s1"), A("aW"), O.subtract)
+        ts(A("OFC"), A("s1", 0, 4), -1.0, O.add, 0.0, O.max)
+        ts(A("q1"), A("tW", 0, 4), 0.0, O.max)
+        tt(A("isl"), A("tW", 0, 4), A("tW", 4, 8), O.not_equal)
+        tt(A("q2"), A("q1"), A("isl"), O.mult)
+        ts(A("q1"), A("q2"), 0.0, O.is_equal)
+        tt(A("q3"), A("q1"), A("dW"), O.mult)
+        tt(A("q1"), A("q2"), A("q3"), O.add)
+        cp(A("Q%d" % t, QG + 512, QG + 576), IX(A("Q%d" % t, QG, QG + 512), A("OFC")))
+
+    def cut511():
+        cp(A("c511"), A("B5", 511, 512))
+        mm(A("B7", 0, 1), A("TriB"), A("c511"))
+        act(A("bs"), A("B7", 0, 1), F.Copy)
+        act(A("B7"), A("B5"), F.Identity, A("bs"))
+
+    def consume(t):
+        tt(A("x0c"), A("x0c"), A("B7"), O.max)
+        if t < RO - 1:
+            dma("y", A("X", 0, 8192, 1, 0, 128, 16), A("x0c"))
+        act(A("SG", t * 512, t * 512 + 512), A("x0c"), F.Sign, A("bB"))
+
+    def merge(t):
+        Q = "Q%d" % t
+        nP, dP, nT, d2, d3 = A(Q, 64, 65), A(Q, 65, 66), A(Q, 200, 201), A(Q, 201, 202), A(Q, 202, 203)
+        ts(A("mi", 0, 32), A("iW"), nP, O.is_ge, dP, O.mult)
+        tt(A("mi", 32, 64), A("mi", 0, 32), A("iW"), O.add)
+        tt(A("sN", 0, 1), nP, nT, O.add)
+        tt(A("sN", 1, 2), A("sN", 0, 1), nT, O.add)
+        ts(A("A1"), A("sN", 1, 2), -1.0, O.add)
+        ts(A("OFD"), A("q1"), A("A1"), O.add)
+        sct(A("Dw"), A("OFD"), A("i64b"))
+        scan(A("DS"), A("Dw", 0, 512), A("Dw", 0, 512), 0.0, O.max, O.max)
+        for r in range(16):
+            mm(A("B3", 0, 32), A("Lsel", r * 128, r * 128 + 128), A("DS", r, 512, 16), r == 0, r == 15)
+        cut511()
+        ts(A("mi", 64, 96), A("iW"), A("sN", 0, 1), O.is_ge, d2, O.mult)
+        ts(A("mi", 96, 128), A("iW"), A("sN", 1, 2), O.is_ge, d3, O.mult)
+        tt(A("mi", 128, 160), A("mi", 32, 64), A("mi", 64, 96), O.add)
+        tt(A("mi", 160, 192), A("mi", 128, 160), A("mi", 96, 128), O.add)
+        tt(A("mi", 0, 32), A("B3", 0, 32), A("mi", 160, 192), O.add)
+        cp(A("MI"), A("mi", 0, 32))
+        for c in range(2):
+            o = A("Gn", 256 * c, 256 * c + 256) if t == RO - 1 else A("Q%d" % (t + 1), QG + 256 * c, QG + 256 * c + 256)
+            cp(o, IX(A(Q), A("MI", 16 * c, 16 * c + 16)))
+        if t < RO - 1:
+            iota(A("Dw"), [[0, DW]], 0, 0)
+
+    def reverse(t):
+        for c in range(4):
+            mm(A("B6", c * 128, c * 128 + 128), A("SG", t * 512 + c * 128, t * 512 + c * 128 + 128), A("Pm"))
+        act(A("RV1"), A("B6"), F.Copy)
+        for c in range(4):
+            mm(A("B5", (3 - c) * 128, (3 - c) * 128 + 128), A("RV1", c * 128, c * 128 + 128), A("Jm"))
+
+    def utable(first):
+        tt(A("okl"), A("B5"), A("i512") if first else A("okl"), O.min)
+        scan(A("oks"), A("okl"), A("okl"), -16384.0, O.max, O.max)
+        ts(A("tot"), A("oks", 511, 512), A("b512"), O.add)
+        ts(A("dg"), A("idf"), A("tot"), O.mult)
+        mm(A("B7", 0, 128), A("onef", 0, 128), A("dg"))
+
+    def utable2():
+        tt(A("cmx"), A("B7", 0, 128), A("cm"), O.mult)
+        run("v", [A("cry")], [A("cmx")], lambda: V.tensor_reduce(A("cry")[0], A("cmx")[0], AxisListType.X, O.max))
+        ts(A("Ut"), A("oks"), A("b512"), O.add, A("cry"), O.max)
+        dma("y", A("Urep", 0, 8192, 1, 0, 128, 16), A("Ut"))
+
+    for t in range(RO):
+        if t == 0:
+            consts0()
+        else:
+            consume(t - 1)
+        p1a(t, 0)
+        reps0(t)
+        p1a(t, 1)
+        p1b(0)
+        lists(0)
+        lists2(0)
+        p1b(1)
+        lists(1)
+        reps1(t)
+        if t == 0:
+            consts1()
+            consts2()
+            reverse(4)
+        else:
+            reverse(t - 1)
+        patterns(0)
+        if t == 0:
+            lists2(1)
+            consts3()
+        gather(0, 0, 4)
+        if t > 0:
+            lists2(1)
+        patterns(1)
+        act(A("UU", 0, 64, 2), A("UF", 16, 48), F.Copy, None, 64.0)
+        act(A("UU", 1, 64, 2), A("UF", 16, 48), F.Copy)
+        gather(0, 4, 8)
+        sgather(12, "B3", 0)
+        gather(0, 8, 12)
+        sgather2(12, "B3")
+        utable(t == 0)
+        gather(0, 12, 16, True)
+        sgather(14, "B4", 1)
+        gather(1, 0, 4)
+        sgather2(14, "B4")
+        utable2()
+        gather(1, 4, 8)
+        gather(1, 8, 10)
+        gather(1, 10, 11)
+        gather(1, 11, 12, True)
+        if t < RO - 1:
+            weights(t + 1)
+        lowest(0)
+        lowest(1)
+        decode()
+        choose()
+        resolve()
+        give(t)
+        order(t)
+        merge(t)
+    dma("y", (T.yg[:, :], []), A("Gn"))
+    consume(RO - 1)
+    for t in range(RO):
+        mm(A("B5"), A("idb"), A("SG", t * 512, t * 512 + 512), t == 0, t == RO - 1)
+    ts(A("Yt"), A("B5"), -0.5, O.mult, 3.0, O.add)
+    ts(A("Yu"), A("B5"), -3.0, O.is_ge)
+    tt(A("Yt"), A("Yt"), A("Yu"), O.mult)
+    dma("y", (T.yc[:, :], []), A("Yt"))
+    for s in count:
+        if known["g"].get(s, 0) < count[s]:
+            g.wait_ge(T.sem[s], count[s])

@@ -1,26 +1,31 @@
 from concourse.mybir import AluOpType as O, AxisListType, ActivationFunctionType as F
+from concourse.bass import DstId, RemoteDMATransfer
 
 RO = 4
-QW = 784
-QG = 208
-DW = 976
-BIG = 1.0e9
+QW = 768
+QG = 192
+BIG = 16777216.0
+M16 = 1.5 * 2.0 ** 27
+M512 = 1.5 * 2.0 ** 32
+PATH = [2, 3, 2, 3, 1, 3, 2, 1, 3, 1, 2, 3, 1, 3, 1, 1]
+KB = [(0, 8), (8, 12), (12, 16)]
+SSEL = [c for c in range(32) if c % 2]
 
-_f = "x0c:512b okl:512 oks:512 Ut:512 RV1:512b SG:2560b Yt:512 Yu:512 idf:128 idb:128b BM:128b BMgf:8 tri:128b oneb:512b onef:512 O16:16b"
-_f += " tri2:128 BO2:128 id2:64 maskJ:512 i64b:64b i64f:64 mW:64 t32:32 z16:128 rs16:512 rs64:256 Kpat:512b Mpat:512b c16:128b c16f:128 thr:1 thS:32"
-_f += " Bpat:128b TriB:128b cm:128 Pm:128b Jm:128b pi:1i pj:1i rcol:1 b512:1 acol:1 iW:32 dW:4 aW:8 i512:512 rself:128 rselb:128b kA:16i kB:16i kAf:16 kBf:16"
-_f += " iM:16 slS:32i slL:32i tA:128 tB:128 X:8192b Urep:8256 A0:8192 Ab:8192b Gr0:1024b Gr1:1024b xs2:1024b wti:4i kmi:16i thi:1i wf:4 kf:16 Lw:2048b Lsel:2048b"
-_f += " Wf:8b Wff:8 ui:64i U:64i sq:64i Fi:64i UF:64 FF:64 UU:64 T0:256i T1:256i T1f:256 OT0:256u OT1:256u KS0:512 KS1:512 Ki:64i kp:64i pr:64 tt:32i tf:32 tc:32i CD:64i CDl:64i"
-_f += " VL:192b f1:32 f2:32 fit:32b rsel:32 OH:2048b Ls:24 cds:12 Vp:4 DG:512 EQ:256 SC:256 vm:4 win:4 E5:4 OE:264 rid:4 tmA:128 tmB:128 EW:8i cW:4i s1:8i tW:8 isl:4 q1:4 q2:4 q3:4"
-_f += " OFF:24u OFC:4u OFD:4u UG:128 xg:192b yv:192b mk:192b mP:72b mT:136b PL:8i hiI:8i loI:8i hiF:8 loF:8 HH:1024b sgn:4096b c511:1b bs:1 bA:1 bB:1 Dw:976b DS:512b sN:2b A1:1 mi:192 MI:32u"
-_f += " tot:1 dg:128 cmx:128 cry:1 Gn:512b"
+_f = "x0c:512b oks:512 Ut:512 RV1:512b SG:2560b Yt:512 Z4:512 Rb:512b G0:512b idf:128 idb:128b nidb:128b BM:128b nBMh:128b BMgf:8 BMg4:32 tri:128b oneb:512b onef:128"
+_f += " O16:16b O16n:16b O16d:16b i65:66b n65:66b ia64:64b mW:128 t32:32 id2:64 z16:128b rsA:512b rsB:256b rs64:256b ph:1i tE:32 Pat:1024b KM:32 KMm:32 thr:1 thS:32 c16f:128"
+_f += " Bp:128b Rp:128b B16:32b nB16:32 TriB:128b TBc:128b cm:130 Pm:128b Jm:128b IO:512b sel15:128b neg1:1b pi:1i pj:1i rcol:1 r32:1 r0m:1 r1m:1 b512:1 iW:96 j255:512"
+_f += " rself:128 rselb:128b n1k:64b kA:16i kB:16i iM:16 slS:32i slL:32i tA:128b tB:128b tC:128b X:8208b Urep:8256 A0:8192b Ab:8192b xq:1024b o32:128b zb:128b wti:4i kmi:16i thi:1i wf:4 nwf:4 kf:16"
+_f += " Lw:2048b Wn:8b Wp:32b Wff:8 BMw:128b c255:128b ui:64i U:64i sq:64i Fi:64i UF:64 FF:64 UU:64 T:512i Tf:256 OT:512u KS:1024 KAB:64 Ki:64i kp:64i pr:64 tf:32 tc:32i"
+_f += " cI:32i DI:32i f1:32 lim:32 fit:32b rsel:32 ST:2112b VZ:1040b Pc:64 Pd:64b Cc:128b Ck:128b Cq:128b Cs:128b wv:10 tmA:128 tmB:128 tsA:64 tsB:64 EQ:256 SC:256 win:4b"
+_f += " Mk:512b Jc:8b cvec:4 pos:4u mC:4 t0:4 t1:4 h16:4 SW:1600b swA:64 swB:64 INV:4u OFU:4u OF2:4u OFX:8u OFP:4u OFC:4u UG:128 u1A:64 u1B:64 u2A:64 u2B:64 XG:256b XP:64b"
+_f += " mP:64b mT:128b ts_:8 hs:8 nb:8 HH:1024b sgn:4096b LL:512b EE:128b SS:128b S1:96b dT:128b MI:32u tot:1 dg:128 cmx:130 cry:1 Gn:512b bA:1 bB:1 b2:1"
 _dt = {"b": "bfloat16", "i": "int32", "u": "uint16"}
 _pool, _where, SCRATCH = {}, {}, {}
 for _x in _f.split():
     _n, _c = _x.split(":")
     _d = _dt.get(_c[-1], "float32")
     _c = int(_c if _d == "float32" else _c[:-1])
-    if _c <= 264 and _n not in ("mP", "mT"):
+    if _c <= 264 and _n not in ("mP", "mT", "mC", "XG", "XP"):
         _p = "pool_" + _d
         _where[_n] = (_p, _pool.get(_p, 0), _c)
         _pool[_p] = _pool.get(_p, 0) + (_c + 15) // 16 * 16
@@ -31,13 +36,60 @@ for _x in _f.split():
 for _t in range(RO):
     SCRATCH["Q%d" % _t] = ("sbuf", [128, QW], "bfloat16")
     _where["Q%d" % _t] = ("Q%d" % _t, 0, QW)
+    SCRATCH["C%d" % _t] = ("sbuf", [128, 8], "float32")
+    _where["C%d" % _t] = ("C%d" % _t, 0, 8)
 for _t in range(8):
     SCRATCH["B%d" % _t] = ("psum", [128, 512], "float32")
     _where["B%d" % _t] = ("B%d" % _t, 0, 512)
-NDMA = 48
+NDMA = 24
 SEMAPHORES = ["sv", "ss", "st", "sg"] + ["d%d" % _t for _t in range(NDMA)]
 for _t in range(RO):
-    SEMAPHORES += ["aP%d" % _t, "aT%d" % _t, "lP%d" % _t, "lT%d" % _t]
+    SEMAPHORES += ["aP%d" % _t, "aT%d" % _t, "lP%d" % _t, "lT%d" % _t, "cP%d" % _t, "cT%d" % _t, "lC%d" % _t]
+
+CY, PE_CY, GA, SCA, HOP, DMA_T, REM_T = 1.04e-3, 0.75e-3, 1.56, 3.8, 0.1, 1.6, 2.2
+_order = {}
+
+
+def _lay_out(ops):
+    n = len(ops)
+    succ = [[] for _ in range(n)]
+    for i, o in enumerate(ops):
+        for d in o["dep"]:
+            succ[d].append(i)
+
+    def gap(a, b):
+        return 0.0 if (ops[a]["q"] == "t" and ops[b]["q"] == "t") or a in ops[b]["ord"] else HOP
+
+    level = [0.0] * n
+    for i in range(n - 1, -1, -1):
+        o = ops[i]
+        level[i] = o["busy"] + o["lat"] + max([gap(i, s) + level[s] - (o["lat"] if i in ops[s]["ord"] else 0.0) for s in succ[i]] + [0.0])
+    first = [0.0] * n
+    for i in range(n - 1, -1, -1):
+        first[i] = max([ops[i]["first"]] + [first[s] for s in succ[i]])
+    level = [a + b for a, b in zip(level, first)]
+    start, end = [0.0] * n, [0.0] * n
+    lanes = {}
+    for i in sorted(range(n), key=lambda i: (-level[i], i)):
+        o = ops[i]
+        t = max([(start[d] + ops[d]["busy"] if d in o["ord"] else end[d] + gap(d, i)) for d in o["dep"]] + [0.0])
+        lane = lanes.setdefault(o["q"], [])
+        if o["busy"] > 0:
+            k = 0
+            lo, hi = 0, len(lane)
+            while lo < hi:
+                mid = (lo + hi) // 2
+                if lane[mid][1] <= t:
+                    lo = mid + 1
+                else:
+                    hi = mid
+            k = lo
+            while k < len(lane) and lane[k][0] < t + o["busy"] - 1e-9:
+                t = max(t, lane[k][1])
+                k += 1
+            lane.insert(k, (t, t + o["busy"]))
+        start[i], end[i] = t, t + o["busy"] + o["lat"]
+    return sorted(range(n), key=lambda i: (start[i], -level[i], i))
 
 
 def rank_program(g, core, T, topo):
@@ -46,37 +98,568 @@ def rank_program(g, core, T, topo):
         return
     queues = {"v": g.vector, "s": g.scalar, "t": g.tensor, "g": g, "y": g.sync}
     own = {"v": "sv", "s": "ss", "t": "st", "g": "sg"}
-    count, log = {}, {}
-    known = {q: {} for q in queues}
+    ops, log, banks, early = [], {}, {}, [0.0]
 
     def A(n, lo=0, hi=None, st=1, p0=0, p1=128, pst=1):
         p, o, c = _where[n]
         hi = c if hi is None else hi
-        hi = min(hi, lo + (hi - lo - 1) // st * st + 1)
+        k = (hi - lo - 1) // st + 1
+        hi = lo + (k - 1) * st + 1
         ap = T[p][p0:p1:pst, o + lo:o + hi:st] if (pst != 1 or st != 1) else T[p][p0:p1, o + lo:o + hi]
-        return (ap, [(p, o + lo, o + hi, st, p0, p1)])
+        return (ap, [(p, o + lo, o + hi, st, p0, p1)], k, SCRATCH[p][2], SCRATCH[p][0])
 
     def IX(win, off):
-        return (win[0].indirect(off[0]), win[1] + off[1])
+        return (win[0].indirect(off[0]), win[1] + off[1], 16 * off[2], win[3], "ix")
 
     def hit(a, b):
         if a[1] >= b[2] or b[1] >= a[2] or a[4] >= b[5] or b[4] >= a[5]:
             return False
         return not (a[3] == b[3] and a[3] > 1 and (a[1] - b[1]) % a[3])
 
-    def need(q, reads, writes):
-        w = {}
-        for regs, isw in ((reads, False), (writes, True)):
+    def rg(xs):
+        return [r for x in xs if isinstance(x, tuple) for r in x[1]]
+
+    def ap(x):
+        return x[0] if isinstance(x, tuple) else x
+
+    def add(q, outs, ins, f, busy, lat=0.0, start=None, sem=None, inc=1, after=()):
+        i = len(ops)
+        dep = set(after)
+        o = {"q": q, "f": f, "busy": busy, "lat": lat, "dep": dep, "ord": set(after), "sem": sem or own.get(q), "inc": inc, "grp": None, "first": early[0]}
+        ops.append(o)
+        for regs, isw in ((rg(ins), False), (rg(outs), True)):
             for r in regs:
-                bank = r[0][0] == "B" and r[0][1:].isdigit()
-                for (r2, w2, q2, sem, n, snap) in log.get(r[0], []):
-                    if q2 == q and q2 in own:
-                        if not (isw or w2) or not hit(r, r2) or (isw and q == "t"):
-                            continue
-                    elif not bank and (not (isw or w2) or not hit(r, r2)):
-                        continue
-                    if known[q].get(sem, 0) < n and w.get(sem, (0,))[0] < n:
-                        w[sem] = (n, snap)
+                if r[0][0] == "B" and r[0][1:].isdigit():
+                    b = banks.setdefault(r[0], {"q": None, "run": [], "prev": [], "grp": None})
+                    if b["q"] != q:
+                        b["q"], b["prev"], b["run"] = q, b["run"], []
+                    dep.update(b["prev"])
+                    if q == "t":
+                        if start:
+                            dep.update(b["run"])
+                            b["grp"], b["new"] = [i], [(r, i)]
+                        else:
+                            dep.add(b["grp"][0])
+                            b["grp"].append(i)
+                            was = [j for (r2, j) in b["new"] if hit(r, r2)]
+                            dep.update(was)
+                            if not was:
+                                b["new"].append((r, i))
+                        o["grp"], o["rows"] = b["grp"], (r[4], r[5])
+                    if i not in b["run"]:
+                        b["run"].append(i)
+                    continue
+                L = log.setdefault(r[0], [])
+                for (r2, w2, j) in L:
+                    if (isw or w2) and hit(r, r2):
+                        dep.add(j)
+                if isw:
+                    L[:] = [e for e in L if not (e[0][1] >= r[1] and e[0][2] <= r[2] and (r[3] == 1 or e[0] == r) and e[0][4] >= r[4] and e[0][5] <= r[5])]
+                L.append((r, isw, i))
+        dep.discard(i)
+        return i
+
+    def cost(o, xs, per=None, fixed=0.05):
+        xs = [x for x in xs if isinstance(x, tuple)]
+        if xs[0][4] == "ix":
+            return fixed + xs[0][2] * GA * CY
+        if per is None:
+            per = 0.5 if o[3] in ("bfloat16", "uint16") and xs[0][3] in ("bfloat16", "uint16") else 1.0
+        return max(64, xs[0][2] * per) * CY
+
+    V, SE, PE = g.vector, g.scalar, g.tensor
+
+    def cp(o, i):
+        add("v", [o], [i], lambda s: V.tensor_copy(ap(o), ap(i)), cost(o, [i]))
+
+    def sct(win, off, i):
+        add("v", [win], [off, i], lambda s: V.tensor_copy(win[0].indirect(off[0]), ap(i)), 0.05 + i[2] * SCA * CY)
+
+    def tt(o, a, b, op):
+        add("v", [o], [a, b], lambda s: V.tensor_tensor(ap(o), ap(a), ap(b), op), cost(o, [a], 1.0 if "psum" in (a[4], b[4]) else 2.0))
+
+    def ts(o, a, s1, op0, s2=None, op1=None):
+        if op1 is None:
+            add("v", [o], [a, s1], lambda s: V.tensor_scalar(ap(o), ap(a), ap(s1), None, op0), cost(o, [a]))
+        else:
+            add("v", [o], [a, s1, s2], lambda s: V.tensor_scalar(ap(o), ap(a), ap(s1), ap(s2), op0, op1), cost(o, [a]))
+
+    def scan(o, a, b, init, op0, op1):
+        add("v", [o], [a, b, init], lambda s: V.tensor_tensor_scan(ap(o), ap(a), ap(b), ap(init), op0, op1), cost(o, [a], 1.0))
+
+    def ms(o, c):
+        add("v", [o], [], lambda s: V.memset(ap(o), c), cost(o, [o]))
+
+    def act(o, i, f, bias=None, scale=None):
+        kw = {}
+        if bias is not None:
+            kw["bias"] = ap(bias)
+        if scale is not None:
+            kw["scale"] = ap(scale)
+        add("s", [o], [i, bias, scale], lambda s: SE.activation(ap(o), ap(i), f, **kw), cost(o, [i], 1.0, 0.065))
+
+    def mm(o, l, r, start=True):
+        add("t", [o], [l, r], lambda s: PE.matmul(ap(o), ap(l), ap(r), start, s), max(min(64, l[2]), r[2]) * PE_CY * (4 if l[3] == "float32" else 1), start=start)
+
+    def iota(o, pat, base, ch, small=True):
+        kw = {"allow_small_or_imprecise_dtypes": True} if small else {}
+        add("g", [o], [], lambda s: g.iota(ap(o), pat, base, ch, **kw), 0.13 + 2 * o[2] * CY)
+
+    def sel(o, i, pat, op, base, ch):
+        add("g", [o], [i], lambda s: g.affine_select(ap(o), ap(i), pat, op, 0.0, base, ch), 0.17 + 2 * o[2] * CY)
+
+    nd = [0]
+
+    def dma(o, i, t=0.3, after=()):
+        nd[0] += 1
+        return add("y", [o], [i], lambda s: g.sync.dma_start(ap(o), ap(i)), 0.05, DMA_T + t, sem="d%d" % (nd[0] - 1), inc=16, after=after)
+
+    def hbm(x):
+        return (x, [], 0, "", "dram")
+
+    def remote(local, parts):
+        trs = []
+        for (r, e, src, land, sem) in parts:
+            rid, pid, _ = topo.addr(T.cores[r])
+            trs.append((rid, pid, sum(1 << x for x in e), src[0], land[0], T.sem[sem]))
+
+        def f(s):
+            if len(trs) == 1:
+                rid, pid, m, a, b, sm = trs[0]
+                g.remote_dma(out_ap=b, in_ap=a, remote_sem=sm, local_sem=T.sem[local], pid=pid, routing_id=rid, dma_engine_mask=m)
+            else:
+                g.remote_dma_fused([RemoteDMATransfer(dst_ids=[DstId(rid=rid, pnc=pid)], dma_engine_mask=m, remote_sem=sm, src=a, dst=b) for (rid, pid, m, a, b, sm) in trs],
+                                   local_sem=T.sem[local])
+        i = add("g", [], [p[2] for p in parts], f, 0.3, REM_T, sem=local, inc=-sum(len(p[1]) for p in parts))
+        for (r, e, src, land, sem) in parts:
+            add("r", [land], [], None, 0.0, REM_T, sem=sem, inc=-len(e), after=[i])
+
+    eP = topo.engines(core, T.cores[rank ^ 1])[8:16]
+    eT = topo.engines(core, T.cores[rank ^ 4])[:8]
+
+    d = [dma(A("G0"), hbm(T.gd[:, :]))]
+    d.append(dma(A("wti"), hbm(T.wt[:, :]), after=d[-1:]))
+    d.append(dma(A("kmi"), hbm(T.km[:, :]), after=d[-1:]))
+    d.append(dma(A("x0c"), hbm(T.xs[0:128:16, :]), after=d[-1:]))
+    d.append(dma(A("thi"), hbm(T.th[:, :]), after=d[-1:]))
+    dma(A("X", 0, 8192), hbm(T.xs[:, :]), 7.0, after=d[-1:])
+    o128 = A("oneb", 0, 128)
+
+    def consts():
+        ms(A("oneb"), 1.0)
+        ms(A("onef"), 1.0)
+        ms(A("c255"), 255.0)
+        ms(A("X", 8192, 8208), 255.0)
+        ms(A("Lw"), 0.0)
+        ms(A("VZ"), 0.0)
+        sel(A("BM"), o128, [[-16, 8], [0, 16]], O.is_ge, 0, 1)
+        sel(A("BM"), A("BM"), [[16, 8], [0, 16]], O.is_ge, 15, -1)
+        iota(A("pi"), [[0, 1]], 0, 1, False)
+        iota(A("iM"), [[64, 16]], 0, 0)
+        cp(A("wf"), A("wti"))
+        ts(A("nwf"), A("wti"), -1.0, O.mult)
+        cp(A("BMgf"), A("BM", 0, 128, 16))
+        for b in range(4):
+            act(A("BMg4", 8 * b, 8 * b + 8), A("BM", 0, 128, 16), F.Copy)
+        cp(A("kf"), A("kmi"))
+        ts(A("Q0", QG, QG + 256), A("G0", 0, 256), -1.0, O.mult, 255.0, O.add)
+        ts(A("Q0", QG + 256, QG + 512), A("G0", 256, 512), -1.0, O.mult, 255.0, O.add)
+        ts(A("pj"), A("pi"), 15, O.bitwise_and)
+        cp(A("rcol"), A("pj"))
+        ts(A("b512"), A("pj"), 512.0, O.mult)
+        ts(A("r32"), A("pj"), 32.0, O.add)
+        ts(A("r0m"), A("pj"), 0.0, O.is_equal)
+        ts(A("r1m"), A("pj"), 1.0, O.is_equal)
+        ms(A("rsA"), 0.0)
+        ms(A("rsA", 0, 512, 8), BIG)
+        ms(A("rsB"), 0.0)
+        ms(A("rsB", 0, 256, 4), BIG)
+        for n, c in (("O16", 1024.0), ("O16n", -1024.0), ("O16d", 2048.0)):
+            act(A(n, 0, 16, 2), A("BMgf"), F.Copy, None, c)
+            act(A(n, 1, 16, 2), A("BMgf"), F.Copy, None, c)
+        ts(A("kA"), A("kmi"), 6, O.logical_shift_right)
+        ts(A("kB"), A("kmi"), 63, O.bitwise_and)
+        for (a, b) in KB:
+            for k, n in enumerate(("kA", "kB")):
+                c = 2 * a + k * (b - a)
+                ts(A("KM", c, c + b - a), A(n, a, b), A("r0m"), O.mult)
+                act(A("KMm", c, c + b - a), A("iM", a, b), F.Copy, None, A("r1m"))
+        tt(A("KM"), A("KM"), A("KMm"), O.add)
+        for (a, b) in KB:
+            w, o = 2 * (b - a), 64 * a
+            for q in range(8):
+                act(A("Pat", o + q * w, o + q * w + w), A("KM", 2 * a, 2 * b), F.Copy, None, A("BMgf", q, q + 1))
+            act(A("Pat", o + 8 * w, o + 16 * w), A("Pat", o, o + 8 * w), F.Copy)
+            act(A("Pat", o + 16 * w, o + 32 * w), A("Pat", o, o + 16 * w), F.Copy)
+        sel(A("idf"), A("onef"), [[-1, 128]], O.is_equal, 0, 1)
+        act(A("idb"), A("idf"), F.Copy)
+        act(A("nidb"), A("idf"), F.Copy, None, -1.0)
+        sel(A("Pm"), o128, [[-16, 8], [1, 16]], O.is_equal, -15, 1)
+        sel(A("Jm"), o128, [[1, 128]], O.is_equal, -127, 1)
+        act(A("Jm"), A("Jm"), F.Copy, None, -8192.0)
+        iota(A("j255"), [[1, 512]], -255, 0)
+        iota(A("IO"), [[16, 32], [0, 16]], 0, 0)
+        iota(A("RV1"), [[0, 32], [1, 16]], 1, 0)
+        cp(A("IO", 0, 512, 1, 32, 64), A("RV1", 0, 512, 1, 32, 64))
+        ms(A("o32"), 1.0 / 32)
+        ms(A("zb"), 0.0)
+        sel(A("cm", 0, 128), A("onef"), [[-1, 128]], O.is_gt, 0, 1)
+        tt(A("cm", 0, 128), A("cm", 0, 128), A("BM"), O.mult)
+        ms(A("cm", 128, 130), 1.0)
+        sel(A("tri"), o128, [[1, 128]], O.is_ge, 0, -1)
+        sel(A("tB"), o128, [[1, 128]], O.is_gt, 0, -1)
+        tt(A("tB"), A("tB"), A("BM"), O.mult)
+        act(A("tA"), A("tB"), F.Copy, None, 2.0)
+        tt(A("TriB"), A("tA"), A("idb"), O.add)
+        iota(A("i65"), [[1, 66]], 1, 0)
+        act(A("n65"), A("i65"), F.Identity, 0.5, -1.0)
+        iota(A("ia64"), [[1, 64]], 0, 0)
+        iota(A("slS"), [[128, 4], [0, 8]], 0, 1, False)
+        ms(A("bA"), 191.5)
+        ms(A("bB"), -256.0)
+        ms(A("b2"), 2.0)
+        ms(A("neg1"), -1.0)
+        ms(A("n1k"), -1024.0)
+        act(A("SG", 2048, 2560), A("x0c"), F.Sign, A("bA"), -1.0)
+        tt(A("id2"), A("idf", 0, 64), A("idf", 64, 128), O.add)
+        tt(A("t32"), A("id2", 0, 32), A("id2", 32, 64), O.add)
+        tt(A("mW", 0, 16), A("t32", 0, 16), A("t32", 16, 32), O.add)
+        for k in (16, 32, 64):
+            act(A("mW", k, 2 * k), A("mW", 0, k), F.Copy)
+        ms(A("c16f"), 0.0625)
+        ms(A("z16"), 1.0)
+        ms(A("z16", 0, 128, 16), 0.0)
+        ms(A("rs64"), -BIG)
+        ms(A("rs64", 0, 256, 64), BIG)
+        act(A("rself"), A("BM"), F.Copy, None, A("r0m"))
+        act(A("rselb"), A("BM"), F.Copy, None, A("r0m"))
+        ts(A("tot"), A("pj"), 15.0, O.is_equal, -1.0, O.mult)
+        act(A("sel15"), A("BM"), F.Copy, None, A("tot"))
+        act(A("nBMh"), A("BM"), F.Copy, None, -0.5)
+        act(A("tC"), A("BM"), F.Identity, -4096.0, 4096.0)
+        iota(A("Bp"), [[0, 8], [512, 16]], 0, 0)
+        tt(A("Bp"), A("Bp"), A("BM"), O.mult)
+        tt(A("Bp"), A("Bp"), A("tC"), O.add)
+        iota(A("Rp"), [[0, 8], [1, 16]], -8, 0)
+        tt(A("Rp"), A("Rp"), A("BM"), O.mult)
+        tt(A("Rp"), A("Rp"), A("tC"), O.add)
+        iota(A("B16"), [[16, 32]], 0, 0)
+        act(A("nB16"), A("B16"), F.Identity, 0.5, -1.0)
+        iota(A("iW"), [[-64, 3], [16, 32]], -64, 0)
+        ts(A("iW"), A("iW"), A("rcol"), O.add)
+        ts(A("slL"), A("slS"), 63, O.bitwise_and)
+        cp(A("VZ", 21, 1040, 32), A("slL"))
+        tt(A("VZ", 20, 1040, 32), A("slS"), A("slL"), O.subtract)
+        ms(A("VZ", 22, 1040, 32), 1.0)
+        ms(A("VZ", 23, 1040, 32), 1.0)
+        wv = [A("wv", k, k + 1) for k in range(10)]
+        ts(A("ph"), A("pj"), 1, O.logical_shift_right)
+        ts(wv[0], A("ph"), 0.0, O.is_equal, 0.5, O.mult)
+        ts(wv[1], A("ph"), 1.0, O.is_equal, 256.0, O.mult)
+        ts(wv[2], A("ph"), 2.0, O.is_equal, 0.5, O.mult)
+        ts(wv[3], A("pj"), 6.0, O.is_equal)
+        ts(wv[4], A("pj"), 7.0, O.is_equal, -0.25, O.mult)
+        ts(wv[5], wv[3], 32.0, O.mult, wv[0], O.add)
+        ts(wv[6], wv[3], 92.0, O.mult, wv[2], O.add)
+        ts(wv[7], wv[3], -2097152.0, O.mult, wv[2], O.add)
+        ts(wv[8], wv[7], wv[1], O.add)
+        ts(wv[9], wv[7], wv[1], O.add, wv[4], O.add)
+        for n, k in (("Cc", 5), ("Cs", 6), ("Cq", 8), ("Ck", 9)):
+            act(A(n), A("BM"), F.Copy, None, wv[k])
+        iota(A("t1"), [[128, 4]], 1024, 0)
+        ts(A("t0", 0, 1), A("rcol"), 8.0, O.mult)
+        ts(A("t1"), A("t1"), A("t0", 0, 1), O.add)
+        cp(A("Jc", 0, 4), A("t1"))
+        ms(A("Jc", 4, 5), -64.0)
+        for k in range(4):
+            act(A("Mk", 128 * k, 128 * k + 128), A("nidb"), F.Copy, None, A("t1", k, k + 1))
+        ms(A("cvec", 3, 4), 0.0)
+        ms(A("cvec", 0, 1), 1.0)
+        ms(A("cvec", 1, 2), -1.0)
+        ms(A("cvec", 2, 3), 2.0)
+        ms(A("SW", 0, 64), 0.0)
+        cp(A("thr"), A("thi"))
+        ts(A("tE"), A("BMg4"), A("thr"), O.mult)
+        mm(A("B6", 0, 32), A("c16f"), A("tE"))
+        cp(A("thS"), A("B6", 0, 32))
+
+    def weights(t):
+        w, nw = A("wf", t, t + 1), A("nwf", t, t + 1)
+        act(A("Wff"), A("BMgf"), F.Copy, None, nw)
+        act(A("Wn"), A("BMgf"), F.Copy, None, nw)
+        act(A("Wp"), A("BMg4"), F.Copy, None, w)
+        act(A("BMw"), A("BM"), F.Copy, None, w)
+        for q in range(8):
+            act(A("Lw", 16 * q, 16 * q + 1936, 129), A("oneb", 0, 16), F.Copy, None, A("Wff", q, q + 1))
+
+    def lists(t):
+        Q = "Q%d" % t
+        mm(A("B4", 0, 32), A("BMw"), A("c255", 0, 32), True)
+        mm(A("B4", 32, 64), A("c255"), A("Wp"), False)
+        for r in range(16):
+            mm(A("B4", 0, 32), A("Lw", r * 128, r * 128 + 128), A(Q, QG + r, QG + 512, 16), False)
+        for b in range(4):
+            mm(A("B4", 32 + 8 * b, 40 + 8 * b), A(Q, QG + 128 * b, QG + 128 * b + 128), A("Wn"), False)
+        cp(A("ui"), A("B4", 0, 64))
+        ts(A("U"), A("ui"), 4095, O.bitwise_and)
+        tt(A("sq"), A("U"), A("U"), O.mult)
+        cp(A("UF"), A("U"))
+        ts(A("Fi"), A("sq"), 5, O.logical_shift_right)
+        cp(A("FF"), A("Fi"))
+        for b in range(32):
+            u, f = A("UF", b, b + 1), A("FF", b, b + 1)
+            if b % 2:
+                act(A("Tf", b // 2, 256, 16), A("kf"), F.Identity, f, u)
+            else:
+                ts(A("T", b, 512, 32), A("kf"), u, O.mult, f, O.add)
+        for (a, b) in ((0, 4), (4, 16)):
+            cp(A("T", 32 * a + 1, 32 * b, 2), A("Tf", 16 * a, 16 * b))
+            ts(A("T", 32 * a, 32 * b), A("T", 32 * a, 32 * b), 8191, O.bitwise_and)
+            cp(A("OT", 32 * a, 32 * b), A("T", 32 * a, 32 * b))
+        act(A("UU", 0, 64, 2), A("UF", 32, 64), F.Copy, None, 64.0)
+        act(A("UU", 1, 64, 2), A("UF", 32, 64), F.Copy)
+
+    def gathers(t):
+        Q, n3 = "Q%d" % t, 0
+        for k, (a, b) in enumerate(KB):
+            mm(A("B%d" % k, 0, 64 * (b - a)), o128, A("Pat", 64 * a, 64 * b), True)
+        for m in range(16):
+            k = [i for i, (a, b) in enumerate(KB) if a <= m < b][0]
+            a, b = KB[k]
+            cuts = ((0, 256), (256, 512)) if m >= 14 else ((0, 512),)
+            for (lo, hi) in cuts:
+                o = 512 * m
+                src, h = IX(A("X"), A("OT", 32 * m + lo // 16, 32 * m + hi // 16)), A(Q, QG + lo, QG + hi)
+                a0, ab = A("A0", o + lo, o + hi), A("Ab", o + lo, o + hi)
+                if PATH[m] == 3:
+                    bank, x = A("B%d" % (3 + n3 % 2), 0, hi - lo), A("xq", 512 * (n3 % 2), 512 * (n3 % 2) + hi - lo)
+                    n3 += 1
+                    act(x, src, F.Copy)
+                    mm(bank, A("nidb"), h, True)
+                    mm(bank, A("idb"), x, False)
+                    act(ab, bank, F.Abs)
+                else:
+                    tt(a0, src, h, O.subtract)
+                    if PATH[m] == 2:
+                        act(ab, a0, F.Abs)
+                    else:
+                        ts(ab, a0, 0.0, O.max)
+                for c in range(lo // 128, hi // 128):
+                    w = b - a
+                    out = A("B%d" % k, c * 16 * w + m - a, (c + 1) * 16 * w, w)
+                    if PATH[m] == 1:
+                        mm(out, A("A0", o + 128 * c, o + 128 * c + 128), A("O16n"), False)
+                    mm(out, A("Ab", o + 128 * c, o + 128 * c + 128), A("O16d" if PATH[m] == 1 else "O16"), False)
+            if m == b - 1:
+                scan(A("KS", 64 * a, 64 * b), A("rsA" if b - a == 8 else "rsB"), A("B%d" % k, 0, 64 * (b - a)), 0.0, O.max, O.min)
+        tt(A("KAB"), A("KS", 7, 512, 8), A("KS", 515, 768, 4), O.min)
+        tt(A("Ki"), A("KAB"), A("KS", 771, 1024, 4), O.min)
+
+    def utable(t):
+        for c in range(4):
+            o = c * 128
+            mm(A("B6", o, o + 128), A("SG", 2048 + o, 2048 + o + 128), A("Pm"), c == 0)
+            if t:
+                mm(A("B6", o, o + 128), A("SG", (t - 1) * 512 + o, (t - 1) * 512 + o + 128), A("Pm"), False)
+        act(A("RV1"), A("B6"), F.Identity, A("b2"), 1.0 if t else 2.0)
+        mm(A("B7"), A("o32", 0, 128, 1, 0, 64), A("IO", 0, 512, 1, 0, 64), True)
+        for c in range(4):
+            mm(A("B7", (3 - c) * 128, (3 - c) * 128 + 128), A("RV1", c * 128, c * 128 + 128), A("Jm"), False)
+        scan(A("oks"), A("B7"), A("oneb"), -16384.0, O.max, O.mult)
+        act(A("tot"), A("oks", 511, 512), F.Identity, A("b512"))
+        act(A("dg"), A("idf"), F.Copy, None, A("tot"))
+        mm(A("B6", 0, 128), A("onef"), A("dg"), True)
+        mm(A("B6", 128, 129), A("sel15"), A("SG", t * 512 - 1, t * 512) if t else A("neg1"), False)
+        tt(A("cmx", 0, 129), A("B6", 0, 129), A("cm", 0, 129), O.mult)
+        add("v", [A("cry")], [A("cmx", 0, 129)], lambda s: V.tensor_reduce(A("cry")[0], A("cmx", 0, 129)[0], AxisListType.X, O.max), 129 * CY)
+        ts(A("Ut"), A("oks"), A("b512"), O.add, A("cry"), O.max)
+        dma(A("Urep", 0, 8192, 1, 0, 128, 16), A("Ut"), 0.6)
+
+    def choose():
+        ts(A("kp"), A("Ki"), 63, O.bitwise_and)
+        ts(A("DI"), A("Ki", 0, 64, 2), 10, O.logical_shift_right)
+        tt(A("pr"), A("kp"), A("UU"), O.mult)
+        tt(A("f1"), A("DI"), A("thS"), O.is_lt)
+        tt(A("tf"), A("pr", 0, 64, 2), A("pr", 1, 64, 2), O.add)
+        ts(A("lim"), A("f1"), 8096.0, O.mult)
+        tt(A("tc"), A("tf"), A("FF", 32, 64), O.add)
+        ts(A("cI"), A("tc"), 8191, O.bitwise_and)
+        tt(A("fit"), A("cI"), A("lim"), O.is_lt)
+        mm(A("B3", 0, 32), A("tri"), A("fit"), True)
+        mm(A("B3", 8, 32), o128, A("fit", 0, 24), False)
+        mm(A("B3", 16, 32), o128, A("fit", 0, 16), False)
+        mm(A("B3", 24, 32), o128, A("fit", 0, 8), False)
+        for v, n in ((16, "cI"), (18, "DI")):
+            cp(A("VZ", v, 1040, 32), A(n))
+            tt(A("VZ", v + 1, 1040, 32), A(n), A("VZ", v, 1040, 32), O.subtract)
+        tt(A("rsel"), A("B3", 0, 32), A("fit"), O.mult)
+        mm(A("B4", 0, 65), A("zb"), A("i65", 0, 65), True)
+        for c in range(32):
+            st = A("ST", c * 66, c * 66 + 65)
+            if c in SSEL:
+                act(st, A("n65", 0, 65), F.Sign, A("rsel", c, c + 1))
+            else:
+                ts(st, A("i65", 0, 65), A("rsel", c, c + 1), O.is_le, 2.0, O.mult)
+            w, p = 16 + 32 * c - 16 * (c % 2), 32 * (c % 8 // 2)
+            mm(A("B4", 0, 65, 1, p, p + 32), A("VZ", w, w + 32), st, False)
+        cp(A("Pc"), A("B4", 1, 65))
+        tt(A("Pd"), A("B4", 0, 64), A("Pc"), O.subtract)
+        mm(A("B0", 0, 64), A("Cc"), A("Pd"), True)
+        mm(A("B0", 64, 128), A("Ck"), A("Pd"), False)
+        for k in range(4):
+            mm(A("B0", 128 + 64 * k, 192 + 64 * k), A("Cq"), A("Pd"), False)
+        mm(A("B0", 384, 448), A("Cs"), A("Pd"), False)
+
+    def wrap(a, b, src):
+        n = src[2]
+        tt(A(a, 0, n), src, A("mW", 0, n), O.mult)
+        scan(A(b, 0, n), A("z16", 0, n), A(a, 0, n), 0.0, O.mult, O.add)
+        return A(b, 15, n, 16)
+
+    def marks(k, c):
+        ts(A("hs", k, k + 4), A("ts_", k, k + 4), M512, O.add, M512, O.subtract)
+        tt(A("nb", k, k + 4), A("hs", k, k + 4), A("ts_", k, k + 4), O.subtract)
+        for i in range(k, k + 4):
+            hh = A("HH", 128 * i, 128 * i + 128)
+            act(A("sgn", 512 * i, 512 * i + 512), A("j255"), F.Sign, A("nb", i, i + 1))
+            ts(hh, A("Bp"), A("hs", i, i + 1), O.is_equal, c, O.mult)
+            mm(A("B5"), hh, A("sgn", 512 * i, 512 * i + 512), i == 0)
+
+    def give(t):
+        Q, C = "Q%d" % t, "C%d" % t
+        wrap("tmA", "tmB", A("B0", 0, 128))
+        cW = A("tmB", 15, 64, 16)
+        for k in range(4):
+            ts(A("EQ", 64 * k, 64 * k + 64), A("B0", 0, 64), A("tmB", 15 + 16 * k, 16 + 16 * k), O.is_equal)
+        tt(A("EQ"), A("EQ"), A("B0", 128, 384), O.mult)
+        sW = wrap("tsA", "tsB", A("B0", 384, 448))
+        scan(A("SC"), A("rs64"), A("EQ"), 0.0, O.max, O.min)
+        tt(A("win"), A("SC", 63, 256, 64), A("tmB", 79, 128, 16), O.is_gt)
+        mm(A("B1", 0, 5), A("idb"), A("Jc", 0, 5), True)
+        mm(A("B1", 0, 4), A("tB"), A("win"), False)
+        for k in range(4):
+            mm(A("B1", k, k + 1), A("Mk", 128 * k, 128 * k + 128), A("win", k, k + 1), False)
+            mm(A("B1", k + 1, 5), A("BM"), A("win", 0, 4 - k), False)
+        ts(A("mC"), A("cvec"), A("B1", 4, 5), O.mult)
+        remote("lC%d" % t, [(rank ^ 1, eP, A("mC"), A(C, 0, 4), "cP%d" % t), (rank ^ 4, eT, A("mC"), A(C, 4, 8), "cT%d" % t)])
+        cp(A("pos"), A("B1", 0, 4))
+        tt(A("t0"), sW, A("B1", 0, 4), O.subtract)
+        sct(A("SW"), A("pos"), A("ia64"))
+        cp(A("INV"), wrap("swA", "swB", A("SW", 0, 64)))
+        ts(A("OFU"), cW, -1.0, O.mult, 8239.0, O.add)
+        act(A("UG", 0, 64), IX(A("Urep"), A("OFU")), F.Copy)
+        mm(A("B6", 0, 64), A("rself"), A("UG", 0, 64))
+        r1 = wrap("u1A", "u1B", A("B6", 0, 64))
+        ts(A("OF2"), r1, -9.0, O.add, 0.0, O.max)
+        act(A("UG", 64, 128), IX(A("Urep"), A("OF2")), F.Copy)
+        mm(A("B7", 0, 64), A("rself"), A("UG", 64, 128))
+        r2 = wrap("u2A", "u2B", A("B7", 0, 64))
+        ts(A("OFX", 0, 4), r1, -1.0, O.mult, 8192.0, O.add)
+        ts(A("OFX", 4, 8), r2, -1.0, O.mult, 8192.0, O.add)
+        act(A("XG", 64, 128), IX(A("X"), A("OFX", 0, 4)), F.Copy)
+        act(A("XG", 128, 192), IX(A("X"), A("OFX", 4, 8)), F.Copy)
+        ts(A("OFP"), cW, -54.0, O.add, 0.0, O.max)
+        act(A("XG", 0, 64), IX(A("X"), A("OFP")), F.Copy)
+        mm(A("B2", 0, 64), A("idb"), A("n1k"), True)
+        mm(A("B2", 0, 64), A("rselb"), A("XG", 0, 64), False)
+        tt(A("XP"), A("XG", 0, 64), A("B2", 0, 64), O.max)
+        ts(A("OFC"), sW, -184.0, O.add, 0.0, O.max)
+        act(A("XG", 192, 256), IX(A(Q, QG, QG + 512), A("OFC")), F.Copy)
+        ts(A("mP"), IX(A("XP"), A("INV")), 255.0, O.min)
+        remote("lP%d" % t, [(rank ^ 1, eP, A("mP"), A(Q, 0, 64), "aP%d" % t)])
+        act(A("mT", 0, 64), IX(A("XG", 64, 128), A("INV")), F.Copy)
+        cp(A("mT", 64, 128), IX(A("XG", 128, 192), A("INV")))
+        remote("lT%d" % t, [(rank ^ 4, eT, A("mT"), A(Q, 64, 192), "aT%d" % t)])
+        act(A(Q, QG + 512, QW), IX(A("XG", 192, 256), A("INV")), F.Copy)
+        ts(A("ts_", 0, 4), cW, -319.5, O.add)
+        marks(0, 4096.0)
+        ts(A("ts_", 4, 8), r2, -1.0, O.mult, 7937.5, O.add)
+        marks(4, -4096.0)
+        for i in range(8):
+            mm(A("B2", 64, 65), A("HH", 128 * i, 128 * i + 128), A("oneb", 0, 1), i == 0)
+        ts(A("TBc"), A("TriB"), A("B2", 64, 65), O.mult)
+        mm(A("B5"), A("TBc"), A("oneb"), False)
+        if t < RO - 1:
+            tt(A("x0c"), A("x0c"), A("B5"), O.max)
+            dma(A("X", 0, 8192, 1, 0, 128, 16), A("x0c"))
+            act(A("SG", t * 512, t * 512 + 512), A("x0c"), F.Sign, A("bB"))
+        else:
+            mm(A("B5"), A("idb"), A("Rb"), False)
+            tt(A("Yt"), A("Z4"), A("B5"), O.min)
+            dma(hbm(T.yc[:, :]), A("Yt"), 0.6)
+
+    def merge(t):
+        Q, C = "Q%d" % t, "C%d" % t
+        nP, dP, nT, dT, n2 = A(C, 0, 1), A(C, 1, 2), A(C, 4, 5), A(C, 5, 6), A(C, 6, 7)
+        ts(A("t1"), A("t0"), nP, O.add, n2, O.add)
+        ts(A("h16"), A("t1"), M16, O.add, M16, O.subtract)
+        ts(A("S1", 0, 32), A("iW", 0, 32), nP, O.is_ge, dP, O.mult)
+        ts(A("S1", 32, 64), A("iW", 32, 64), nP, O.subtract, nT, O.is_ge)
+        ts(A("S1", 64, 96), A("iW", 64, 96), nP, O.subtract, n2, O.is_ge)
+        act(A("dT"), A("idb"), F.Copy, None, dT)
+        out = A("B3", 0, 32)
+        mm(out, A("idb"), A("B16"), True)
+        mm(out, A("idb"), A("S1", 0, 32), False)
+        mm(out, A("dT"), A("S1", 32, 64), False)
+        mm(out, A("dT"), A("S1", 64, 96), False)
+        for k in range(4):
+            h = A("h16", k, k + 1)
+            act(A("SS", 32 * k, 32 * k + 32), A("nB16"), F.Sign, h)
+            mm(out, A("nBMh"), A("SS", 32 * k, 32 * k + 32), False)
+            ts(A("LL", 128 * k, 128 * k + 128), A("Rp"), h, O.add, A("t1", k, k + 1), O.is_ge)
+            ts(A("EE", 32 * k, 32 * k + 32), A("B16"), h, O.is_equal)
+            mm(out, A("LL", 128 * k, 128 * k + 128), A("EE", 32 * k, 32 * k + 32), False)
+        ts(A("MI"), out, A("r32"), O.add, A("mC", 0, 1), O.add)
+        a, b = IX(A(Q), A("MI", 0, 16)), IX(A(Q), A("MI", 16, 32))
+        if t < RO - 1:
+            cp(A("Q%d" % (t + 1), QG, QG + 256), a)
+            act(A("Q%d" % (t + 1), QG + 256, QG + 512), b, F.Copy)
+        else:
+            ts(A("Gn", 0, 256), a, -1.0, O.mult, 255.0, O.add)
+            act(A("Gn", 256, 512), b, F.Identity, 255.0, -1.0)
+            dma(hbm(T.yg[:, :]), A("Gn"))
+
+    early[0] = 1000.0
+    consts()
+    for t in range(RO):
+        early[0] = 0.0 if t else 2000.0
+        weights(t)
+        lists(t)
+        early[0] = 0.0
+        if t == 0:
+            for k in range(8):
+                iota(A("Urep", 1032 * k, 1032 * k + 1032), [[0, 1032]], 0, 0)
+        utable(t)
+        if t == RO - 1:
+            for k in range(3):
+                mm(A("B7"), A("idb"), A("SG", k * 512, k * 512 + 512), k == 0)
+            act(A("Z4"), A("B7"), F.Identity, 2.5, -0.5)
+            act(A("Rb"), A("x0c"), F.Relu, A("bB"))
+        gathers(t)
+        choose()
+        give(t)
+        merge(t)
+
+    if "order" not in _order:
+        _order["order"] = _lay_out(ops)
+    order = _order["order"]
+    place = {i: k for k, i in enumerate(order)}
+    count, done = {}, {}
+    known = {q: {} for q in queues}
+    for i in order:
+        o = ops[i]
+        q = o["q"]
+        if q == "r":
+            count[o["sem"]] = -o["inc"]
+            done[i] = (o["sem"], -o["inc"], {})
+            continue
+        w = {}
+        for j in o["dep"]:
+            if j in o["ord"] or (q == "t" and ops[j]["q"] == "t"):
+                continue
+            sem, n, snap = done[j]
+            if known[q].get(sem, 0) < n and w.get(sem, (0,))[0] < n:
+                w[sem] = (n, snap)
         for sem in sorted(w, key=lambda s: -len(w[s][1])):
             n, snap = w[sem]
             if known[q].get(sem, 0) >= n:
@@ -85,542 +668,12 @@ def rank_program(g, core, T, topo):
             for k in snap:
                 known[q][k] = max(snap[k], known[q].get(k, 0))
             known[q][sem] = n
-
-    def note(q, reads, writes, sem, n, snap):
-        for regs, isw in ((reads, False), (writes, True)):
-            for r in regs:
-                L = log.setdefault(r[0], [])
-                if isw:
-                    L[:] = [e for e in L if not (e[0][1] >= r[1] and e[0][2] <= r[2] and r[3] == 1 and e[0][4] >= r[4] and e[0][5] <= r[5])]
-                else:
-                    L[:] = [e for e in L if not (e[2] == q and not e[1] and e[0] == r and q in own)]
-                L.append((r, isw, q, sem, n, snap))
-
-    def rg(xs):
-        return [r for x in xs if isinstance(x, tuple) for r in x[1]]
-
-    def ap(x):
-        return x[0] if isinstance(x, tuple) else x
-
-    def run(q, outs, ins, f):
-        r, w, s = rg(ins), rg(outs), own[q]
-        need(q, r, w)
-        count[s] = count.get(s, 0) + 1
-        f().then_inc(T.sem[s], 1)
-        note(q, r, w, s, count[s], dict(known[q]))
-
-    V, SE, PE = g.vector, g.scalar, g.tensor
-
-    def cp(o, i):
-        run("v", [o], [i], lambda: V.tensor_copy(ap(o), ap(i)))
-
-    def sct(win, off, i):
-        run("v", [win], [off, i], lambda: V.tensor_copy(win[0].indirect(off[0]), ap(i)))
-
-    def tt(o, a, b, op):
-        run("v", [o], [a, b], lambda: V.tensor_tensor(ap(o), ap(a), ap(b), op))
-
-    def ts(o, a, s1, op0, s2=None, op1=None):
-        if op1 is None:
-            run("v", [o], [a, s1], lambda: V.tensor_scalar(ap(o), ap(a), ap(s1), None, op0))
-        else:
-            run("v", [o], [a, s1, s2], lambda: V.tensor_scalar(ap(o), ap(a), ap(s1), ap(s2), op0, op1))
-
-    def scan(o, a, b, init, op0, op1):
-        run("v", [o], [a, b, init], lambda: V.tensor_tensor_scan(ap(o), ap(a), ap(b), ap(init), op0, op1))
-
-    def ms(o, c):
-        run("v", [o], [], lambda: V.memset(ap(o), c))
-
-    def act(o, i, f, bias=None, scale=None):
-        kw = {}
-        if bias is not None:
-            kw["bias"] = ap(bias)
-        if scale is not None:
-            kw["scale"] = ap(scale)
-        run("s", [o], [i, bias, scale], lambda: SE.activation(ap(o), ap(i), f, **kw))
-
-    def mm(o, l, r, start=True, stop=True):
-        run("t", [o], [l, r], lambda: PE.matmul(ap(o), ap(l), ap(r), start, stop))
-
-    def iota(o, pat, base, ch, small=True):
-        kw = {"allow_small_or_imprecise_dtypes": True} if small else {}
-        run("g", [o], [], lambda: g.iota(ap(o), pat, base, ch, **kw))
-
-    def sel(o, i, pat, op, base, ch):
-        run("g", [o], [i], lambda: g.affine_select(ap(o), ap(i), pat, op, 0.0, base, ch))
-
-    nd = [0]
-
-    def dma(q, o, i):
-        r, w = rg([i]), rg([o])
-        need(q, r, w)
-        s = "d%d" % nd[0]
-        nd[0] += 1
-        queues[q].dma_start(ap(o), ap(i)).then_inc(T.sem[s], 16)
-        count[s] = 16
-        note("d" + s, r, w, s, 16, dict(known[q]))
-
-    dma("y", A("Q0", QG, QG + 512), (T.gd[:, :], []))
-    dma("y", A("wti"), (T.wt[:, :], []))
-    dma("y", A("kmi"), (T.km[:, :], []))
-    dma("y", A("x0c"), (T.xs[0:128:16, :], []))
-    dma("y", A("thi"), (T.th[:, :], []))
-    dma("y", A("X"), (T.xs[:, :], []))
-    o128 = A("oneb", 0, 128)
-
-    def weights(t):
-        act(A("Wff"), A("BMgf"), F.Copy, None, A("wf", t, t + 1))
-        act(A("Wf"), A("BMgf"), F.Copy, None, A("wf", t, t + 1))
-        for q in range(8):
-            act(A("Lw", 16 * q, 16 * q + 1936, 129), A("oneb", 0, 16), F.Copy, None, A("Wff", q, q + 1))
-
-    def consts0():
-        ms(A("oneb"), 1.0)
-        sel(A("BM"), o128, [[-16, 8], [0, 16]], O.is_ge, 0, 1)
-        sel(A("BM"), A("BM"), [[16, 8], [0, 16]], O.is_ge, 15, -1)
-        iota(A("pi"), [[0, 1]], 0, 1, False)
-        iota(A("iM"), [[64, 16]], 0, 0)
-        ms(A("Lw"), 0.0)
-        ms(A("onef"), 1.0)
-        cp(A("wf"), A("wti"))
-        cp(A("BMgf"), A("BM", 0, 128, 16))
-        weights(0)
-        cp(A("kf"), A("kmi"))
-
-    def consts1():
-        ms(A("c16"), 0.0625)
-        ms(A("rs16"), 0.0)
-        ms(A("rs16", 0, 512, 16), BIG)
-        ts(A("O16", 0, 16, 2), A("BMgf"), 1024.0, O.mult)
-        ts(A("O16", 1, 16, 2), A("BMgf"), 1024.0, O.mult)
-        ts(A("kA"), A("kmi"), 6, O.logical_shift_right)
-        ts(A("kB"), A("kmi"), 63, O.bitwise_and)
-        cp(A("kAf"), A("kA"))
-        cp(A("kBf"), A("kB"))
-        for q in range(8):
-            m = A("BMgf", q, q + 1)
-            act(A("Kpat", q * 32, q * 32 + 16), A("kAf"), F.Copy, None, m)
-            act(A("Kpat", q * 32 + 16, q * 32 + 32), A("kBf"), F.Copy, None, m)
-            act(A("Mpat", q * 32, q * 32 + 16), A("iM"), F.Copy, None, m)
-            act(A("Mpat", q * 32 + 16, q * 32 + 32), A("iM"), F.Copy, None, m)
-        act(A("Kpat", 256, 512), A("Kpat", 0, 256), F.Copy)
-        act(A("Mpat", 256, 512), A("Mpat", 0, 256), F.Copy)
-
-    def consts2():
-        sel(A("idf"), A("onef", 0, 128), [[-1, 128]], O.is_equal, 0, 1)
-        sel(A("Pm"), o128, [[-16, 8], [1, 16]], O.is_equal, -15, 1)
-        sel(A("Jm"), o128, [[1, 128]], O.is_equal, -127, 1)
-        iota(A("i512"), [[1, 512]], 0, 0)
-        sel(A("cm"), A("onef", 0, 128), [[-1, 128]], O.is_gt, 0, 1)
-        sel(A("tri"), o128, [[1, 128]], O.is_ge, 0, -1)
-        sel(A("tB"), A("onef", 0, 128), [[1, 128]], O.is_gt, 0, -1)
-        iota(A("i64f"), [[1, 64]], 1, 0)
-        iota(A("tA"), [[0, 8], [1, 16]], 5, 0)
-        iota(A("iW"), [[16, 32]], 0, 0)
-        iota(A("dW"), [[16, 4]], 706, 0)
-        iota(A("aW"), [[1, 2], [16, 4]], 0, 0)
-        iota(A("slS"), [[128, 4], [0, 8]], 1, 1, False)
-        iota(A("Urep"), [[0, 8256]], 0, 0)
-        iota(A("Dw"), [[0, DW]], 0, 0)
-        ms(A("bA"), 191.5)
-        ms(A("bB"), -256.0)
-        act(A("SG", 2048, 2560), A("x0c"), F.Sign, A("bA"), -1.0)
-        act(A("idb"), A("idf"), F.Copy)
-        act(A("Jm"), A("Jm"), F.Copy, None, -16384.0)
-        ts(A("pj"), A("pi"), 15, O.bitwise_and)
-        cp(A("rcol"), A("pj"))
-        ts(A("b512"), A("rcol"), 512.0, O.mult)
-        ts(A("pj"), A("pi"), 63, O.bitwise_and)
-        ts(A("acol"), A("pj"), -262144.0, O.add)
-        tt(A("cm"), A("cm"), A("BM"), O.mult)
-
-    def consts3():
-        act(A("Lsel"), A("Lw"), F.Copy, None, 0.0)
-        for q in range(8):
-            act(A("Lsel", 16 * q, 16 * q + 1936, 129), A("c16", 0, 16), F.Copy, None, A("BMgf", q, q + 1))
-        act(A("i64b"), A("i64f"), F.Copy)
-        tt(A("id2"), A("idf", 0, 64), A("idf", 64, 128), O.add)
-        tt(A("t32"), A("id2", 0, 32), A("id2", 32, 64), O.add)
-        for k in range(4):
-            tt(A("mW", 16 * k, 16 * k + 16), A("t32", 0, 16), A("t32", 16, 32), O.add)
-        ms(A("c16f"), 0.0625)
-        ms(A("z16"), 1.0)
-        ms(A("z16", 0, 128, 16), 0.0)
-        ms(A("rs64"), -BIG)
-        ms(A("rs64", 0, 256, 64), BIG)
-        cp(A("tri2"), A("tri"))
-        ms(A("tri2", 64, 128, 1, 0, 64), 0.0)
-        ms(A("BO2"), 0.0)
-        ms(A("BO2", 0, 64, 1, 0, 64), 1.0)
-        ms(A("BO2", 64, 128, 1, 64, 128), 1.0)
-        ms(A("maskJ"), 0.0)
-        for j in range(4):
-            for h in range(2):
-                c = j * 128 + (2 * j + h) * 16
-                ms(A("maskJ", c, c + 16, 1, 64 * h, 64 * h + 64), 1.0)
-        ts(A("bs"), A("rcol"), 0.0, O.is_equal)
-        ts(A("rself"), A("BM"), A("bs"), O.mult)
-        cp(A("rselb"), A("rself"))
-        tt(A("tA"), A("tA"), A("BM"), O.mult)
-        ts(A("Bpat"), A("tA"), -5.0, O.add)
-        tt(A("tA"), A("tB"), A("tri"), O.add)
-        tt(A("TriB"), A("tA"), A("BM"), O.mult)
-        ts(A("iW"), A("iW"), A("rcol"), O.add)
-        ts(A("dW"), A("dW"), A("rcol"), O.add)
-        ts(A("aW"), A("aW"), A("rcol"), O.add)
-        ts(A("slL"), A("slS"), 63, O.bitwise_and)
-        cp(A("VL", 160, 192), A("slL"))
-        tt(A("VL", 64, 96), A("slS"), A("slL"), O.subtract)
-        ms(A("mP"), 0.0)
-        ms(A("mT"), 0.0)
-        ms(A("OE"), 0.0)
-        cp(A("thr"), A("thi"))
-        ts(A("tA", 0, 8), A("BMgf"), A("thr"), O.mult)
-        mm(A("B6", 0, 8), A("c16f"), A("tA", 0, 8))
-        for b in range(4):
-            cp(A("thS", 8 * b, 8 * b + 8), A("B6", 0, 8))
-
-    def p1a(t, ch):
-        bank, Q, o = "B2" if ch == 0 else "B4", "Q%d" % t, QG + 256 * ch
-        w, s = (0, 16) if ch == 0 else (16, 0)
-        for r in range(16):
-            mm(A(bank, w, w + 16), A("Lw", r * 128, r * 128 + 128), A(Q, o + r, o + 256, 16), r == 0, r == 15)
-        for b in range(2):
-            mm(A(bank, s + 8 * b, s + 8 * b + 8), A(Q, o + 128 * b, o + 128 * b + 128), A("Wf"))
-
-    def p1b(ch):
-        a, b = 32 * ch, 32 * ch + 32
-        cp(A("ui", a, b), A("B2" if ch == 0 else "B4", 0, 32))
-        ts(A("U", a, b), A("ui", a, b), 4095, O.bitwise_and)
-        tt(A("sq", a, b), A("U", a, b), A("U", a, b), O.mult)
-        cp(A("UF", a, b), A("U", a, b))
-        ts(A("Fi", a, b), A("sq", a, b), 5, O.logical_shift_right)
-        cp(A("FF", a, b), A("Fi", a, b))
-
-    def lists(ch):
-        for b in range(16):
-            k = b + 48 * ch
-            u, f = A("UF", k, k + 1), A("FF", k, k + 1)
-            if ch:
-                act(A("T1f", b, 256, 16), A("kf"), F.Identity, f, u)
-            else:
-                ts(A("T0", b, 256, 16), A("kf"), u, O.mult, f, O.add)
-
-    def lists2(ch):
-        n = "T%d" % ch
-        if ch:
-            cp(A("T1"), A("T1f"))
-        ts(A(n), A(n), 8191, O.bitwise_and)
-        cp(A("O" + n), A(n))
-
-    def reps0(t):
-        for k in range(4):
-            act(A("Gr0", 256 * k, 256 * k + 256), A("Q%d" % t, QG, QG + 256), F.Copy)
-
-    def reps1(t):
-        for k in range(4):
-            dma("y", A("Gr1", 256 * k, 256 * k + 256), A("Q%d" % t, QG + 256, QG + 512))
-
-    def patterns(ch):
-        mm(A("B%d" % ch), A("c16"), A("Kpat"), True, False)
-        mm(A("B%d" % ch), A("c16"), A("Mpat"), False, False)
-
-    def sums(ch, m0, m1, last):
-        for m in range(m0, m1):
-            for b in range(2):
-                a = ch * 4096 + m * 256 + b * 128
-                mm(A("B%d" % ch, b * 256 + m, b * 256 + m + 241, 16), A("Ab", a, a + 128), A("O16"), False, last and m == m1 - 1 and b == 1)
-
-    def gather(ch, m0, m1, last=False):
-        n, o = (m1 - m0) * 256, ch * 4096 + m0 * 256
-        tt(A("A0", o, o + n), IX(A("X"), A("OT%d" % ch, m0 * 16, m1 * 16)), A("Gr%d" % ch, 0, n), O.add)
-        act(A("Ab", o, o + n), A("A0", o, o + n), F.Abs, -255.0)
-        sums(ch, m0, m1, last)
-
-    def sgather(m0, bank, k):
-        act(A("xs2", 512 * k, 512 * k + 512), IX(A("X"), A("OT1", m0 * 16, m0 * 16 + 32)), F.Copy)
-        mm(A(bank), A("idb"), A("xs2", 512 * k, 512 * k + 512), True, False)
-        mm(A(bank), A("idb"), A("Gr1", 0, 512), False, True)
-
-    def sgather2(m0, bank):
-        o = 4096 + m0 * 256
-        act(A("Ab", o, o + 512), A(bank), F.Abs, -255.0)
-        sums(1, m0, m0 + 2, False)
-
-    def lowest(ch):
-        scan(A("KS%d" % ch), A("rs16"), A("B%d" % ch), 0.0, O.max, O.min)
-        cp(A("Ki", 32 * ch, 32 * ch + 32), A("KS%d" % ch, 15, 512, 16))
-
-    def decode():
-        ts(A("kp"), A("Ki"), 63, O.bitwise_and)
-        ts(A("CD", 32, 64), A("Ki", 0, 64, 2), 10, O.logical_shift_right)
-        tt(A("pr"), A("kp"), A("UU"), O.mult)
-        tt(A("f1"), A("CD", 32, 64), A("thS"), O.is_lt)
-        tt(A("tf"), A("pr", 0, 64, 2), A("pr", 1, 64, 2), O.add)
-        tt(A("tc"), A("tf"), A("FF", 16, 48), O.add)
-        ts(A("tt"), A("tc"), 8191, O.bitwise_and)
-        ts(A("CD", 0, 32), A("tt"), 64.0, O.add)
-        ts(A("f2"), A("tt"), 8096.0, O.is_lt)
-        tt(A("fit"), A("f1"), A("f2"), O.mult)
-
-    def choose():
-        mm(A("B2", 0, 32), A("tri"), A("fit"), True, False)
-        mm(A("B2", 8, 32), o128, A("fit", 0, 24), False, False)
-        mm(A("B2", 16, 32), o128, A("fit", 0, 16), False, False)
-        mm(A("B2", 24, 32), o128, A("fit", 0, 8), False, True)
-        ts(A("CDl"), A("CD"), 63, O.bitwise_and)
-        tt(A("VL", 0, 64), A("CD"), A("CDl"), O.subtract)
-        cp(A("VL", 96, 160), A("CDl"))
-        tt(A("rsel"), A("B2", 0, 32), A("fit"), O.mult)
-        for q in range(8):
-            for b in range(4):
-                c = b * 8 + q
-                ts(A("OH", c * 64, c * 64 + 64), A("i64b"), A("rsel", c, c + 1), O.is_equal)
-                h, j = q % 2, q // 2
-                mm(A("B3", j, j + 21, 4, 64 * h, 64 * h + 64), A("OH", c * 64, c * 64 + 64), A("VL", c, c + 161, 32), b == 0, b == 3)
-
-    def resolve():
-        cp(A("Ls"), A("B3", 0, 24))
-        tt(A("cds"), A("Ls", 0, 12), A("Ls", 12, 24), O.add)
-
-        def diag(to, col):
-            for j in (2, 3):
-                act(A("DG", to + 64 * j, to + 64 * j + 64), A("id2"), F.Copy, None, A(col, j, j + 1))
-            for j in (0, 1):
-                ts(A("DG", to + 64 * j, to + 64 * j + 64), A("id2"), A(col, j, j + 1), O.mult)
-
-        diag(0, "cds")
-        mm(A("B4", 0, 256), A("BO2"), A("DG", 0, 256))
-        ts(A("Vp"), A("cds", 4, 8), 64.0, O.mult, A("acol"), O.add)
-        diag(256, "Vp")
-        mm(A("B5", 0, 256), A("BO2"), A("DG", 256, 512))
-        ts(A("E5"), A("cds", 0, 4), 1024.0, O.mult)
-        tt(A("E5"), A("E5"), A("cds", 8, 12), O.add)
-        ts(A("vm"), A("cds", 0, 4), 64.0, O.is_ge)
-        for j in range(4):
-            ts(A("EQ", 64 * j, 64 * j + 64), A("B4", 64 * j, 64 * j + 64), A("cds", j, j + 1), O.is_equal)
-        tt(A("EQ"), A("EQ"), A("B5", 0, 256), O.mult)
-        scan(A("SC"), A("rs64"), A("EQ"), 0.0, O.max, O.min)
-        tt(A("win"), A("SC", 63, 256, 64), A("Vp"), O.is_equal)
-        tt(A("OE", 65, 264, 66), A("win"), A("vm"), O.mult)
-        mm(A("B3", 32, 36), A("tri2"), A("OE", 65, 264, 66))
-        tt(A("rid"), A("B3", 32, 36), A("OE", 65, 264, 66), O.mult)
-        for j in range(4):
-            ts(A("OE", 66 * j, 66 * j + 64), A("i64f"), A("rid", j, j + 1), O.is_equal, A("E5", j, j + 1), O.mult)
-            mm(A("B6", 0, 66), A("maskJ", 128 * j, 128 * j + 128), A("OE", 66 * j, 66 * j + 66), j == 0, j == 3)
-
-    def wrap(src, src2=None):
-        tt(A("tmA", 0, 64), src, A("mW"), O.mult)
-        if src2 is not None:
-            tt(A("tmA", 64, 128), src2, A("mW"), O.mult)
-        n = 64 if src2 is None else 128
-        scan(A("tmB", 0, n), A("z16", 0, n), A("tmA", 0, n), 0.0, O.mult, O.add)
-        return A("tmB", 15, n, 16)
-
-    def send(t, what):
-        dst = T.cores[rank ^ (1 if what == "P" else 4)]
-        e = topo.engines(core, dst)
-        e = e[8:16] if what == "P" else e[:8]
-        rid, pid, _ = topo.addr(dst)
-        src = A("m" + what)
-        land = A("Q%d" % t, 0, 72) if what == "P" else A("Q%d" % t, 72, QG)
-        need("g", src[1], [])
-        la, aa = "l%s%d" % (what, t), "a%s%d" % (what, t)
-        g.remote_dma(out_ap=land[0], in_ap=src[0], remote_sem=T.sem[aa], local_sem=T.sem[la], pid=pid, routing_id=rid, dma_engine_mask=sum(1 << x for x in e))
-        count[la] = count[aa] = len(e)
-        note("r", src[1], [], la, len(e), dict(known["g"]))
-        note("r", [], land[1], aa, len(e), {})
-
-    def marks(k):
-        ts(A("hiI", k, k + 4), A("PL", k, k + 4), 9, O.arith_shift_right)
-        ts(A("loI", k, k + 4), A("PL", k, k + 4), 511, O.bitwise_and)
-        ts(A("loF", k, k + 4), A("loI", k, k + 4), -1.0, O.mult, 0.5, O.add)
-        cp(A("hiF", k, k + 4), A("hiI", k, k + 4))
-        for i in range(k, k + 4):
-            act(A("sgn", 512 * i, 512 * i + 512), A("i512"), F.Sign, A("loF", i, i + 1))
-
-    def blocks(k):
-        for i in range(k, k + 4):
-            ts(A("HH", 128 * i, 128 * i + 128), A("Bpat"), A("hiF", i, i + 1), O.is_equal, 4096.0 if k == 0 else -4096.0, O.mult)
-
-    def cover(k):
-        for i in range(k, k + 4):
-            mm(A("B5"), A("HH", 128 * i, 128 * i + 128), A("sgn", 512 * i, 512 * i + 512), i == 0, i == 7)
-
-    def give(t):
-        n = A("B6", 65, 66)
-        cp(A("EW"), wrap(A("B6", 0, 64), A("B6", 1, 65)))
-        ts(A("cW"), A("EW", 0, 4), 10, O.logical_shift_right)
-        ts(A("OFF", 4, 8), A("cW"), -1.0, O.mult, 8239.0, O.add)
-        cp(A("UG", 0, 64), IX(A("Urep"), A("OFF", 4, 8)))
-        mm(A("B0", 0, 64), A("rself"), A("UG", 0, 64))
-        act(A("mP", 64, 65), n, F.Copy)
-        act(A("mP", 65, 66), n, F.Copy, 72.0, -1.0)
-        act(A("mT", 128, 129), n, F.Copy)
-        act(A("mT", 129, 130), n, F.Copy, 64.0, -1.0)
-        act(A("mT", 130, 131), n, F.Copy, 72.0, -1.0)
-        ts(A("OFF", 0, 4), A("cW"), -54.0, O.add, 0.0, O.max)
-        cp(A("xg", 0, 64), IX(A("X"), A("OFF", 0, 4)))
-        mm(A("B7", 0, 64), A("rselb"), A("xg", 0, 64))
-        ts(A("yv", 0, 64), A("xg", 0, 64), -1.0, O.mult, 255.0, O.add)
-        ts(A("PL", 0, 4), A("cW"), -64.0, O.add)
-        marks(0)
-        e1 = wrap(A("B0", 0, 64))
-        ts(A("OFF", 16, 20), e1, -8.0, O.add, 0.0, O.max)
-        cp(A("UG", 64, 128), IX(A("Urep"), A("OFF", 16, 20)))
-        mm(A("B1", 0, 64), A("rself"), A("UG", 64, 128))
-        ts(A("OFF", 8, 12), e1, -1.0, O.mult, 8191.0, O.add)
-        ts(A("mk", 0, 64), A("B7", 0, 64), 256.0, O.is_lt)
-        tt(A("mP", 0, 64), A("mk", 0, 64), A("yv", 0, 64), O.mult)
-        send(t, "P")
-        e2 = wrap(A("B1", 0, 64))
-        ts(A("OFF", 12, 16), e2, -1.0, O.mult, 8191.0, O.add)
-        cp(A("xg", 64, 192), IX(A("X"), A("OFF", 8, 16)))
-        mm(A("B7", 64, 192), A("rselb"), A("xg", 64, 192))
-        ts(A("yv", 64, 192), A("xg", 64, 192), -1.0, O.mult, 255.0, O.add)
-        ts(A("PL", 4, 8), e2, -1.0, O.mult, 8192.0, O.add)
-        ts(A("mk", 64, 192), A("B7", 64, 192), 256.0, O.is_lt)
-        tt(A("mT", 0, 128), A("mk", 64, 192), A("yv", 64, 192), O.mult)
-        send(t, "T")
-        marks(4)
-        blocks(0)
-        cover(0)
-        blocks(4)
-        cover(4)
-
-    def order(t):
-        ts(A("s1"), A("EW"), 1023, O.bitwise_and)
-        tt(A("tW"), A("s1"), A("aW"), O.subtract)
-        ts(A("OFC"), A("s1", 0, 4), -1.0, O.add, 0.0, O.max)
-        ts(A("q1"), A("tW", 0, 4), 0.0, O.max)
-        tt(A("isl"), A("tW", 0, 4), A("tW", 4, 8), O.not_equal)
-        tt(A("q2"), A("q1"), A("isl"), O.mult)
-        ts(A("q1"), A("q2"), 0.0, O.is_equal)
-        tt(A("q3"), A("q1"), A("dW"), O.mult)
-        tt(A("q1"), A("q2"), A("q3"), O.add)
-        cp(A("Q%d" % t, QG + 512, QG + 576), IX(A("Q%d" % t, QG, QG + 512), A("OFC")))
-
-    def cut511():
-        cp(A("c511"), A("B5", 511, 512))
-        mm(A("B7", 0, 1), A("TriB"), A("c511"))
-        act(A("bs"), A("B7", 0, 1), F.Copy)
-        act(A("B7"), A("B5"), F.Identity, A("bs"))
-
-    def consume(t):
-        tt(A("x0c"), A("x0c"), A("B7"), O.max)
-        if t < RO - 1:
-            dma("y", A("X", 0, 8192, 1, 0, 128, 16), A("x0c"))
-        act(A("SG", t * 512, t * 512 + 512), A("x0c"), F.Sign, A("bB"))
-
-    def merge(t):
-        Q = "Q%d" % t
-        nP, dP, nT, d2, d3 = A(Q, 64, 65), A(Q, 65, 66), A(Q, 200, 201), A(Q, 201, 202), A(Q, 202, 203)
-        ts(A("mi", 0, 32), A("iW"), nP, O.is_ge, dP, O.mult)
-        tt(A("mi", 32, 64), A("mi", 0, 32), A("iW"), O.add)
-        tt(A("sN", 0, 1), nP, nT, O.add)
-        tt(A("sN", 1, 2), A("sN", 0, 1), nT, O.add)
-        ts(A("A1"), A("sN", 1, 2), -1.0, O.add)
-        ts(A("OFD"), A("q1"), A("A1"), O.add)
-        sct(A("Dw"), A("OFD"), A("i64b"))
-        scan(A("DS"), A("Dw", 0, 512), A("Dw", 0, 512), 0.0, O.max, O.max)
-        for r in range(16):
-            mm(A("B3", 0, 32), A("Lsel", r * 128, r * 128 + 128), A("DS", r, 512, 16), r == 0, r == 15)
-        cut511()
-        ts(A("mi", 64, 96), A("iW"), A("sN", 0, 1), O.is_ge, d2, O.mult)
-        ts(A("mi", 96, 128), A("iW"), A("sN", 1, 2), O.is_ge, d3, O.mult)
-        tt(A("mi", 128, 160), A("mi", 32, 64), A("mi", 64, 96), O.add)
-        tt(A("mi", 160, 192), A("mi", 128, 160), A("mi", 96, 128), O.add)
-        tt(A("mi", 0, 32), A("B3", 0, 32), A("mi", 160, 192), O.add)
-        cp(A("MI"), A("mi", 0, 32))
-        for c in range(2):
-            o = A("Gn", 256 * c, 256 * c + 256) if t == RO - 1 else A("Q%d" % (t + 1), QG + 256 * c, QG + 256 * c + 256)
-            cp(o, IX(A(Q), A("MI", 16 * c, 16 * c + 16)))
-        if t < RO - 1:
-            iota(A("Dw"), [[0, DW]], 0, 0)
-
-    def reverse(t):
-        for c in range(4):
-            mm(A("B6", c * 128, c * 128 + 128), A("SG", t * 512 + c * 128, t * 512 + c * 128 + 128), A("Pm"))
-        act(A("RV1"), A("B6"), F.Copy)
-        for c in range(4):
-            mm(A("B5", (3 - c) * 128, (3 - c) * 128 + 128), A("RV1", c * 128, c * 128 + 128), A("Jm"))
-
-    def utable(first):
-        tt(A("okl"), A("B5"), A("i512") if first else A("okl"), O.min)
-        scan(A("oks"), A("okl"), A("okl"), -16384.0, O.max, O.max)
-        ts(A("tot"), A("oks", 511, 512), A("b512"), O.add)
-        ts(A("dg"), A("idf"), A("tot"), O.mult)
-        mm(A("B7", 0, 128), A("onef", 0, 128), A("dg"))
-
-    def utable2():
-        tt(A("cmx"), A("B7", 0, 128), A("cm"), O.mult)
-        run("v", [A("cry")], [A("cmx")], lambda: V.tensor_reduce(A("cry")[0], A("cmx")[0], AxisListType.X, O.max))
-        ts(A("Ut"), A("oks"), A("b512"), O.add, A("cry"), O.max)
-        dma("y", A("Urep", 0, 8192, 1, 0, 128, 16), A("Ut"))
-
-    for t in range(RO):
-        if t == 0:
-            consts0()
-        else:
-            consume(t - 1)
-        p1a(t, 0)
-        reps0(t)
-        p1a(t, 1)
-        p1b(0)
-        lists(0)
-        lists2(0)
-        p1b(1)
-        lists(1)
-        reps1(t)
-        if t == 0:
-            consts1()
-            consts2()
-            reverse(4)
-        else:
-            reverse(t - 1)
-        patterns(0)
-        if t == 0:
-            lists2(1)
-            consts3()
-        gather(0, 0, 4)
-        if t > 0:
-            lists2(1)
-        patterns(1)
-        act(A("UU", 0, 64, 2), A("UF", 16, 48), F.Copy, None, 64.0)
-        act(A("UU", 1, 64, 2), A("UF", 16, 48), F.Copy)
-        gather(0, 4, 8)
-        sgather(12, "B3", 0)
-        gather(0, 8, 12)
-        sgather2(12, "B3")
-        utable(t == 0)
-        gather(0, 12, 16, True)
-        sgather(14, "B4", 1)
-        gather(1, 0, 4)
-        sgather2(14, "B4")
-        utable2()
-        gather(1, 4, 8)
-        gather(1, 8, 10)
-        gather(1, 10, 11)
-        gather(1, 11, 12, True)
-        if t < RO - 1:
-            weights(t + 1)
-        lowest(0)
-        lowest(1)
-        decode()
-        choose()
-        resolve()
-        give(t)
-        order(t)
-        merge(t)
-    dma("y", (T.yg[:, :], []), A("Gn"))
-    consume(RO - 1)
-    for t in range(RO):
-        mm(A("B5"), A("idb"), A("SG", t * 512, t * 512 + 512), t == 0, t == RO - 1)
-    ts(A("Yt"), A("B5"), -0.5, O.mult, 3.0, O.add)
-    ts(A("Yu"), A("B5"), -3.0, O.is_ge)
-    tt(A("Yt"), A("Yt"), A("Yu"), O.mult)
-    dma("y", (T.yc[:, :], []), A("Yt"))
+        s = o["sem"]
+        r = o["f"](o["grp"] is not None and place[i] == max(place[j] for j in o["grp"] if ops[j]["rows"][0] < o["rows"][1] and o["rows"][0] < ops[j]["rows"][1]))
+        if o["inc"] > 0:
+            r.then_inc(T.sem[s], o["inc"])
+        count[s] = count.get(s, 0) + abs(o["inc"])
+        done[i] = (s, count[s], dict(known[q]))
     for s in count:
         if known["g"].get(s, 0) < count[s]:
             g.wait_ge(T.sem[s], count[s])

@@ -7,18 +7,22 @@ QG = 192
 BIG = 16777216.0
 M16 = 1.5 * 2.0 ** 27
 M512 = 1.5 * 2.0 ** 32
-PATH = [2, 3, 2, 3, 1, 3, 2, 1, 3, 1, 2, 3, 1, 3, 1, 1]
+PATH = [1, 3, 1, 3, 1, 3, 1, 3, 1, 3, 2, 1, 3, 1, 3, 1]
+HALVED = [14, 15]
+LCUT = [(0, 4), (4, 16)]
+VSTEP = [4, 5, 6, 7]
+URGE = {"U": 0.0, "X": 0.0, "g": 1000.0, "c": 0.0, "l": 0.0}
 KB = [(0, 8), (8, 12), (12, 16)]
 SSEL = [c for c in range(32) if c % 2]
 
 _f = "x0c:512b oks:512 Ut:512 RV1:512b SG:2560b Yt:512 Z4:512 Rb:512b G0:512b idf:128 idb:128b nidb:128b BM:128b nBMh:128b BMgf:8 BMg4:32 tri:128b oneb:512b onef:128"
 _f += " O16:16b O16n:16b O16d:16b i65:66b n65:66b ia64:64b mW:128 t32:32 id2:64 z16:128b rsA:512b rsB:256b rs64:256b ph:1i tE:32 Pat:1024b KM:32 KMm:32 thr:1 thS:32 c16f:128"
 _f += " Bp:128b Rp:128b B16:32b nB16:32 TriB:128b TBc:128b cm:130 Pm:128b Jm:128b IO:512b sel15:128b neg1:1b pi:1i pj:1i rcol:1 r32:1 r0m:1 r1m:1 b512:1 iW:96 j255:512"
-_f += " rself:128 rselb:128b n1k:64b kA:16i kB:16i iM:16 slS:32i slL:32i tA:128b tB:128b tC:128b X:8208b Urep:8256 A0:8192b Ab:8192b xq:1024b o32:128b zb:128b wti:4i kmi:16i thi:1i wf:4 nwf:4 kf:16"
+_f += " rself:128 rselb:128b n1k:64b kA:16i kB:16i iM:16 slS:32i slL:32i tA:128b tB:128b tC:128b X:8208b Urep:8256 A0:8192b Ab:8192b xq:1536b o32:128b zb:128b half:1b j256:256b nb2:8 nb3:8 wti:4i kmi:16i thi:1i wf:4 nwf:4 kf:16"
 _f += " Lw:2048b Wn:8b Wp:32b Wff:8 BMw:128b c255:128b ui:64i U:64i sq:64i Fi:64i UF:64 FF:64 UU:64 T:512i Tf:256 OT:512u KS:1024 KAB:64 Ki:64i kp:64i pr:64 tf:32 tc:32i"
 _f += " cI:32i DI:32i f1:32 lim:32 fit:32b rsel:32 ST:2112b VZ:1040b Pc:64 Pd:64b Cc:128b Ck:128b Cq:128b Cs:128b wv:10 tmA:128 tmB:128 tsA:64 tsB:64 EQ:256 SC:256 win:4b"
-_f += " Mk:512b Jc:8b cvec:4 pos:4u mC:4 t0:4 t1:4 h16:4 SW:1600b swA:64 swB:64 INV:4u OFU:4u OF2:4u OFX:8u OFP:4u OFC:4u UG:128 u1A:64 u1B:64 u2A:64 u2B:64 XG:256b XP:64b"
-_f += " mP:64b mT:128b ts_:8 hs:8 nb:8 HH:1024b sgn:4096b LL:512b EE:128b SS:128b S1:96b dT:128b MI:32u tot:1 dg:128 cmx:130 cry:1 Gn:512b bA:1 bB:1 b2:1"
+_f += " Mk:512b Jc:8b cvec:4 pos:4u mC:4 t0:4 t1:4 h16:4 OFU:4u OF2:4u OFX:8u OFP:4u OFC:4u UG:128 u1A:64 u1B:64 u2A:64 u2B:64 XG:256b XP:64b"
+_f += " mP:1600b mT:1664b ts_:8 hs:8 nb:8 HH:1024b sgn:4096b LL:512b EE:128b SS:128b S1:96b dT:128b MI:32u tot:1 dg:128 cmx:130 cry:1 Gn:512b bA:1 bB:1 b2:1"
 _dt = {"b": "bfloat16", "i": "int32", "u": "uint16"}
 _pool, _where, SCRATCH = {}, {}, {}
 for _x in _f.split():
@@ -34,8 +38,8 @@ for _x in _f.split():
         _where[_n] = (_n, 0, _c)
         SCRATCH[_n] = ("sbuf", [128, _c], _d)
 for _t in range(RO):
-    SCRATCH["Q%d" % _t] = ("sbuf", [128, QW], "bfloat16")
-    _where["Q%d" % _t] = ("Q%d" % _t, 0, QW)
+    SCRATCH["Q%d" % _t] = ("sbuf", [128, QW + 1536], "bfloat16")
+    _where["Q%d" % _t] = ("Q%d" % _t, 0, QW + 1536)
     SCRATCH["C%d" % _t] = ("sbuf", [128, 8], "float32")
     _where["C%d" % _t] = ("C%d" % _t, 0, 8)
 for _t in range(8):
@@ -46,7 +50,8 @@ SEMAPHORES = ["sv", "ss", "st", "sg"] + ["d%d" % _t for _t in range(NDMA)]
 for _t in range(RO):
     SEMAPHORES += ["aP%d" % _t, "aT%d" % _t, "lP%d" % _t, "lT%d" % _t, "cP%d" % _t, "cT%d" % _t, "lC%d" % _t]
 
-CY, PE_CY, GA, SCA, HOP, DMA_T, REM_T = 1.04e-3, 0.75e-3, 1.56, 3.8, 0.1, 1.6, 2.2
+CY, PE_CY, GA, SCA, HOP, DMA_T, REM_T = 0.96e-3, 0.5e-3, 1.56, 3.8, 0.13, 1.6, 2.0
+PASSES = 8
 _order = {}
 
 
@@ -63,33 +68,53 @@ def _lay_out(ops):
     level = [0.0] * n
     for i in range(n - 1, -1, -1):
         o = ops[i]
-        level[i] = o["busy"] + o["lat"] + max([gap(i, s) + level[s] - (o["lat"] if i in ops[s]["ord"] else 0.0) for s in succ[i]] + [0.0])
+        level[i] = o["busy"] + o["lat"] + o.get("urge", 0.0) + max([gap(i, s) + level[s] - (o["lat"] if i in ops[s]["ord"] else 0.0) for s in succ[i]] + [0.0])
     first = [0.0] * n
     for i in range(n - 1, -1, -1):
         first[i] = max([ops[i]["first"]] + [first[s] for s in succ[i]])
     level = [a + b for a, b in zip(level, first)]
-    start, end = [0.0] * n, [0.0] * n
-    lanes = {}
-    for i in sorted(range(n), key=lambda i: (-level[i], i)):
-        o = ops[i]
-        t = max([(start[d] + ops[d]["busy"] if d in o["ord"] else end[d] + gap(d, i)) for d in o["dep"]] + [0.0])
-        lane = lanes.setdefault(o["q"], [])
-        if o["busy"] > 0:
-            k = 0
-            lo, hi = 0, len(lane)
-            while lo < hi:
-                mid = (lo + hi) // 2
-                if lane[mid][1] <= t:
-                    lo = mid + 1
-                else:
-                    hi = mid
-            k = lo
-            while k < len(lane) and lane[k][0] < t + o["busy"] - 1e-9:
-                t = max(t, lane[k][1])
-                k += 1
-            lane.insert(k, (t, t + o["busy"]))
-        start[i], end[i] = t, t + o["busy"] + o["lat"]
-    return sorted(range(n), key=lambda i: (start[i], -level[i], i))
+    pre = [[(d, 0.0 if d in o["ord"] else ops[d]["lat"] + gap(d, i)) for d in o["dep"]] for i, o in enumerate(ops)]
+    post = [[] for _ in range(n)]
+    for i in range(n):
+        for (d, w) in pre[i]:
+            post[d].append((i, w))
+
+    def lay(order, edges, least):
+        start, lanes = [0.0] * n, {}
+        for i in order:
+            b = ops[i]["busy"]
+            t = max([start[d] + ops[d]["busy"] + w for (d, w) in edges[i]] + [least[i]])
+            if b > 0:
+                lane = lanes.setdefault(ops[i]["q"], [])
+                lo, hi = 0, len(lane)
+                while lo < hi:
+                    mid = (lo + hi) // 2
+                    if lane[mid][1] <= t:
+                        lo = mid + 1
+                    else:
+                        hi = mid
+                while lo < len(lane) and lane[lo][0] < t + b - 1e-9:
+                    t = max(t, lane[lo][1])
+                    lo += 1
+                lane.insert(lo, (t, t + b))
+            start[i] = t
+        return start
+
+    zero, tail = [0.0] * n, [o["lat"] for o in ops]
+    order = sorted(range(n), key=lambda i: (-level[i], i))
+    best = None
+    for _ in range(PASSES):
+        start = lay(order, pre, zero)
+        rank_ = {i: k for k, i in enumerate(order)}
+        span = max(start[i] + ops[i]["busy"] + tail[i] for i in range(n))
+        if best is None or span < best[0]:
+            best = (span, sorted(range(n), key=lambda i: (start[i], rank_[i])))
+        back = sorted(range(n), key=lambda i: (-(start[i] + ops[i]["busy"]), -rank_[i]))
+        late = lay(back, post, tail)
+        rank_ = {i: k for k, i in enumerate(back)}
+        order = sorted(range(n), key=lambda i: (-(late[i] + ops[i]["busy"]), -rank_[i]))
+    _order["span"] = best[0]
+    return best[1]
 
 
 def rank_program(g, core, T, topo):
@@ -125,7 +150,7 @@ def rank_program(g, core, T, topo):
     def add(q, outs, ins, f, busy, lat=0.0, start=None, sem=None, inc=1, after=()):
         i = len(ops)
         dep = set(after)
-        o = {"q": q, "f": f, "busy": busy, "lat": lat, "dep": dep, "ord": set(after), "sem": sem or own.get(q), "inc": inc, "grp": None, "first": early[0]}
+        o = {"q": q, "f": f, "busy": busy, "lat": lat, "dep": dep, "ord": set(after), "sem": sem or own.get(q), "inc": inc, "grp": None, "first": early[0] + (URGE["g"] if q == "g" and start == "c" else 0.0)}
         ops.append(o)
         for regs, isw in ((rg(ins), False), (rg(outs), True)):
             for r in regs:
@@ -203,10 +228,10 @@ def rank_program(g, core, T, topo):
 
     def iota(o, pat, base, ch, small=True):
         kw = {"allow_small_or_imprecise_dtypes": True} if small else {}
-        add("g", [o], [], lambda s: g.iota(ap(o), pat, base, ch, **kw), 0.13 + 2 * o[2] * CY)
+        add("g", [o], [], lambda s: g.iota(ap(o), pat, base, ch, **kw), 0.13 + 2 * o[2] * CY, start="c" if o[2] < 1000 else None)
 
     def sel(o, i, pat, op, base, ch):
-        add("g", [o], [i], lambda s: g.affine_select(ap(o), ap(i), pat, op, 0.0, base, ch), 0.17 + 2 * o[2] * CY)
+        add("g", [o], [i], lambda s: g.affine_select(ap(o), ap(i), pat, op, 0.0, base, ch), 0.17 + 2 * o[2] * CY, start="c")
 
     nd = [0]
 
@@ -241,8 +266,8 @@ def rank_program(g, core, T, topo):
     d.append(dma(A("wti"), hbm(T.wt[:, :]), after=d[-1:]))
     d.append(dma(A("kmi"), hbm(T.km[:, :]), after=d[-1:]))
     d.append(dma(A("x0c"), hbm(T.xs[0:128:16, :]), after=d[-1:]))
-    d.append(dma(A("thi"), hbm(T.th[:, :]), after=d[-1:]))
-    dma(A("X", 0, 8192), hbm(T.xs[:, :]), 7.0, after=d[-1:])
+    d.append(dma(A("X", 0, 8192), hbm(T.xs[:, :]), 7.0, after=d[-1:]))
+    dma(A("thi"), hbm(T.th[:, :]), 7.0, after=d[-1:])
     o128 = A("oneb", 0, 128)
 
     def consts():
@@ -303,6 +328,8 @@ def rank_program(g, core, T, topo):
         cp(A("IO", 0, 512, 1, 32, 64), A("RV1", 0, 512, 1, 32, 64))
         ms(A("o32"), 1.0 / 32)
         ms(A("zb"), 0.0)
+        ms(A("half"), 0.5)
+        iota(A("j256"), [[1, 256]], 0, 0)
         sel(A("cm", 0, 128), A("onef"), [[-1, 128]], O.is_gt, 0, 1)
         tt(A("cm", 0, 128), A("cm", 0, 128), A("BM"), O.mult)
         ms(A("cm", 128, 130), 1.0)
@@ -313,7 +340,6 @@ def rank_program(g, core, T, topo):
         tt(A("TriB"), A("tA"), A("idb"), O.add)
         iota(A("i65"), [[1, 66]], 1, 0)
         act(A("n65"), A("i65"), F.Identity, 0.5, -1.0)
-        iota(A("ia64"), [[1, 64]], 0, 0)
         iota(A("slS"), [[128, 4], [0, 8]], 0, 1, False)
         ms(A("bA"), 191.5)
         ms(A("bB"), -256.0)
@@ -377,7 +403,10 @@ def rank_program(g, core, T, topo):
         ms(A("cvec", 0, 1), 1.0)
         ms(A("cvec", 1, 2), -1.0)
         ms(A("cvec", 2, 3), 2.0)
-        ms(A("SW", 0, 64), 0.0)
+        ms(A("mP", 0, 64), 0.0)
+        ms(A("mT", 0, 128), 0.0)
+        for t in range(RO):
+            ms(A("Q%d" % t, QG + 512, QW), 0.0)
         cp(A("thr"), A("thi"))
         ts(A("tE"), A("BMg4"), A("thr"), O.mult)
         mm(A("B6", 0, 32), A("c16f"), A("tE"))
@@ -412,7 +441,7 @@ def rank_program(g, core, T, topo):
                 act(A("Tf", b // 2, 256, 16), A("kf"), F.Identity, f, u)
             else:
                 ts(A("T", b, 512, 32), A("kf"), u, O.mult, f, O.add)
-        for (a, b) in ((0, 4), (4, 16)):
+        for (a, b) in LCUT:
             cp(A("T", 32 * a + 1, 32 * b, 2), A("Tf", 16 * a, 16 * b))
             ts(A("T", 32 * a, 32 * b), A("T", 32 * a, 32 * b), 8191, O.bitwise_and)
             cp(A("OT", 32 * a, 32 * b), A("T", 32 * a, 32 * b))
@@ -426,13 +455,13 @@ def rank_program(g, core, T, topo):
         for m in range(16):
             k = [i for i, (a, b) in enumerate(KB) if a <= m < b][0]
             a, b = KB[k]
-            cuts = ((0, 256), (256, 512)) if m >= 14 else ((0, 512),)
+            cuts = ((0, 256), (256, 512)) if m in HALVED else ((0, 512),)
             for (lo, hi) in cuts:
                 o = 512 * m
                 src, h = IX(A("X"), A("OT", 32 * m + lo // 16, 32 * m + hi // 16)), A(Q, QG + lo, QG + hi)
                 a0, ab = A("A0", o + lo, o + hi), A("Ab", o + lo, o + hi)
                 if PATH[m] == 3:
-                    bank, x = A("B%d" % (3 + n3 % 2), 0, hi - lo), A("xq", 512 * (n3 % 2), 512 * (n3 % 2) + hi - lo)
+                    bank, x = A("B%d" % (3 + n3 % 3), 0, hi - lo), A("xq", 512 * (n3 % 3), 512 * (n3 % 3) + hi - lo)
                     n3 += 1
                     act(x, src, F.Copy)
                     mm(bank, A("nidb"), h, True)
@@ -473,7 +502,7 @@ def rank_program(g, core, T, topo):
         tt(A("cmx", 0, 129), A("B6", 0, 129), A("cm", 0, 129), O.mult)
         add("v", [A("cry")], [A("cmx", 0, 129)], lambda s: V.tensor_reduce(A("cry")[0], A("cmx", 0, 129)[0], AxisListType.X, O.max), 129 * CY)
         ts(A("Ut"), A("oks"), A("b512"), O.add, A("cry"), O.max)
-        dma(A("Urep", 0, 8192, 1, 0, 128, 16), A("Ut"), 0.6)
+        ops[dma(A("Urep", 0, 8192, 1, 0, 128, 16), A("Ut"), 0.6)]["urge"] = URGE["U"]
 
     def choose():
         ts(A("kp"), A("Ki"), 63, O.bitwise_and)
@@ -507,8 +536,8 @@ def rank_program(g, core, T, topo):
         mm(A("B0", 0, 64), A("Cc"), A("Pd"), True)
         mm(A("B0", 64, 128), A("Ck"), A("Pd"), False)
         for k in range(4):
-            mm(A("B0", 128 + 64 * k, 192 + 64 * k), A("Cq"), A("Pd"), False)
-        mm(A("B0", 384, 448), A("Cs"), A("Pd"), False)
+            mm(A("B3", 128 + 64 * k, 192 + 64 * k), A("Cq"), A("Pd"), k == 0)
+        mm(A("B3", 384, 448), A("Cs"), A("Pd"), False)
 
     def wrap(a, b, src):
         n = src[2]
@@ -519,10 +548,17 @@ def rank_program(g, core, T, topo):
     def marks(k, c):
         ts(A("hs", k, k + 4), A("ts_", k, k + 4), M512, O.add, M512, O.subtract)
         tt(A("nb", k, k + 4), A("hs", k, k + 4), A("ts_", k, k + 4), O.subtract)
+        if VSTEP[-1] >= k and VSTEP[0] < k + 4:
+            ts(A("nb2", k, k + 4), A("nb", k, k + 4), -1.0, O.mult, 255.0, O.add)
+            ts(A("nb3", k, k + 4), A("nb", k, k + 4), -1.0, O.mult, -1.0, O.add)
         for i in range(k, k + 4):
             hh = A("HH", 128 * i, 128 * i + 128)
-            act(A("sgn", 512 * i, 512 * i + 512), A("j255"), F.Sign, A("nb", i, i + 1))
-            ts(hh, A("Bp"), A("hs", i, i + 1), O.is_equal, c, O.mult)
+            if i in VSTEP:
+                for h, n in enumerate(("nb2", "nb3")):
+                    ts(A("sgn", 512 * i + 256 * h, 512 * i + 256 * h + 256), A("j256"), A(n, i, i + 1), O.is_gt, 0.5, O.subtract)
+            else:
+                act(A("sgn", 512 * i, 512 * i + 512), A("j255"), F.Sign, A("nb", i, i + 1))
+            ts(hh, A("Bp"), A("hs", i, i + 1), O.is_equal, 2 * c if i in VSTEP else c, O.mult)
             mm(A("B5"), hh, A("sgn", 512 * i, 512 * i + 512), i == 0)
 
     def give(t):
@@ -531,21 +567,22 @@ def rank_program(g, core, T, topo):
         cW = A("tmB", 15, 64, 16)
         for k in range(4):
             ts(A("EQ", 64 * k, 64 * k + 64), A("B0", 0, 64), A("tmB", 15 + 16 * k, 16 + 16 * k), O.is_equal)
-        tt(A("EQ"), A("EQ"), A("B0", 128, 384), O.mult)
-        sW = wrap("tsA", "tsB", A("B0", 384, 448))
+        tt(A("EQ"), A("EQ"), A("B3", 128, 384), O.mult)
+        sW = wrap("tsA", "tsB", A("B3", 384, 448))
         scan(A("SC"), A("rs64"), A("EQ"), 0.0, O.max, O.min)
         tt(A("win"), A("SC", 63, 256, 64), A("tmB", 79, 128, 16), O.is_gt)
-        mm(A("B1", 0, 5), A("idb"), A("Jc", 0, 5), True)
+        mm(A("B1", 0, 4), A("idb"), A("Jc", 0, 4), True)
         mm(A("B1", 0, 4), A("tB"), A("win"), False)
+        mm(A("B4", 0, 1), A("idb"), A("Jc", 4, 5), True)
         for k in range(4):
             mm(A("B1", k, k + 1), A("Mk", 128 * k, 128 * k + 128), A("win", k, k + 1), False)
-            mm(A("B1", k + 1, 5), A("BM"), A("win", 0, 4 - k), False)
-        ts(A("mC"), A("cvec"), A("B1", 4, 5), O.mult)
+            if k:
+                mm(A("B1", k, 4), A("BM"), A("win", 0, 4 - k), False)
+            mm(A("B4", 0, 1), A("BM"), A("win", k, k + 1), False)
+        ts(A("mC"), A("cvec"), A("B4", 0, 1), O.mult)
         remote("lC%d" % t, [(rank ^ 1, eP, A("mC"), A(C, 0, 4), "cP%d" % t), (rank ^ 4, eT, A("mC"), A(C, 4, 8), "cT%d" % t)])
         cp(A("pos"), A("B1", 0, 4))
         tt(A("t0"), sW, A("B1", 0, 4), O.subtract)
-        sct(A("SW"), A("pos"), A("ia64"))
-        cp(A("INV"), wrap("swA", "swB", A("SW", 0, 64)))
         ts(A("OFU"), cW, -1.0, O.mult, 8239.0, O.add)
         act(A("UG", 0, 64), IX(A("Urep"), A("OFU")), F.Copy)
         mm(A("B6", 0, 64), A("rself"), A("UG", 0, 64))
@@ -565,23 +602,24 @@ def rank_program(g, core, T, topo):
         tt(A("XP"), A("XG", 0, 64), A("B2", 0, 64), O.max)
         ts(A("OFC"), sW, -184.0, O.add, 0.0, O.max)
         act(A("XG", 192, 256), IX(A(Q, QG, QG + 512), A("OFC")), F.Copy)
-        ts(A("mP"), IX(A("XP"), A("INV")), 255.0, O.min)
-        remote("lP%d" % t, [(rank ^ 1, eP, A("mP"), A(Q, 0, 64), "aP%d" % t)])
-        act(A("mT", 0, 64), IX(A("XG", 64, 128), A("INV")), F.Copy)
-        cp(A("mT", 64, 128), IX(A("XG", 128, 192), A("INV")))
-        remote("lT%d" % t, [(rank ^ 4, eT, A("mT"), A(Q, 64, 192), "aT%d" % t)])
-        act(A(Q, QG + 512, QW), IX(A("XG", 192, 256), A("INV")), F.Copy)
+        ts(A("XP"), A("XP"), 255.0, O.min)
+        sct(A("mT", 0, 1600), A("pos"), A("XG", 64, 128))
+        sct(A("mT", 64, 1664), A("pos"), A("XG", 128, 192))
+        remote("lT%d" % t, [(rank ^ 4, eT, A("mT", 0, 128), A(Q, 64, 192), "aT%d" % t)])
+        sct(A("mP"), A("pos"), A("XP"))
+        remote("lP%d" % t, [(rank ^ 1, eP, A("mP", 0, 64), A(Q, 0, 64), "aP%d" % t)])
+        sct(A(Q, QG + 512, QG + 512 + 1600), A("pos"), A("XG", 192, 256))
         ts(A("ts_", 0, 4), cW, -319.5, O.add)
         marks(0, 4096.0)
         ts(A("ts_", 4, 8), r2, -1.0, O.mult, 7937.5, O.add)
         marks(4, -4096.0)
         for i in range(8):
-            mm(A("B2", 64, 65), A("HH", 128 * i, 128 * i + 128), A("oneb", 0, 1), i == 0)
+            mm(A("B2", 64, 65), A("HH", 128 * i, 128 * i + 128), A("half") if i in VSTEP else A("oneb", 0, 1), i == 0)
         ts(A("TBc"), A("TriB"), A("B2", 64, 65), O.mult)
         mm(A("B5"), A("TBc"), A("oneb"), False)
         if t < RO - 1:
             tt(A("x0c"), A("x0c"), A("B5"), O.max)
-            dma(A("X", 0, 8192, 1, 0, 128, 16), A("x0c"))
+            ops[dma(A("X", 0, 8192, 1, 0, 128, 16), A("x0c"))]["urge"] = URGE["X"]
             act(A("SG", t * 512, t * 512 + 512), A("x0c"), F.Sign, A("bB"))
         else:
             mm(A("B5"), A("idb"), A("Rb"), False)
@@ -610,7 +648,7 @@ def rank_program(g, core, T, topo):
             ts(A("EE", 32 * k, 32 * k + 32), A("B16"), h, O.is_equal)
             mm(out, A("LL", 128 * k, 128 * k + 128), A("EE", 32 * k, 32 * k + 32), False)
         ts(A("MI"), out, A("r32"), O.add, A("mC", 0, 1), O.add)
-        a, b = IX(A(Q), A("MI", 0, 16)), IX(A(Q), A("MI", 16, 32))
+        a, b = IX(A(Q, 0, QW), A("MI", 0, 16)), IX(A(Q, 0, QW), A("MI", 16, 32))
         if t < RO - 1:
             cp(A("Q%d" % (t + 1), QG, QG + 256), a)
             act(A("Q%d" % (t + 1), QG + 256, QG + 512), b, F.Copy)
@@ -619,10 +657,10 @@ def rank_program(g, core, T, topo):
             act(A("Gn", 256, 512), b, F.Identity, 255.0, -1.0)
             dma(hbm(T.yg[:, :]), A("Gn"))
 
-    early[0] = 1000.0
+    early[0] = URGE["c"]
     consts()
     for t in range(RO):
-        early[0] = 0.0 if t else 2000.0
+        early[0] = 0.0 if t else URGE["l"]
         weights(t)
         lists(t)
         early[0] = 0.0

@@ -7,29 +7,29 @@ QG = 192
 BIG = 16777216.0
 M16 = 1.5 * 2.0 ** 27
 M512 = 1.5 * 2.0 ** 32
-PATH = [1, 3, 1, 3, 1, 3, 1, 3, 1, 3, 2, 1, 3, 1, 3, 1]
+PATH = [3, 3, 1, 3, 1, 3, 1, 3, 1, 3, 1, 3, 1, 1, 3, 1]
 HALVED = [14, 15]
-LCUT = [(0, 4), (4, 16)]
-VSTEP = [4, 5, 6, 7]
-URGE = {"U": 0.0, "X": 0.0, "g": 1000.0, "c": 0.0, "l": 0.0}
+LCUT = [(0, 1), (1, 3), (3, 16)]
+VMUL = [0]
+VSTEP = [6, 7]
 KB = [(0, 8), (8, 12), (12, 16)]
 SSEL = [c for c in range(32) if c % 2]
 
-_f = "x0c:512b oks:512 Ut:512 RV1:512b SG:2560b Yt:512 Z4:512 Rb:512b G0:512b idf:128 idb:128b nidb:128b BM:128b nBMh:128b BMgf:8 BMg4:32 tri:128b oneb:512b onef:128"
-_f += " O16:16b O16n:16b O16d:16b i65:66b n65:66b ia64:64b mW:128 t32:32 id2:64 z16:128b rsA:512b rsB:256b rs64:256b ph:1i tE:32 Pat:1024b KM:32 KMm:32 thr:1 thS:32 c16f:128"
-_f += " Bp:128b Rp:128b B16:32b nB16:32 TriB:128b TBc:128b cm:130 Pm:128b Jm:128b IO:512b sel15:128b neg1:1b pi:1i pj:1i rcol:1 r32:1 r0m:1 r1m:1 b512:1 iW:96 j255:512"
-_f += " rself:128 rselb:128b n1k:64b kA:16i kB:16i iM:16 slS:32i slL:32i tA:128b tB:128b tC:128b X:8208b Urep:8256 A0:8192b Ab:8192b xq:1536b o32:128b zb:128b half:1b j256:256b nb2:8 nb3:8 wti:4i kmi:16i thi:1i wf:4 nwf:4 kf:16"
-_f += " Lw:2048b Wn:8b Wp:32b Wff:8 BMw:128b c255:128b ui:64i U:64i sq:64i Fi:64i UF:64 FF:64 UU:64 T:512i Tf:256 OT:512u KS:1024 KAB:64 Ki:64i kp:64i pr:64 tf:32 tc:32i"
-_f += " cI:32i DI:32i f1:32 lim:32 fit:32b rsel:32 ST:2112b VZ:1040b Pc:64 Pd:64b Cc:128b Ck:128b Cq:128b Cs:128b wv:10 tmA:128 tmB:128 tsA:64 tsB:64 EQ:256 SC:256 win:4b"
-_f += " Mk:512b Jc:8b cvec:4 pos:4u mC:4 t0:4 t1:4 h16:4 OFU:4u OF2:4u OFX:8u OFP:4u OFC:4u UG:128 u1A:64 u1B:64 u2A:64 u2B:64 XG:256b XP:64b"
-_f += " mP:1600b mT:1664b ts_:8 hs:8 nb:8 HH:1024b sgn:4096b LL:512b EE:128b SS:128b S1:96b dT:128b MI:32u tot:1 dg:128 cmx:130 cry:1 Gn:512b bA:1 bB:1 b2:1"
+_f = "x0c:512b oks:512 Ut:512 RV1:512b SG:2560b Yt:512 Z4:512 Rb:512b G0:512b idf:128 idb:128b nidb:128b BM:128b BMf:128 nBMh:128b BMgf:8 BMg4:32 tri:128b oneb:512b onef:128"
+_f += " O16:16b O16n:16b O16d:16b i65:66b n65:66b mW:128 t32:32 id2:64 z16:128b rsA:512b rsB:256b rs64:256b ph:1i tE:32 Pat:1024b KM:32 KMm:32 thr:1 thS:32 c16f:128"
+_f += " Bp:128b Rp:128b B16:32b nB16:32 TriB:128b TBc:128b cm:18 Pm:128b Jm:128b IO:512b sel15:128b neg1:1b pi:1i pj:1i rcol:1 r32:1 r0m:1 r1m:1 b512:1 iW:96 j255:512"
+_f += " rself:128 rselb:128b n1k:64b kA:16i kB:16i iM:16 slS:32i slL:32i tA:128b tB:128b tC:128b X:8208b Urep:8256 A0:8192b Ab:8192b xq:1536b o32:128b zb:128b half:1b j256:256b"
+_f += " nb2:8 nb3:8 wti:4i kmi:16i thi:1i wf:4 nwf:4 kf:16 Lw:2048b Wn:8b Wp:32b Wff:8 BMw:128b c255:128b ui:64i U:64i sq:64i Fi:64i UF:64 UU:64 T:512i Tf:512 OT:512u KS:1024"
+_f += " KAB:64 Ki:64i kp:64i pr:64 tf:32 tc:32i cI:32i DI:32i f1:32 lim:32 fit:32b rsel:32 ST:2112b VZ:1040b Pc:64 Pd:64b Cc:128b Ck:128b Cq:128b Cs:128b wv:11 tmA:128 tmB:128"
+_f += " tsA:64 tsB:64 EQ:256 SC:256 win:4b Mk:512b Jc:8b Jf:8 cvec:4 pos:4u mC:4 t0:4 t1:4 h16:4 OFU:4u OF2:4u OFX:8u OFP:4u OFC:4u UG:128 u1A:64 u1B:64 u2A:64 u2B:64 XG:256b XP:64b"
+_f += " mP:1600b mT:1664b ts_:8 hs:8 nb:8 HH:1024b sgn:4096b LL:512b EE:128b SS:128b S1:96b dT:128b MI:32u tot:1 dg:16 cmx:18 cry:1 Gn:512b bA:1 bB:1 b2:1"
 _dt = {"b": "bfloat16", "i": "int32", "u": "uint16"}
 _pool, _where, SCRATCH = {}, {}, {}
 for _x in _f.split():
     _n, _c = _x.split(":")
     _d = _dt.get(_c[-1], "float32")
     _c = int(_c if _d == "float32" else _c[:-1])
-    if _c <= 264 and _n not in ("mP", "mT", "mC", "XG", "XP"):
+    if _c <= 264 and _n not in ("mC", "XG", "XP"):
         _p = "pool_" + _d
         _where[_n] = (_p, _pool.get(_p, 0), _c)
         _pool[_p] = _pool.get(_p, 0) + (_c + 15) // 16 * 16
@@ -50,8 +50,8 @@ SEMAPHORES = ["sv", "ss", "st", "sg"] + ["d%d" % _t for _t in range(NDMA)]
 for _t in range(RO):
     SEMAPHORES += ["aP%d" % _t, "aT%d" % _t, "lP%d" % _t, "lT%d" % _t, "cP%d" % _t, "cT%d" % _t, "lC%d" % _t]
 
-CY, PE_CY, GA, SCA, HOP, DMA_T, REM_T = 0.96e-3, 0.5e-3, 1.56, 3.8, 0.13, 1.6, 2.0
-PASSES = 8
+CY, PE_CY, GA, SCA, HOP, DMA_T, REM_T, X_T = 0.88e-3, 0.45e-3, 1.56, 3.8, 0.2, 1.6, 2.0, 6.0
+PASSES, SEED, SHAKE, CASES = 210, 1, 6.0, ((1.0, 0.22), (1.15, 0.15), (1.3, 0.2))
 _order = {}
 
 
@@ -65,19 +65,15 @@ def _lay_out(ops):
     def gap(a, b):
         return 0.0 if (ops[a]["q"] == "t" and ops[b]["q"] == "t") or a in ops[b]["ord"] else HOP
 
-    level = [0.0] * n
-    for i in range(n - 1, -1, -1):
-        o = ops[i]
-        level[i] = o["busy"] + o["lat"] + o.get("urge", 0.0) + max([gap(i, s) + level[s] - (o["lat"] if i in ops[s]["ord"] else 0.0) for s in succ[i]] + [0.0])
-    first = [0.0] * n
-    for i in range(n - 1, -1, -1):
-        first[i] = max([ops[i]["first"]] + [first[s] for s in succ[i]])
-    level = [a + b for a, b in zip(level, first)]
     pre = [[(d, 0.0 if d in o["ord"] else ops[d]["lat"] + gap(d, i)) for d in o["dep"]] for i, o in enumerate(ops)]
     post = [[] for _ in range(n)]
     for i in range(n):
         for (d, w) in pre[i]:
             post[d].append((i, w))
+    level, first = [0.0] * n, [0.0] * n
+    for i in range(n - 1, -1, -1):
+        level[i] = ops[i]["busy"] + max([w + level[s] for (s, w) in post[i]] + [ops[i]["lat"]])
+        first[i] = max([ops[i]["first"]] + [first[s] for s in succ[i]])
 
     def lay(order, edges, least):
         start, lanes = [0.0] * n, {}
@@ -100,19 +96,49 @@ def _lay_out(ops):
             start[i] = t
         return start
 
+    def play(order, slow, hop):
+        free, done = {}, [0.0] * n
+        for i in order:
+            o = ops[i]
+            t = free.get(o["q"], 0.0) if o["busy"] > 0 else 0.0
+            for (d, w) in pre[i]:
+                w = done[d] + (w if w == 0.0 else w - HOP + hop)
+                if w > t:
+                    t = w
+            done[i] = t + o["busy"] * slow
+            if o["busy"] > 0:
+                free[o["q"]] = done[i]
+        return max(done[i] + tail[i] for i in range(n))
+
     zero, tail = [0.0] * n, [o["lat"] for o in ops]
-    order = sorted(range(n), key=lambda i: (-level[i], i))
-    best = None
-    for _ in range(PASSES):
+    order = sorted(range(n), key=lambda i: (-level[i] - first[i], i))
+    best, seed = None, [SEED]
+
+    def draw():
+        seed[0] = (seed[0] * 1103515245 + 12345) % 2147483648
+        return seed[0] / 2147483648.0
+
+    for k in range(PASSES):
         start = lay(order, pre, zero)
-        rank_ = {i: k for k, i in enumerate(order)}
-        span = max(start[i] + ops[i]["busy"] + tail[i] for i in range(n))
+        at = {i: j for j, i in enumerate(order)}
+        issue = sorted(range(n), key=lambda i: (start[i], at[i]))
+        span = sum(play(issue, s, h) / s for (s, h) in CASES) / len(CASES)
         if best is None or span < best[0]:
-            best = (span, sorted(range(n), key=lambda i: (start[i], rank_[i])))
-        back = sorted(range(n), key=lambda i: (-(start[i] + ops[i]["busy"]), -rank_[i]))
+            best = (span, issue, start, order)
+        if k % 3 == 2:
+            start, order = best[2], best[3]
+            at = {i: j for j, i in enumerate(order)}
+        back = sorted(range(n), key=lambda i: (-(start[i] + ops[i]["busy"]), -at[i]))
         late = lay(back, post, tail)
-        rank_ = {i: k for k, i in enumerate(back)}
-        order = sorted(range(n), key=lambda i: (-(late[i] + ops[i]["busy"]), -rank_[i]))
+        key = [late[i] + ops[i]["busy"] for i in range(n)]
+        if k % 3 == 2:
+            a = draw() * max(key)
+            b, c = a + 1.0 + 6.0 * draw(), SHAKE * draw()
+            key = [x + c * draw() if a <= x < b else x for x in key]
+            for i in back:
+                key[i] = max([key[i]] + [key[s] + 1e-6 for s in succ[i]])
+        at = {i: j for j, i in enumerate(back)}
+        order = sorted(range(n), key=lambda i: (-key[i], -at[i]))
     _order["span"] = best[0]
     return best[1]
 
@@ -123,7 +149,7 @@ def rank_program(g, core, T, topo):
         return
     queues = {"v": g.vector, "s": g.scalar, "t": g.tensor, "g": g, "y": g.sync}
     own = {"v": "sv", "s": "ss", "t": "st", "g": "sg"}
-    ops, log, banks, early = [], {}, {}, [0.0]
+    ops, log, banks = [], {}, {}
 
     def A(n, lo=0, hi=None, st=1, p0=0, p1=128, pst=1):
         p, o, c = _where[n]
@@ -147,10 +173,10 @@ def rank_program(g, core, T, topo):
     def ap(x):
         return x[0] if isinstance(x, tuple) else x
 
-    def add(q, outs, ins, f, busy, lat=0.0, start=None, sem=None, inc=1, after=()):
+    def add(q, outs, ins, f, busy, lat=0.0, start=None, sem=None, inc=1, after=(), first=0.0):
         i = len(ops)
         dep = set(after)
-        o = {"q": q, "f": f, "busy": busy, "lat": lat, "dep": dep, "ord": set(after), "sem": sem or own.get(q), "inc": inc, "grp": None, "first": early[0] + (URGE["g"] if q == "g" and start == "c" else 0.0)}
+        o = {"q": q, "f": f, "busy": busy, "lat": lat, "dep": dep, "ord": set(after), "sem": sem or own.get(q), "inc": inc, "grp": None, "first": first}
         ops.append(o)
         for regs, isw in ((rg(ins), False), (rg(outs), True)):
             for r in regs:
@@ -228,10 +254,10 @@ def rank_program(g, core, T, topo):
 
     def iota(o, pat, base, ch, small=True):
         kw = {"allow_small_or_imprecise_dtypes": True} if small else {}
-        add("g", [o], [], lambda s: g.iota(ap(o), pat, base, ch, **kw), 0.13 + 2 * o[2] * CY, start="c" if o[2] < 1000 else None)
+        add("g", [o], [], lambda s: g.iota(ap(o), pat, base, ch, **kw), 0.13 + 2 * o[2] * CY, first=1000.0 if o[2] < 1000 else 0.0)
 
     def sel(o, i, pat, op, base, ch):
-        add("g", [o], [i], lambda s: g.affine_select(ap(o), ap(i), pat, op, 0.0, base, ch), 0.17 + 2 * o[2] * CY, start="c")
+        add("g", [o], [i], lambda s: g.affine_select(ap(o), ap(i), pat, op, 0.0, base, ch), 0.17 + 2 * o[2] * CY, first=1000.0)
 
     nd = [0]
 
@@ -266,8 +292,8 @@ def rank_program(g, core, T, topo):
     d.append(dma(A("wti"), hbm(T.wt[:, :]), after=d[-1:]))
     d.append(dma(A("kmi"), hbm(T.km[:, :]), after=d[-1:]))
     d.append(dma(A("x0c"), hbm(T.xs[0:128:16, :]), after=d[-1:]))
-    d.append(dma(A("X", 0, 8192), hbm(T.xs[:, :]), 7.0, after=d[-1:]))
-    dma(A("thi"), hbm(T.th[:, :]), 7.0, after=d[-1:])
+    d.append(dma(A("X", 0, 8192), hbm(T.xs[:, :]), X_T, after=d[-1:]))
+    dma(A("thi"), hbm(T.th[:, :]), X_T, after=d[-1:])
     o128 = A("oneb", 0, 128)
 
     def consts():
@@ -284,11 +310,11 @@ def rank_program(g, core, T, topo):
         cp(A("wf"), A("wti"))
         ts(A("nwf"), A("wti"), -1.0, O.mult)
         cp(A("BMgf"), A("BM", 0, 128, 16))
+        act(A("BMf"), A("BM"), F.Copy)
         for b in range(4):
             act(A("BMg4", 8 * b, 8 * b + 8), A("BM", 0, 128, 16), F.Copy)
         cp(A("kf"), A("kmi"))
-        ts(A("Q0", QG, QG + 256), A("G0", 0, 256), -1.0, O.mult, 255.0, O.add)
-        ts(A("Q0", QG + 256, QG + 512), A("G0", 256, 512), -1.0, O.mult, 255.0, O.add)
+        ts(A("Q0", QG, QG + 512), A("G0"), -1.0, O.mult, 255.0, O.add)
         ts(A("pj"), A("pi"), 15, O.bitwise_and)
         cp(A("rcol"), A("pj"))
         ts(A("b512"), A("pj"), 512.0, O.mult)
@@ -330,9 +356,6 @@ def rank_program(g, core, T, topo):
         ms(A("zb"), 0.0)
         ms(A("half"), 0.5)
         iota(A("j256"), [[1, 256]], 0, 0)
-        sel(A("cm", 0, 128), A("onef"), [[-1, 128]], O.is_gt, 0, 1)
-        tt(A("cm", 0, 128), A("cm", 0, 128), A("BM"), O.mult)
-        ms(A("cm", 128, 130), 1.0)
         sel(A("tri"), o128, [[1, 128]], O.is_ge, 0, -1)
         sel(A("tB"), o128, [[1, 128]], O.is_gt, 0, -1)
         tt(A("tB"), A("tB"), A("BM"), O.mult)
@@ -340,6 +363,8 @@ def rank_program(g, core, T, topo):
         tt(A("TriB"), A("tA"), A("idb"), O.add)
         iota(A("i65"), [[1, 66]], 1, 0)
         act(A("n65"), A("i65"), F.Identity, 0.5, -1.0)
+        ts(A("cm", 0, 16), A("i65", 0, 16), A("rcol"), O.is_le)
+        ms(A("cm", 16, 17), 1.0)
         iota(A("slS"), [[128, 4], [0, 8]], 0, 1, False)
         ms(A("bA"), 191.5)
         ms(A("bB"), -256.0)
@@ -359,8 +384,9 @@ def rank_program(g, core, T, topo):
         ms(A("rs64", 0, 256, 64), BIG)
         act(A("rself"), A("BM"), F.Copy, None, A("r0m"))
         act(A("rselb"), A("BM"), F.Copy, None, A("r0m"))
-        ts(A("tot"), A("pj"), 15.0, O.is_equal, -1.0, O.mult)
-        act(A("sel15"), A("BM"), F.Copy, None, A("tot"))
+        wv = [A("wv", k, k + 1) for k in range(11)]
+        ts(wv[10], A("pj"), 15.0, O.is_equal, -1.0, O.mult)
+        act(A("sel15"), A("BM"), F.Copy, None, wv[10])
         act(A("nBMh"), A("BM"), F.Copy, None, -0.5)
         act(A("tC"), A("BM"), F.Identity, -4096.0, 4096.0)
         iota(A("Bp"), [[0, 8], [512, 16]], 0, 0)
@@ -378,7 +404,6 @@ def rank_program(g, core, T, topo):
         tt(A("VZ", 20, 1040, 32), A("slS"), A("slL"), O.subtract)
         ms(A("VZ", 22, 1040, 32), 1.0)
         ms(A("VZ", 23, 1040, 32), 1.0)
-        wv = [A("wv", k, k + 1) for k in range(10)]
         ts(A("ph"), A("pj"), 1, O.logical_shift_right)
         ts(wv[0], A("ph"), 0.0, O.is_equal, 0.5, O.mult)
         ts(wv[1], A("ph"), 1.0, O.is_equal, 256.0, O.mult)
@@ -392,13 +417,12 @@ def rank_program(g, core, T, topo):
         ts(wv[9], wv[7], wv[1], O.add, wv[4], O.add)
         for n, k in (("Cc", 5), ("Cs", 6), ("Cq", 8), ("Ck", 9)):
             act(A(n), A("BM"), F.Copy, None, wv[k])
-        iota(A("t1"), [[128, 4]], 1024, 0)
-        ts(A("t0", 0, 1), A("rcol"), 8.0, O.mult)
-        ts(A("t1"), A("t1"), A("t0", 0, 1), O.add)
-        cp(A("Jc", 0, 4), A("t1"))
+        ts(A("Jf", 4, 8), A("B16", 0, 4), A("rcol"), O.add, 128.0, O.add)
+        ts(A("Jf", 0, 4), A("Jf", 4, 8), 8.0, O.mult)
+        cp(A("Jc", 0, 4), A("Jf", 0, 4))
         ms(A("Jc", 4, 5), -64.0)
         for k in range(4):
-            act(A("Mk", 128 * k, 128 * k + 128), A("nidb"), F.Copy, None, A("t1", k, k + 1))
+            act(A("Mk", 128 * k, 128 * k + 128), A("nidb"), F.Copy, None, A("Jf", k, k + 1))
         ms(A("cvec", 3, 4), 0.0)
         ms(A("cvec", 0, 1), 1.0)
         ms(A("cvec", 1, 2), -1.0)
@@ -409,8 +433,10 @@ def rank_program(g, core, T, topo):
             ms(A("Q%d" % t, QG + 512, QW), 0.0)
         cp(A("thr"), A("thi"))
         ts(A("tE"), A("BMg4"), A("thr"), O.mult)
-        mm(A("B6", 0, 32), A("c16f"), A("tE"))
-        cp(A("thS"), A("B6", 0, 32))
+        mm(A("B5", 0, 32), A("c16f"), A("tE"))
+        cp(A("thS"), A("B5", 0, 32))
+        for k in range(8):
+            iota(A("Urep", 1032 * k, 1032 * k + 1032), [[0, 1032]], 0, 0)
 
     def weights(t):
         w, nw = A("wf", t, t + 1), A("nwf", t, t + 1)
@@ -431,18 +457,19 @@ def rank_program(g, core, T, topo):
             mm(A("B4", 32 + 8 * b, 40 + 8 * b), A(Q, QG + 128 * b, QG + 128 * b + 128), A("Wn"), False)
         cp(A("ui"), A("B4", 0, 64))
         ts(A("U"), A("ui"), 4095, O.bitwise_and)
-        tt(A("sq"), A("U"), A("U"), O.mult)
+        tt(A("sq", 0, 32), A("U", 0, 32), A("U", 0, 32), O.mult)
+        ts(A("Fi", 0, 32), A("sq", 0, 32), 5, O.logical_shift_right)
         cp(A("UF"), A("U"))
-        ts(A("Fi"), A("sq"), 5, O.logical_shift_right)
-        cp(A("FF"), A("Fi"))
-        for b in range(32):
-            u, f = A("UF", b, b + 1), A("FF", b, b + 1)
-            if b % 2:
-                act(A("Tf", b // 2, 256, 16), A("kf"), F.Identity, f, u)
-            else:
-                ts(A("T", b, 512, 32), A("kf"), u, O.mult, f, O.add)
+        tt(A("sq", 32, 64), A("U", 32, 64), A("U", 32, 64), O.mult)
+        ts(A("Fi", 32, 64), A("sq", 32, 64), 5, O.logical_shift_right)
         for (a, b) in LCUT:
-            cp(A("T", 32 * a + 1, 32 * b, 2), A("Tf", 16 * a, 16 * b))
+            for m in range(a, b):
+                ku = A("Tf", 32 * m, 32 * m + 32)
+                if m in VMUL:
+                    ts(ku, A("U", 0, 32), A("kf", m, m + 1), O.mult)
+                else:
+                    act(ku, A("UF", 0, 32), F.Copy, None, A("kf", m, m + 1))
+                tt(A("T", 32 * m, 32 * m + 32), ku, A("Fi", 0, 32), O.add)
             ts(A("T", 32 * a, 32 * b), A("T", 32 * a, 32 * b), 8191, O.bitwise_and)
             cp(A("OT", 32 * a, 32 * b), A("T", 32 * a, 32 * b))
         act(A("UU", 0, 64, 2), A("UF", 32, 64), F.Copy, None, 64.0)
@@ -496,13 +523,13 @@ def rank_program(g, core, T, topo):
             mm(A("B7", (3 - c) * 128, (3 - c) * 128 + 128), A("RV1", c * 128, c * 128 + 128), A("Jm"), False)
         scan(A("oks"), A("B7"), A("oneb"), -16384.0, O.max, O.mult)
         act(A("tot"), A("oks", 511, 512), F.Identity, A("b512"))
-        act(A("dg"), A("idf"), F.Copy, None, A("tot"))
-        mm(A("B6", 0, 128), A("onef"), A("dg"), True)
-        mm(A("B6", 128, 129), A("sel15"), A("SG", t * 512 - 1, t * 512) if t else A("neg1"), False)
-        tt(A("cmx", 0, 129), A("B6", 0, 129), A("cm", 0, 129), O.mult)
-        add("v", [A("cry")], [A("cmx", 0, 129)], lambda s: V.tensor_reduce(A("cry")[0], A("cmx", 0, 129)[0], AxisListType.X, O.max), 129 * CY)
+        act(A("dg"), A("mW", 0, 16), F.Copy, None, A("tot"))
+        mm(A("B6", 0, 16), A("BMf"), A("dg"), True)
+        mm(A("B6", 16, 17), A("sel15"), A("SG", t * 512 - 1, t * 512) if t else A("neg1"), False)
+        tt(A("cmx", 0, 17), A("B6", 0, 17), A("cm", 0, 17), O.mult)
+        add("v", [A("cry")], [A("cmx", 0, 17)], lambda s: V.tensor_reduce(A("cry")[0], A("cmx", 0, 17)[0], AxisListType.X, O.max), 64 * CY)
         ts(A("Ut"), A("oks"), A("b512"), O.add, A("cry"), O.max)
-        ops[dma(A("Urep", 0, 8192, 1, 0, 128, 16), A("Ut"), 0.6)]["urge"] = URGE["U"]
+        dma(A("Urep", 0, 8192, 1, 0, 128, 16), A("Ut"), 0.6)
 
     def choose():
         ts(A("kp"), A("Ki"), 63, O.bitwise_and)
@@ -511,7 +538,7 @@ def rank_program(g, core, T, topo):
         tt(A("f1"), A("DI"), A("thS"), O.is_lt)
         tt(A("tf"), A("pr", 0, 64, 2), A("pr", 1, 64, 2), O.add)
         ts(A("lim"), A("f1"), 8096.0, O.mult)
-        tt(A("tc"), A("tf"), A("FF", 32, 64), O.add)
+        tt(A("tc"), A("tf"), A("Fi", 32, 64), O.add)
         ts(A("cI"), A("tc"), 8191, O.bitwise_and)
         tt(A("fit"), A("cI"), A("lim"), O.is_lt)
         mm(A("B3", 0, 32), A("tri"), A("fit"), True)
@@ -548,7 +575,7 @@ def rank_program(g, core, T, topo):
     def marks(k, c):
         ts(A("hs", k, k + 4), A("ts_", k, k + 4), M512, O.add, M512, O.subtract)
         tt(A("nb", k, k + 4), A("hs", k, k + 4), A("ts_", k, k + 4), O.subtract)
-        if VSTEP[-1] >= k and VSTEP[0] < k + 4:
+        if [i for i in VSTEP if k <= i < k + 4]:
             ts(A("nb2", k, k + 4), A("nb", k, k + 4), -1.0, O.mult, 255.0, O.add)
             ts(A("nb3", k, k + 4), A("nb", k, k + 4), -1.0, O.mult, -1.0, O.add)
         for i in range(k, k + 4):
@@ -619,7 +646,7 @@ def rank_program(g, core, T, topo):
         mm(A("B5"), A("TBc"), A("oneb"), False)
         if t < RO - 1:
             tt(A("x0c"), A("x0c"), A("B5"), O.max)
-            ops[dma(A("X", 0, 8192, 1, 0, 128, 16), A("x0c"))]["urge"] = URGE["X"]
+            dma(A("X", 0, 8192, 1, 0, 128, 16), A("x0c"))
             act(A("SG", t * 512, t * 512 + 512), A("x0c"), F.Sign, A("bB"))
         else:
             mm(A("B5"), A("idb"), A("Rb"), False)
@@ -657,16 +684,10 @@ def rank_program(g, core, T, topo):
             act(A("Gn", 256, 512), b, F.Identity, 255.0, -1.0)
             dma(hbm(T.yg[:, :]), A("Gn"))
 
-    early[0] = URGE["c"]
     consts()
     for t in range(RO):
-        early[0] = 0.0 if t else URGE["l"]
         weights(t)
         lists(t)
-        early[0] = 0.0
-        if t == 0:
-            for k in range(8):
-                iota(A("Urep", 1032 * k, 1032 * k + 1032), [[0, 1032]], 0, 0)
         utable(t)
         if t == RO - 1:
             for k in range(3):

@@ -7,19 +7,22 @@ QG = 192
 BIG = 16777216.0
 M16 = 1.5 * 2.0 ** 27
 M512 = 1.5 * 2.0 ** 32
-PATH = [3, 3, 1, 3, 1, 3, 1, 3, 1, 3, 1, 3, 1, 1, 3, 1]
-HALVED = [14, 15]
-LCUT = [(0, 1), (1, 3), (3, 16)]
+PATH = [3, 1, 3, 1, 3, 1, 3, 3, 1, 3, 1, 1, 1, 1, 3, 3]
+HALVED = [13, 15]
+LCUT = [(0, 1), (1, 3), (3, 8), (8, 16)]
+PAIR = []
+RSEL = 0
+NB3, LURGE, USPLIT, ESIG, EQS = 3, [0.3, 0.3, 0.0, 0.0, 0.0], 1, [], 1
 VMUL = [0]
-VSTEP = [6, 7]
-KB = [(0, 8), (8, 12), (12, 16)]
+VSTEP = [5, 6, 7]
+KB = [(0, 8), (8, 13), (13, 16)]
 SSEL = [c for c in range(32) if c % 2]
 
 _f = "x0c:512b oks:512 Ut:512 RV1:512b SG:2560b Yt:512 Z4:512 Rb:512b G0:512b idf:128 idb:128b nidb:128b BM:128b BMf:128 nBMh:128b BMgf:8 BMg4:32 tri:128b oneb:512b onef:128"
-_f += " O16:16b O16n:16b O16d:16b i65:66b n65:66b mW:128 t32:32 id2:64 z16:128b rsA:512b rsB:256b rs64:256b ph:1i tE:32 Pat:1024b KM:32 KMm:32 thr:1 thS:32 c16f:128"
-_f += " Bp:128b Rp:128b B16:32b nB16:32 TriB:128b TBc:128b cm:18 Pm:128b Jm:128b IO:512b sel15:128b neg1:1b pi:1i pj:1i rcol:1 r32:1 r0m:1 r1m:1 b512:1 iW:96 j255:512"
-_f += " rself:128 rselb:128b n1k:64b kA:16i kB:16i iM:16 slS:32i slL:32i tA:128b tB:128b tC:128b X:8208b Urep:8256 A0:8192b Ab:8192b xq:1536b o32:128b zb:128b half:1b j256:256b"
-_f += " nb2:8 nb3:8 wti:4i kmi:16i thi:1i wf:4 nwf:4 kf:16 Lw:2048b Wn:8b Wp:32b Wff:8 BMw:128b c255:128b ui:64i U:64i sq:64i Fi:64i UF:64 UU:64 T:512i Tf:512 OT:512u KS:1024"
+_f += " O16:16b O16n:16b O16d:16b i65:66b n65:66b mW:128 t32:32 id2:64 z16:128b rsK:1024b rs64:256b ph:1i tE:32 Pat:1024b KM:32 KMm:32 thr:1 thS:32 c16f:128"
+_f += " Bp:128b Rp:128b B16:32b nB16:32 TriB:128b TBc:128b cm:18 Pm:128b Jm:128b IO:512b sel15:128b neg1:1b pi:1i pj:1i rcol:1 r32:1 r0m:1 r1m:1 b512:1 iW:96 j255:512b"
+_f += " rself:128 rselb:128b n1k:64b kA:16i kB:16i iM:16 slS:32i slL:32i tA:128b tB:128b tC:128b X:8208b Urep:8288 i8k:128b mC0:64b A0:8192b Ab:8192b o32:128b zb:128b half:1b j256:256b"
+_f += " nb2:8 nb3:8 wti:4i kmi:16i thi:1i wf:4 nwf:4 kf:16 Lw:144b Wp:32b BMw:128b c255:128b ui:64i U:64i sq:64i Fi:64i UF:64 UU:64 AD:256b i22:128b c8256:64b mB:128b rs16:128b cb:18b k1024:128b n1024:32b T:512i Tf:512 OT:512u KS:1024"
 _f += " KAB:64 Ki:64i kp:64i pr:64 tf:32 tc:32i cI:32i DI:32i f1:32 lim:32 fit:32b rsel:32 ST:2112b VZ:1040b Pc:64 Pd:64b Cc:128b Ck:128b Cq:128b Cs:128b wv:11 tmA:128 tmB:128"
 _f += " tsA:64 tsB:64 EQ:256 SC:256 win:4b Mk:512b Jc:8b Jf:8 cvec:4 pos:4u mC:4 t0:4 t1:4 h16:4 OFU:4u OF2:4u OFX:8u OFP:4u OFC:4u UG:128 u1A:64 u1B:64 u2A:64 u2B:64 XG:256b XP:64b"
 _f += " mP:1600b mT:1664b ts_:8 hs:8 nb:8 HH:1024b sgn:4096b LL:512b EE:128b SS:128b S1:96b dT:128b MI:32u tot:1 dg:16 cmx:18 cry:1 Gn:512b bA:1 bB:1 b2:1"
@@ -51,7 +54,8 @@ for _t in range(RO):
     SEMAPHORES += ["aP%d" % _t, "aT%d" % _t, "lP%d" % _t, "lT%d" % _t, "cP%d" % _t, "cT%d" % _t, "lC%d" % _t]
 
 CY, PE_CY, GA, SCA, HOP, DMA_T, REM_T, X_T = 0.88e-3, 0.45e-3, 1.56, 3.8, 0.2, 1.6, 2.0, 6.0
-PASSES, SEED, SHAKE, CASES = 210, 1, 6.0, ((1.0, 0.22), (1.15, 0.15), (1.3, 0.2))
+MOVES, SHIFT = 500, 1.5
+PASSES, SEED, SHAKE, CASES = 90, 1, 6.0, ((1.0, 0.22), (1.15, 0.15), (1.3, 0.2))
 _order = {}
 
 
@@ -139,6 +143,31 @@ def _lay_out(ops):
                 key[i] = max([key[i]] + [key[s] + 1e-6 for s in succ[i]])
         at = {i: j for j, i in enumerate(back)}
         order = sorted(range(n), key=lambda i: (-key[i], -at[i]))
+    at = {i: j for j, i in enumerate(best[3])}
+    back = sorted(range(n), key=lambda i: (-(best[2][i] + ops[i]["busy"]), -at[i]))
+    key = [-best[2][i] for i in range(n)]
+    kin = {}
+    for i, o in enumerate(ops):
+        kin.setdefault(o["tag"], []).append(i)
+    tags = sorted((t for t in kin if len(kin[t]) > 1 and t[0] in "vst"), key=lambda t: best[2][kin[t][1]])
+    for k in range(MOVES):
+        a, c, new = int(draw() * len(tags)), (draw() - 0.5) * SHIFT, list(key)
+        for t in tags[a:a + 1 + int(draw() * draw() * 12)]:
+            if t[0] == tags[a][0]:
+                for i in kin[t]:
+                    new[i] += c
+        for i in back:
+            new[i] = max([new[i]] + [new[s] + 1e-6 for s in succ[i]])
+        order = sorted(range(n), key=lambda i: (-new[i], at[i]))
+        start = lay(order, pre, zero)
+        now = {i: j for j, i in enumerate(order)}
+        issue = sorted(range(n), key=lambda i: (start[i], now[i]))
+        span = sum(play(issue, s, h) / s for (s, h) in CASES) / len(CASES)
+        if span < best[0] - 1e-9:
+            best = (span, issue, start, order)
+            key = [-x for x in start]
+            at = now
+            back = sorted(range(n), key=lambda i: (-(start[i] + ops[i]["busy"]), -at[i]))
     _order["span"] = best[0]
     return best[1]
 
@@ -149,7 +178,7 @@ def rank_program(g, core, T, topo):
         return
     queues = {"v": g.vector, "s": g.scalar, "t": g.tensor, "g": g, "y": g.sync}
     own = {"v": "sv", "s": "ss", "t": "st", "g": "sg"}
-    ops, log, banks = [], {}, {}
+    ops, log, banks, seen = [], {}, {}, {}
 
     def A(n, lo=0, hi=None, st=1, p0=0, p1=128, pst=1):
         p, o, c = _where[n]
@@ -158,6 +187,10 @@ def rank_program(g, core, T, topo):
         hi = lo + (k - 1) * st + 1
         ap = T[p][p0:p1:pst, o + lo:o + hi:st] if (pst != 1 or st != 1) else T[p][p0:p1, o + lo:o + hi]
         return (ap, [(p, o + lo, o + hi, st, p0, p1)], k, SCRATCH[p][2], SCRATCH[p][0])
+
+    def back(n):
+        a = A(n)
+        return (T[n][0:128, ::-1],) + a[1:]
 
     def IX(win, off):
         return (win[0].indirect(off[0]), win[1] + off[1], 16 * off[2], win[3], "ix")
@@ -177,6 +210,9 @@ def rank_program(g, core, T, topo):
         i = len(ops)
         dep = set(after)
         o = {"q": q, "f": f, "busy": busy, "lat": lat, "dep": dep, "ord": set(after), "sem": sem or own.get(q), "inc": inc, "grp": None, "first": first}
+        tag = (q,) + tuple((r[0].rstrip("0123") if r[0][0] in "QC" else r[0],) + r[1:] for r in rg(outs)[:1] + rg(ins)[:1])
+        seen[tag] = seen.get(tag, 0) + 1
+        o["tag"] = tag + (seen[tag],)
         ops.append(o)
         for regs, isw in ((rg(ins), False), (rg(outs), True)):
             for r in regs:
@@ -293,7 +329,7 @@ def rank_program(g, core, T, topo):
     d.append(dma(A("kmi"), hbm(T.km[:, :]), after=d[-1:]))
     d.append(dma(A("x0c"), hbm(T.xs[0:128:16, :]), after=d[-1:]))
     d.append(dma(A("X", 0, 8192), hbm(T.xs[:, :]), X_T, after=d[-1:]))
-    dma(A("thi"), hbm(T.th[:, :]), X_T, after=d[-1:])
+    dma(A("thi"), hbm(T.th[:, :]), X_T + 3.0, after=d[-1:])
     o128 = A("oneb", 0, 128)
 
     def consts():
@@ -321,10 +357,9 @@ def rank_program(g, core, T, topo):
         ts(A("r32"), A("pj"), 32.0, O.add)
         ts(A("r0m"), A("pj"), 0.0, O.is_equal)
         ts(A("r1m"), A("pj"), 1.0, O.is_equal)
-        ms(A("rsA"), 0.0)
-        ms(A("rsA", 0, 512, 8), BIG)
-        ms(A("rsB"), 0.0)
-        ms(A("rsB", 0, 256, 4), BIG)
+        ms(A("rsK"), 0.0)
+        for (a, b) in KB:
+            ms(A("rsK", 64 * a, 64 * b, b - a), BIG)
         for n, c in (("O16", 1024.0), ("O16n", -1024.0), ("O16d", 2048.0)):
             act(A(n, 0, 16, 2), A("BMgf"), F.Copy, None, c)
             act(A(n, 1, 16, 2), A("BMgf"), F.Copy, None, c)
@@ -345,17 +380,17 @@ def rank_program(g, core, T, topo):
         sel(A("idf"), A("onef"), [[-1, 128]], O.is_equal, 0, 1)
         act(A("idb"), A("idf"), F.Copy)
         act(A("nidb"), A("idf"), F.Copy, None, -1.0)
-        sel(A("Pm"), o128, [[-16, 8], [1, 16]], O.is_equal, -15, 1)
-        sel(A("Jm"), o128, [[1, 128]], O.is_equal, -127, 1)
-        act(A("Jm"), A("Jm"), F.Copy, None, -8192.0)
+        act(A("i8k"), A("idf"), F.Copy, None, 8192.0)
+        if EQS:
+            act(A("i22"), A("idf"), F.Copy, None, 4194304.0)
+            ms(A("c8256"), 8256.0)
         iota(A("j255"), [[1, 512]], -255, 0)
-        iota(A("IO"), [[16, 32], [0, 16]], 0, 0)
-        iota(A("RV1"), [[0, 32], [1, 16]], 1, 0)
-        cp(A("IO", 0, 512, 1, 32, 64), A("RV1", 0, 512, 1, 32, 64))
+        cp(A("IO", 0, 512, 1, 0, 32), A("j255", 0, 512, 1, 0, 32))
+        ms(A("IO", 0, 512, 1, 32, 64), 255.0)
+        ms(A("IO", 0, 512, 1, 64, 96), 16384.0)
         ms(A("o32"), 1.0 / 32)
         ms(A("zb"), 0.0)
         ms(A("half"), 0.5)
-        iota(A("j256"), [[1, 256]], 0, 0)
         sel(A("tri"), o128, [[1, 128]], O.is_ge, 0, -1)
         sel(A("tB"), o128, [[1, 128]], O.is_gt, 0, -1)
         tt(A("tB"), A("tB"), A("BM"), O.mult)
@@ -363,29 +398,35 @@ def rank_program(g, core, T, topo):
         tt(A("TriB"), A("tA"), A("idb"), O.add)
         iota(A("i65"), [[1, 66]], 1, 0)
         act(A("n65"), A("i65"), F.Identity, 0.5, -1.0)
-        ts(A("cm", 0, 16), A("i65", 0, 16), A("rcol"), O.is_le)
-        ms(A("cm", 16, 17), 1.0)
+        ts(A("cm", 0, 16), A("i65", 0, 16), -1.0, O.add)
+        ts(A("cb", 0, 16), A("cm", 0, 16), A("rcol"), O.is_le, 32768.0, O.mult)
+        ms(A("cb", 16, 17), 8192.0)
         iota(A("slS"), [[128, 4], [0, 8]], 0, 1, False)
         ms(A("bA"), 191.5)
         ms(A("bB"), -256.0)
-        ms(A("b2"), 2.0)
         ms(A("neg1"), -1.0)
         ms(A("n1k"), -1024.0)
         act(A("SG", 2048, 2560), A("x0c"), F.Sign, A("bA"), -1.0)
         tt(A("id2"), A("idf", 0, 64), A("idf", 64, 128), O.add)
         tt(A("t32"), A("id2", 0, 32), A("id2", 32, 64), O.add)
         tt(A("mW", 0, 16), A("t32", 0, 16), A("t32", 16, 32), O.add)
-        for k in (16, 32, 64):
-            act(A("mW", k, 2 * k), A("mW", 0, k), F.Copy)
+        act(A("mB", 0, 16), A("mW", 0, 16), F.Identity, BIG / 2, -BIG / 2)
+        for k in (16, 32):
+            act(A("mB", k, 2 * k), A("mB", 0, k), F.Copy)
+        act(A("mB", 64, 128), A("mB", 0, 64), F.Copy)
+        ts(A("mC0"), A("mB", 0, 64), 8256.0, O.max)
         ms(A("c16f"), 0.0625)
-        ms(A("z16"), 1.0)
-        ms(A("z16", 0, 128, 16), 0.0)
+        ms(A("rs16"), -BIG)
+        ms(A("rs16", 0, 128, 16), BIG)
+        if RSEL:
+            act(A("k1024"), A("idf"), F.Copy, None, 1024.0)
+            ms(A("n1024"), -1024.0)
         ms(A("rs64"), -BIG)
         ms(A("rs64", 0, 256, 64), BIG)
         act(A("rself"), A("BM"), F.Copy, None, A("r0m"))
         act(A("rselb"), A("BM"), F.Copy, None, A("r0m"))
         wv = [A("wv", k, k + 1) for k in range(11)]
-        ts(wv[10], A("pj"), 15.0, O.is_equal, -1.0, O.mult)
+        ts(wv[10], A("pj"), 15.0, O.is_equal, 0.5, O.mult)
         act(A("sel15"), A("BM"), F.Copy, None, wv[10])
         act(A("nBMh"), A("BM"), F.Copy, None, -0.5)
         act(A("tC"), A("BM"), F.Identity, -4096.0, 4096.0)
@@ -410,7 +451,7 @@ def rank_program(g, core, T, topo):
         ts(wv[2], A("ph"), 2.0, O.is_equal, 0.5, O.mult)
         ts(wv[3], A("pj"), 6.0, O.is_equal)
         ts(wv[4], A("pj"), 7.0, O.is_equal, -0.25, O.mult)
-        ts(wv[5], wv[3], 32.0, O.mult, wv[0], O.add)
+        ts(wv[5], wv[3], -4128.0, O.mult, wv[0], O.add)
         ts(wv[6], wv[3], 92.0, O.mult, wv[2], O.add)
         ts(wv[7], wv[3], -2097152.0, O.mult, wv[2], O.add)
         ts(wv[8], wv[7], wv[1], O.add)
@@ -435,34 +476,34 @@ def rank_program(g, core, T, topo):
         ts(A("tE"), A("BMg4"), A("thr"), O.mult)
         mm(A("B5", 0, 32), A("c16f"), A("tE"))
         cp(A("thS"), A("B5", 0, 32))
+        ms(A("Urep", 8192, 8288), 8192.0)
         for k in range(8):
-            iota(A("Urep", 1032 * k, 1032 * k + 1032), [[0, 1032]], 0, 0)
+            iota(A("Urep", 1024 * k, 1024 * k + 1024), [[0, 1024]], 0, 0)
 
     def weights(t):
         w, nw = A("wf", t, t + 1), A("nwf", t, t + 1)
-        act(A("Wff"), A("BMgf"), F.Copy, None, nw)
-        act(A("Wn"), A("BMgf"), F.Copy, None, nw)
+        act(A("Lw", 15, 143, 16), A("BMgf"), F.Copy, None, nw)
         act(A("Wp"), A("BMg4"), F.Copy, None, w)
         act(A("BMw"), A("BM"), F.Copy, None, w)
-        for q in range(8):
-            act(A("Lw", 16 * q, 16 * q + 1936, 129), A("oneb", 0, 16), F.Copy, None, A("Wff", q, q + 1))
 
     def lists(t):
         Q = "Q%d" % t
         mm(A("B4", 0, 32), A("BMw"), A("c255", 0, 32), True)
-        mm(A("B4", 32, 64), A("c255"), A("Wp"), False)
+        bs = "B1" if USPLIT else "B4"
+        mm(A(bs, 32, 64), A("c255"), A("Wp"), USPLIT == 1)
         for r in range(16):
-            mm(A("B4", 0, 32), A("Lw", r * 128, r * 128 + 128), A(Q, QG + r, QG + 512, 16), False)
+            mm(A("B4", 0, 32), A("Lw", 15 - r, 143 - r), A(Q, QG + r, QG + 512, 16), False)
         for b in range(4):
-            mm(A("B4", 32 + 8 * b, 40 + 8 * b), A(Q, QG + 128 * b, QG + 128 * b + 128), A("Wn"), False)
-        cp(A("ui"), A("B4", 0, 64))
-        ts(A("U"), A("ui"), 4095, O.bitwise_and)
+            mm(A(bs, 32 + 8 * b, 40 + 8 * b), A(Q, QG + 128 * b, QG + 128 * b + 128), A("Lw", 15, 143, 16), False)
+        for (a, b, n) in ((0, 32, "B4"), (32, 64, bs)) if USPLIT else ((0, 64, "B4"),):
+            cp(A("ui", a, b), A(n, a, b))
+            ts(A("U", a, b), A("ui", a, b), 4095, O.bitwise_and)
+            cp(A("UF", a, b), A("U", a, b))
         tt(A("sq", 0, 32), A("U", 0, 32), A("U", 0, 32), O.mult)
         ts(A("Fi", 0, 32), A("sq", 0, 32), 5, O.logical_shift_right)
-        cp(A("UF"), A("U"))
         tt(A("sq", 32, 64), A("U", 32, 64), A("U", 32, 64), O.mult)
         ts(A("Fi", 32, 64), A("sq", 32, 64), 5, O.logical_shift_right)
-        for (a, b) in LCUT:
+        for j, (a, b) in enumerate(LCUT):
             for m in range(a, b):
                 ku = A("Tf", 32 * m, 32 * m + 32)
                 if m in VMUL:
@@ -472,6 +513,7 @@ def rank_program(g, core, T, topo):
                 tt(A("T", 32 * m, 32 * m + 32), ku, A("Fi", 0, 32), O.add)
             ts(A("T", 32 * a, 32 * b), A("T", 32 * a, 32 * b), 8191, O.bitwise_and)
             cp(A("OT", 32 * a, 32 * b), A("T", 32 * a, 32 * b))
+            ops[-1]["lat"] = LURGE[j]
         act(A("UU", 0, 64, 2), A("UF", 32, 64), F.Copy, None, 64.0)
         act(A("UU", 1, 64, 2), A("UF", 32, 64), F.Copy)
 
@@ -488,9 +530,12 @@ def rank_program(g, core, T, topo):
                 src, h = IX(A("X"), A("OT", 32 * m + lo // 16, 32 * m + hi // 16)), A(Q, QG + lo, QG + hi)
                 a0, ab = A("A0", o + lo, o + hi), A("Ab", o + lo, o + hi)
                 if PATH[m] == 3:
-                    bank, x = A("B%d" % (3 + n3 % 3), 0, hi - lo), A("xq", 512 * (n3 % 3), 512 * (n3 % 3) + hi - lo)
+                    bank, x = A("B%d" % (3 + n3 % NB3), 0, hi - lo), a0
                     n3 += 1
-                    act(x, src, F.Copy)
+                    if m in PAIR:
+                        act(A("A0", o, o + 1024), IX(A("X"), A("OT", 32 * m, 32 * m + 64)), F.Copy)
+                    elif m - 1 not in PAIR:
+                        act(x, src, F.Copy)
                     mm(bank, A("nidb"), h, True)
                     mm(bank, A("idb"), x, False)
                     act(ab, bank, F.Abs)
@@ -505,30 +550,28 @@ def rank_program(g, core, T, topo):
                     out = A("B%d" % k, c * 16 * w + m - a, (c + 1) * 16 * w, w)
                     if PATH[m] == 1:
                         mm(out, A("A0", o + 128 * c, o + 128 * c + 128), A("O16n"), False)
-                    mm(out, A("Ab", o + 128 * c, o + 128 * c + 128), A("O16d" if PATH[m] == 1 else "O16"), False)
+                    mm(out, A("Ab", o + 128 * c, o + 128 * c + 128), A("O16" if PATH[m] in (2, 3) else "O16d"), False)
             if m == b - 1:
-                scan(A("KS", 64 * a, 64 * b), A("rsA" if b - a == 8 else "rsB"), A("B%d" % k, 0, 64 * (b - a)), 0.0, O.max, O.min)
-        tt(A("KAB"), A("KS", 7, 512, 8), A("KS", 515, 768, 4), O.min)
-        tt(A("Ki"), A("KAB"), A("KS", 771, 1024, 4), O.min)
+                scan(A("KS", 64 * a, 64 * b), A("rsK", 64 * a, 64 * b), A("B%d" % k, 0, 64 * (b - a)), 0.0, O.max, O.min)
+        low = [A("KS", 64 * a + b - a - 1, 64 * b, b - a) for (a, b) in KB]
+        if len(low) == 3:
+            tt(A("KAB"), low[0], low[1], O.min)
+        tt(A("Ki"), A("KAB") if len(low) == 3 else low[0], low[-1], O.min)
 
     def utable(t):
-        for c in range(4):
-            o = c * 128
-            mm(A("B6", o, o + 128), A("SG", 2048 + o, 2048 + o + 128), A("Pm"), c == 0)
-            if t:
-                mm(A("B6", o, o + 128), A("SG", (t - 1) * 512 + o, (t - 1) * 512 + o + 128), A("Pm"), False)
-        act(A("RV1"), A("B6"), F.Identity, A("b2"), 1.0 if t else 2.0)
-        mm(A("B7"), A("o32", 0, 128, 1, 0, 64), A("IO", 0, 512, 1, 0, 64), True)
-        for c in range(4):
-            mm(A("B7", (3 - c) * 128, (3 - c) * 128 + 128), A("RV1", c * 128, c * 128 + 128), A("Jm"), False)
-        scan(A("oks"), A("B7"), A("oneb"), -16384.0, O.max, O.mult)
-        act(A("tot"), A("oks", 511, 512), F.Identity, A("b512"))
+        k = (t - 1) % 5 if t else 4
+        mm(A("B7"), A("o32", 0, 128, 1, 0, 96), A("IO", 0, 512, 1, 0, 96), True)
+        mm(A("B7"), A("i8k"), A("SG", 2048, 2560), False)
+        mm(A("B7"), A("i8k"), A("SG", 512 * k, 512 * k + 512), False)
+        scan(back("oks"), back("B7"), A("oneb"), 32768.0, O.min, O.mult)
+        act(A("tot"), A("oks", 0, 1), F.Identity, A("b512"))
         act(A("dg"), A("mW", 0, 16), F.Copy, None, A("tot"))
-        mm(A("B6", 0, 16), A("BMf"), A("dg"), True)
+        mm(A("B6", 0, 17), A("idb"), A("cb", 0, 17), True)
+        mm(A("B6", 0, 16), A("BMf"), A("dg"), False)
+        mm(A("B6", 16, 17), A("sel15"), A("neg1"), False)
         mm(A("B6", 16, 17), A("sel15"), A("SG", t * 512 - 1, t * 512) if t else A("neg1"), False)
-        tt(A("cmx", 0, 17), A("B6", 0, 17), A("cm", 0, 17), O.mult)
-        add("v", [A("cry")], [A("cmx", 0, 17)], lambda s: V.tensor_reduce(A("cry")[0], A("cmx", 0, 17)[0], AxisListType.X, O.max), 64 * CY)
-        ts(A("Ut"), A("oks"), A("b512"), O.add, A("cry"), O.max)
+        add("v", [A("cry")], [A("B6", 0, 17)], lambda s: V.tensor_reduce(A("cry")[0], A("B6", 0, 17)[0], AxisListType.X, O.min), 64 * CY)
+        ts(A("Ut"), A("oks"), A("b512"), O.add, A("cry"), O.min)
         dma(A("Urep", 0, 8192, 1, 0, 128, 16), A("Ut"), 0.6)
 
     def choose():
@@ -541,48 +584,57 @@ def rank_program(g, core, T, topo):
         tt(A("tc"), A("tf"), A("Fi", 32, 64), O.add)
         ts(A("cI"), A("tc"), 8191, O.bitwise_and)
         tt(A("fit"), A("cI"), A("lim"), O.is_lt)
-        mm(A("B3", 0, 32), A("tri"), A("fit"), True)
-        mm(A("B3", 8, 32), o128, A("fit", 0, 24), False)
-        mm(A("B3", 16, 32), o128, A("fit", 0, 16), False)
-        mm(A("B3", 24, 32), o128, A("fit", 0, 8), False)
+        for bank in ("B3", "B1")[:1 + RSEL]:
+            if RSEL:
+                mm(A(bank, 0, 32), A("idb"), A("n1024"), True)
+                mm(A(bank, 0, 32), A("k1024"), A("fit"), False)
+            mm(A(bank, 0, 32), A("tri"), A("fit"), not RSEL)
+            mm(A(bank, 8, 32), o128, A("fit", 0, 24), False)
+            mm(A(bank, 16, 32), o128, A("fit", 0, 16), False)
+            mm(A(bank, 24, 32), o128, A("fit", 0, 8), False)
         for v, n in ((16, "cI"), (18, "DI")):
             cp(A("VZ", v, 1040, 32), A(n))
             tt(A("VZ", v + 1, 1040, 32), A(n), A("VZ", v, 1040, 32), O.subtract)
-        tt(A("rsel"), A("B3", 0, 32), A("fit"), O.mult)
+        if RSEL:
+            act(A("rsel"), A("B1", 0, 32), F.Copy)
+        else:
+            tt(A("rsel"), A("B3", 0, 32), A("fit"), O.mult)
         mm(A("B4", 0, 65), A("zb"), A("i65", 0, 65), True)
         for c in range(32):
             st = A("ST", c * 66, c * 66 + 65)
             if c in SSEL:
                 act(st, A("n65", 0, 65), F.Sign, A("rsel", c, c + 1))
             else:
-                ts(st, A("i65", 0, 65), A("rsel", c, c + 1), O.is_le, 2.0, O.mult)
+                ts(st, A("i65", 0, 65), A("B3" if RSEL else "rsel", c, c + 1), O.is_le, 2.0, O.mult)
             w, p = 16 + 32 * c - 16 * (c % 2), 32 * (c % 8 // 2)
             mm(A("B4", 0, 65, 1, p, p + 32), A("VZ", w, w + 32), st, False)
         cp(A("Pc"), A("B4", 1, 65))
         tt(A("Pd"), A("B4", 0, 64), A("Pc"), O.subtract)
-        mm(A("B0", 0, 64), A("Cc"), A("Pd"), True)
+        mm(A("B0", 0, 64), A("idb"), A("mC0"), True)
+        mm(A("B0", 64, 128), A("idb"), A("mB", 0, 64), False)
+        mm(A("B0", 0, 64), A("Cc"), A("Pd"), False)
         mm(A("B0", 64, 128), A("Ck"), A("Pd"), False)
-        for k in range(4):
-            mm(A("B3", 128 + 64 * k, 192 + 64 * k), A("Cq"), A("Pd"), k == 0)
+        mm(A("B3", 384, 448), A("idb"), A("mB", 0, 64), True)
+        mm(A("B3", 64, 128), A("Cc"), A("Pd"), False)
+        for k in range(4 - EQS):
+            mm(A("B3", 128 + 64 * k, 192 + 64 * k), A("Cq"), A("Pd"), False)
         mm(A("B3", 384, 448), A("Cs"), A("Pd"), False)
 
-    def wrap(a, b, src):
+    def wrap(b, src):
         n = src[2]
-        tt(A(a, 0, n), src, A("mW", 0, n), O.mult)
-        scan(A(b, 0, n), A("z16", 0, n), A(a, 0, n), 0.0, O.mult, O.add)
+        scan(A(b, 0, n), A("rs16", 0, n), src, 0.0, O.max, O.min)
         return A(b, 15, n, 16)
 
     def marks(k, c):
         ts(A("hs", k, k + 4), A("ts_", k, k + 4), M512, O.add, M512, O.subtract)
-        tt(A("nb", k, k + 4), A("hs", k, k + 4), A("ts_", k, k + 4), O.subtract)
-        if [i for i in VSTEP if k <= i < k + 4]:
-            ts(A("nb2", k, k + 4), A("nb", k, k + 4), -1.0, O.mult, 255.0, O.add)
-            ts(A("nb3", k, k + 4), A("nb", k, k + 4), -1.0, O.mult, -1.0, O.add)
+        if [i for i in range(k, k + 4) if i not in VSTEP]:
+            tt(A("nb", k, k + 4), A("hs", k, k + 4), A("ts_", k, k + 4), O.subtract)
+        if [i for i in range(k, k + 4) if i in VSTEP]:
+            tt(A("nb2", k, k + 4), A("ts_", k, k + 4), A("hs", k, k + 4), O.subtract)
         for i in range(k, k + 4):
             hh = A("HH", 128 * i, 128 * i + 128)
             if i in VSTEP:
-                for h, n in enumerate(("nb2", "nb3")):
-                    ts(A("sgn", 512 * i + 256 * h, 512 * i + 256 * h + 256), A("j256"), A(n, i, i + 1), O.is_gt, 0.5, O.subtract)
+                ts(A("sgn", 512 * i, 512 * i + 512), A("j255"), A("nb2", i, i + 1), O.is_gt, 0.5, O.subtract)
             else:
                 act(A("sgn", 512 * i, 512 * i + 512), A("j255"), F.Sign, A("nb", i, i + 1))
             ts(hh, A("Bp"), A("hs", i, i + 1), O.is_equal, 2 * c if i in VSTEP else c, O.mult)
@@ -590,13 +642,24 @@ def rank_program(g, core, T, topo):
 
     def give(t):
         Q, C = "Q%d" % t, "C%d" % t
-        wrap("tmA", "tmB", A("B0", 0, 128))
+        wrap("tmB", A("B0", 0, 128))
         cW = A("tmB", 15, 64, 16)
-        for k in range(4):
-            ts(A("EQ", 64 * k, 64 * k + 64), A("B0", 0, 64), A("tmB", 15 + 16 * k, 16 + 16 * k), O.is_equal)
-        tt(A("EQ"), A("EQ"), A("B3", 128, 384), O.mult)
-        sW = wrap("tsA", "tsB", A("B3", 384, 448))
-        scan(A("SC"), A("rs64"), A("EQ"), 0.0, O.max, O.min)
+        n = 256 - 64 * EQS
+        for k in range(4 - EQS):
+            ts(A("EQ", 64 * k, 64 * k + 64), A("B3", 64, 128), 8256.0, O.add, A("tmB", 15 + 16 * k, 16 + 16 * k), O.is_equal)
+        tt(A("EQ", 0, n), A("EQ", 0, n), A("B3", 128, 128 + n), O.mult)
+        sW = wrap("tsB", A("B3", 384, 448))
+        scan(A("SC", 0, n), A("rs64", 0, n), A("EQ", 0, n), 0.0, O.max, O.min)
+        if EQS:
+            mm(A("B1", 0, 64), A("idb"), A("c8256"), True)
+            mm(A("B1", 0, 64), A("Cc"), A("Pd"), False)
+            for k in range(EQS):
+                mm(A("B2", 64 * k, 64 * k + 64), A("Cq"), A("Pd"), k == 0)
+            for k in range(EQS):
+                c = 15 + 16 * (4 - EQS + k)
+                act(A("AD", 64 * k, 64 * k + 64), A("B1", 0, 64), F.Abs, A("tmB", c, c + 1), -1.0)
+                mm(A("B2", 64 * k, 64 * k + 64), A("i22"), A("AD", 64 * k, 64 * k + 64), False)
+            scan(A("SC", n, 256), A("rs64", n, 256), A("B2", 0, 256 - n), 0.0, O.max, O.min)
         tt(A("win"), A("SC", 63, 256, 64), A("tmB", 79, 128, 16), O.is_gt)
         mm(A("B1", 0, 4), A("idb"), A("Jc", 0, 4), True)
         mm(A("B1", 0, 4), A("tB"), A("win"), False)
@@ -610,19 +673,21 @@ def rank_program(g, core, T, topo):
         remote("lC%d" % t, [(rank ^ 1, eP, A("mC"), A(C, 0, 4), "cP%d" % t), (rank ^ 4, eT, A("mC"), A(C, 4, 8), "cT%d" % t)])
         cp(A("pos"), A("B1", 0, 4))
         tt(A("t0"), sW, A("B1", 0, 4), O.subtract)
-        ts(A("OFU"), cW, -1.0, O.mult, 8239.0, O.add)
+        ts(A("OFU"), cW, 16.0, O.add)
         act(A("UG", 0, 64), IX(A("Urep"), A("OFU")), F.Copy)
-        mm(A("B6", 0, 64), A("rself"), A("UG", 0, 64))
-        r1 = wrap("u1A", "u1B", A("B6", 0, 64))
-        ts(A("OF2"), r1, -9.0, O.add, 0.0, O.max)
+        mm(A("B6", 0, 64), A("idb"), A("mB", 0, 64), True)
+        mm(A("B6", 0, 64), A("rself"), A("UG", 0, 64), False)
+        r1 = wrap("u1B", A("B6", 0, 64))
+        ts(A("OF2"), r1, 8.0, O.add, 8191.0, O.min)
         act(A("UG", 64, 128), IX(A("Urep"), A("OF2")), F.Copy)
-        mm(A("B7", 0, 64), A("rself"), A("UG", 64, 128))
-        r2 = wrap("u2A", "u2B", A("B7", 0, 64))
-        ts(A("OFX", 0, 4), r1, -1.0, O.mult, 8192.0, O.add)
-        ts(A("OFX", 4, 8), r2, -1.0, O.mult, 8192.0, O.add)
+        mm(A("B7", 0, 64), A("idb"), A("mB", 0, 64), True)
+        mm(A("B7", 0, 64), A("rself"), A("UG", 64, 128), False)
+        r2 = wrap("u2B", A("B7", 0, 64))
+        cp(A("OFX", 0, 4), r1)
+        cp(A("OFX", 4, 8), r2)
         act(A("XG", 64, 128), IX(A("X"), A("OFX", 0, 4)), F.Copy)
         act(A("XG", 128, 192), IX(A("X"), A("OFX", 4, 8)), F.Copy)
-        ts(A("OFP"), cW, -54.0, O.add, 0.0, O.max)
+        ts(A("OFP"), cW, 10.0, O.add, 8192.0, O.min)
         act(A("XG", 0, 64), IX(A("X"), A("OFP")), F.Copy)
         mm(A("B2", 0, 64), A("idb"), A("n1k"), True)
         mm(A("B2", 0, 64), A("rselb"), A("XG", 0, 64), False)
@@ -636,9 +701,9 @@ def rank_program(g, core, T, topo):
         sct(A("mP"), A("pos"), A("XP"))
         remote("lP%d" % t, [(rank ^ 1, eP, A("mP", 0, 64), A(Q, 0, 64), "aP%d" % t)])
         sct(A(Q, QG + 512, QG + 512 + 1600), A("pos"), A("XG", 192, 256))
-        ts(A("ts_", 0, 4), cW, -319.5, O.add)
+        ts(A("ts_", 0, 4), cW, -255.5, O.add)
         marks(0, 4096.0)
-        ts(A("ts_", 4, 8), r2, -1.0, O.mult, 7937.5, O.add)
+        ts(A("ts_", 4, 8), r2, -254.5, O.add)
         marks(4, -4096.0)
         for i in range(8):
             mm(A("B2", 64, 65), A("HH", 128 * i, 128 * i + 128), A("half") if i in VSTEP else A("oneb", 0, 1), i == 0)
@@ -686,6 +751,7 @@ def rank_program(g, core, T, topo):
 
     consts()
     for t in range(RO):
+        seen.clear()
         weights(t)
         lists(t)
         utable(t)

@@ -8,25 +8,36 @@ BIG = 16777216.0
 M16 = 1.5 * 2.0 ** 27
 M512 = 1.5 * 2.0 ** 32
 PATH = [3, 1, 3, 1, 3, 1, 3, 3, 1, 3, 1, 1, 1, 1, 3, 3]
+PATHS = [PATH, PATH]
 HALVED = [13, 15]
 LCUT = [(0, 1), (1, 3), (3, 8), (8, 16)]
 PAIR = []
-RSEL = 0
-NB3, LURGE, USPLIT, ESIG, EQS = 3, [0.3, 0.3, 0.0, 0.0, 0.0], 1, [], 1
+NB3, LURGE, EQS = 3, [0.3, 0.3, 0.0, 0.0, 0.0], 3
 VMUL = [0]
-VSTEP = [5, 6, 7]
-KB = [(0, 8), (8, 13), (13, 16)]
-SSEL = [c for c in range(32) if c % 2]
+KUB = []
+KB = [(0, 8), (8, 12), (12, 16)]
+KW = [b - a + (b == 16) for (a, b) in KB]
+KO = [sum(KW[:k]) for k in range(len(KB) + 1)]
+NSC = 14
+NZ = 2
+KK = 32768.0
+M1, M64, M128 = 1.5 * 2.0 ** 23, 1.5 * 2.0 ** 29, 1.5 * 2.0 ** 30
+TWO = 1
+FILLV, UG_, UV_ = 128, 8, 3
+FUSE, WSPLIT, MV, XLAT, HINT = 1, 128, 16, 0.3, 0
+TURN = []
+LLS = [0, 1, 2, 3]
+OV = 0
 
-_f = "x0c:512b oks:512 Ut:512 RV1:512b SG:2560b Yt:512 Z4:512 Rb:512b G0:512b idf:128 idb:128b nidb:128b BM:128b BMf:128 nBMh:128b BMgf:8 BMg4:32 tri:128b oneb:512b onef:128"
-_f += " O16:16b O16n:16b O16d:16b i65:66b n65:66b mW:128 t32:32 id2:64 z16:128b rsK:1024b rs64:256b ph:1i tE:32 Pat:1024b KM:32 KMm:32 thr:1 thS:32 c16f:128"
-_f += " Bp:128b Rp:128b B16:32b nB16:32 TriB:128b TBc:128b cm:18 Pm:128b Jm:128b IO:512b sel15:128b neg1:1b pi:1i pj:1i rcol:1 r32:1 r0m:1 r1m:1 b512:1 iW:96 j255:512b"
-_f += " rself:128 rselb:128b n1k:64b kA:16i kB:16i iM:16 slS:32i slL:32i tA:128b tB:128b tC:128b X:8208b Urep:8288 i8k:128b mC0:64b A0:8192b Ab:8192b o32:128b zb:128b half:1b j256:256b"
-_f += " nb2:8 nb3:8 wti:4i kmi:16i thi:1i wf:4 nwf:4 kf:16 Lw:144b Wp:32b BMw:128b c255:128b ui:64i U:64i sq:64i Fi:64i UF:64 UU:64 AD:256b i22:128b c8256:64b mB:128b rs16:128b cb:18b k1024:128b n1024:32b T:512i Tf:512 OT:512u KS:1024"
-_f += " KAB:64 Ki:64i kp:64i pr:64 tf:32 tc:32i cI:32i DI:32i f1:32 lim:32 fit:32b rsel:32 ST:2112b VZ:1040b Pc:64 Pd:64b Cc:128b Ck:128b Cq:128b Cs:128b wv:11 tmA:128 tmB:128"
-_f += " tsA:64 tsB:64 EQ:256 SC:256 win:4b Mk:512b Jc:8b Jf:8 cvec:4 pos:4u mC:4 t0:4 t1:4 h16:4 OFU:4u OF2:4u OFX:8u OFP:4u OFC:4u UG:128 u1A:64 u1B:64 u2A:64 u2B:64 XG:256b XP:64b"
-_f += " mP:1600b mT:1664b ts_:8 hs:8 nb:8 HH:1024b sgn:4096b LL:512b EE:128b SS:128b S1:96b dT:128b MI:32u tot:1 dg:16 cmx:18 cry:1 Gn:512b bA:1 bB:1 b2:1"
-_dt = {"b": "bfloat16", "i": "int32", "u": "uint16"}
+_f = "x0c:512b xc:512b oks:512 Rr:512 SG:2560b Yt:512 Z4:512 G0:512b idf:128 idb:128b nidb:128b BM:128b BMf:128 nBMh:128b BMgf:8 BMg4:32 tri:128b oneb:512b onef:128"
+_f += " O16:16b O16n:16b O16d:16b i65:66b rp:132b mW:128 t32:32 id2:64 rsK:1088b rs64:256b ph:1i p7:1i tE:32 Pat:1088b KM:34 KMm:34 thr:1 thS:32 c16f:128"
+_f += " Bp:256b Rp:128b Rh:128b B16:32b nB16:32 cm:18 IO:512b sel15:128b neg1:1b pi:1i pj:1i rcol:1 r32:1 r0m:1 r1m:1 r2m:1 b512:1 iW:96 j255:512b jh:512h nK:512b d512:128b"
+_f += " rself:128 rK:128 iB:128b kc:64 bM:1 rselb:128b n1k:64b kA:16i kB:16i iM:16 slS:32i slL:32i tB:128b tC:128b X:8272b Urep:8288 i8k:128b mC0:64b A0:8192b Ab:8192b o128:128b o255:128b bC:1 zb:128b"
+_f += " wti:4i kmi:16i thi:1i wf:4 nwf:4 kf:16 Lw:144b Wp:32b BMw:128b c255:128b ui:64i U:32i sq:32i GA:128 GB:128i GT:128i t2:4 dl:4 MJ:32u HA:128 HB:128i AD:256b i22:128b c8256:64b mB:128b rs16:192b cb:18b T:512i Tf:512 OT:512u KS:1024 KI:512i"
+_f += " triN:128b triP:128b nob:128b pm:32b KAB:64 tc:128i cI:32i DI:32i f1:32 lim:32 fit:32b rsel:32 ST:2112b VZ:1040b Pc:66 P1:66 Pd:64b Cc:128b Ck:128b Cq:128b Cs:128b wv:14 tmB:192"
+_f += " EQ:256 SC:256 win:4b Mk:512b Jc:8b n194:4b Jf:8 cvec:4 pos:4u mC:4 t0:4 t1:4 h16:4 OF:8u OF2:4u OFX:8u UG:128 u1B:64 u2B:64 XG:256b XP:64b"
+_f += " mP:1664b mT:1664b ts_:4 hs:4 hsm:4 nb:4b cmh:4 val:4 mk:64b ini:1 HH:1024h OH:2048h LL:512b EE:128b SS:128b S1:96b dT:128b MI:32u dg:16 cry:1 Gn:512b bA:1 bB:1"
+_dt = {"b": "bfloat16", "i": "int32", "u": "uint16", "h": "float16"}
 _pool, _where, SCRATCH = {}, {}, {}
 for _x in _f.split():
     _n, _c = _x.split(":")
@@ -43,6 +54,8 @@ for _x in _f.split():
 for _t in range(RO):
     SCRATCH["Q%d" % _t] = ("sbuf", [128, QW + 1536], "bfloat16")
     _where["Q%d" % _t] = ("Q%d" % _t, 0, QW + 1536)
+    SCRATCH["R%d" % _t] = ("sbuf", [128, 768], "bfloat16")
+    _where["R%d" % _t] = ("R%d" % _t, 0, 768)
     SCRATCH["C%d" % _t] = ("sbuf", [128, 8], "float32")
     _where["C%d" % _t] = ("C%d" % _t, 0, 8)
 for _t in range(8):
@@ -50,12 +63,15 @@ for _t in range(8):
     _where["B%d" % _t] = ("B%d" % _t, 0, 512)
 NDMA = 24
 SEMAPHORES = ["sv", "ss", "st", "sg"] + ["d%d" % _t for _t in range(NDMA)]
+SEMAPHORES += ["e%d" % _t for _t in range(16) if 4 in (PATHS[0][_t], PATHS[1][_t])]
 for _t in range(RO):
     SEMAPHORES += ["aP%d" % _t, "aT%d" % _t, "lP%d" % _t, "lT%d" % _t, "cP%d" % _t, "cT%d" % _t, "lC%d" % _t]
 
 CY, PE_CY, GA, SCA, HOP, DMA_T, REM_T, X_T = 0.88e-3, 0.45e-3, 1.56, 3.8, 0.2, 1.6, 2.0, 6.0
-MOVES, SHIFT = 500, 1.5
-PASSES, SEED, SHAKE, CASES = 90, 1, 6.0, ((1.0, 0.22), (1.15, 0.15), (1.3, 0.2))
+ADD_Q, ADD_T = 0.8, 2.8
+SLACK, EARLY, WARM = 0.3, 0.3, 0.01
+MOVES, SHIFT, SWAPS = 150, 1.5, 9000
+PASSES, SEED, SHAKE, CASES = 60, 1, 6.0, ((1.0, 0.22), (1.15, 0.15), (1.3, 0.2))
 _order = {}
 
 
@@ -168,8 +184,97 @@ def _lay_out(ops):
             key = [-x for x in start]
             at = now
             back = sorted(range(n), key=lambda i: (-(start[i] + ops[i]["busy"]), -at[i]))
-    _order["span"] = best[0]
-    return best[1]
+    issue, span = list(best[1]), best[0]
+
+    def chain(order, slow, hop):
+        free, done, why, last, ready = {}, [0.0] * n, [None] * n, {}, [0.0] * n
+        before = [None] * n
+        for i in order:
+            o, t, y = ops[i], 0.0, None
+            for (d, w) in pre[i]:
+                w = done[d] + (w if w == 0.0 else w - HOP + hop)
+                if w > t:
+                    t, y = w, d
+            ready[i] = t
+            if o["busy"] > 0:
+                before[i] = last.get(o["q"])
+                if free.get(o["q"], 0.0) > t:
+                    t, y = free[o["q"]], before[i]
+                free[o["q"]], last[o["q"]] = t + o["busy"] * slow, i
+            why[i], done[i] = y, t + o["busy"] * slow
+        end = max(done[i] + tail[i] for i in range(n))
+        late, links = [end - tail[i] for i in range(n)], []
+        for i in reversed(order):
+            t = late[i] - ops[i]["busy"] * slow
+            for (d, w) in pre[i]:
+                late[d] = min(late[d], t - (w if w == 0.0 else w - HOP + hop))
+            p = before[i]
+            if p is not None:
+                late[p] = min(late[p], t)
+            while late[i] - done[i] < SLACK and p is not None and done[p] > ready[i] + 0.03 and ops[i]["q"] != ops[p]["tag"][0] + "t":
+                links.append((p, i))
+                p = before[p]
+        return links
+
+    lane = [{"v": 0, "s": 1, "t": 2, "g": 3, "y": 4, "r": 5}[o["q"]] for o in ops]
+    busy = [o["busy"] for o in ops]
+    (s1, h1), (s2, h2) = CASES[0], CASES[-1]
+    pre2 = [[(d, w if w == 0.0 else w - HOP + h1, w if w == 0.0 else w - HOP + h2) for (d, w) in pre[i]] for i in range(n)]
+
+    def both(order):
+        f1, f2, d1, d2 = [0.0] * 6, [0.0] * 6, [0.0] * n, [0.0] * n
+        for i in order:
+            q = lane[i]
+            t, u = f1[q], f2[q]
+            for (d, w, x) in pre2[i]:
+                w += d1[d]
+                if w > t:
+                    t = w
+                x += d2[d]
+                if x > u:
+                    u = x
+            d1[i] = t = t + busy[i] * s1
+            d2[i] = u = u + busy[i] * s2
+            if q < 5:
+                f1[q], f2[q] = t, u
+        a = max(d1[i] + tail[i] for i in ends) / s1 + max(d2[i] + tail[i] for i in ends) / s2
+        return a / 2 + EARLY * (sum(d1) + sum(d2)) / n
+
+    ends = [i for i in range(n) if not succ[i]]
+
+    def ahead(order, i, p):
+        at = {x: j for j, x in enumerate(order)}
+        if at[i] < at[p]:
+            return order
+        need, todo = {i}, [i]
+        while todo:
+            for (d, w) in pre[todo.pop()]:
+                if at[d] >= at[p] and d not in need:
+                    if d == p:
+                        return order
+                    need.add(d)
+                    todo.append(d)
+        a, b = at[p], at[i] + 1
+        return order[:a] + [x for x in order[a:b] if x in need] + [x for x in order[a:b] if x not in need] + order[b:]
+
+    links, span = [], both(issue)
+    for k in range(SWAPS):
+        if not links or k % 40 == 0:
+            links = chain(issue, *CASES[k % len(CASES)])
+        p, i = links.pop(int(draw() * len(links)))
+        new = issue
+        if len(kin[ops[i]["tag"]]) == len(kin[ops[p]["tag"]]) and draw() < 0.6:
+            for (x, y) in zip(kin[ops[i]["tag"]], kin[ops[p]["tag"]]):
+                new = ahead(new, x, y)
+        else:
+            new = ahead(new, i, p)
+        if new is issue:
+            continue
+        s = both(new)
+        if s < span + WARM * draw() * (1.0 - k / SWAPS):
+            issue, span = new, s
+    _order["span"] = sum(play(issue, s, h) / s for (s, h) in CASES) / len(CASES)
+    return issue
 
 
 def rank_program(g, core, T, topo):
@@ -186,7 +291,7 @@ def rank_program(g, core, T, topo):
         k = (hi - lo - 1) // st + 1
         hi = lo + (k - 1) * st + 1
         ap = T[p][p0:p1:pst, o + lo:o + hi:st] if (pst != 1 or st != 1) else T[p][p0:p1, o + lo:o + hi]
-        return (ap, [(p, o + lo, o + hi, st, p0, p1)], k, SCRATCH[p][2], SCRATCH[p][0])
+        return (ap, [(p, o + lo, o + hi, st, p0, p1, pst)], k, SCRATCH[p][2], SCRATCH[p][0])
 
     def back(n):
         a = A(n)
@@ -197,6 +302,8 @@ def rank_program(g, core, T, topo):
 
     def hit(a, b):
         if a[1] >= b[2] or b[1] >= a[2] or a[4] >= b[5] or b[4] >= a[5]:
+            return False
+        if a[6] == b[6] and (a[4] - b[4]) % a[6]:
             return False
         return not (a[3] == b[3] and a[3] > 1 and (a[1] - b[1]) % a[3])
 
@@ -210,7 +317,7 @@ def rank_program(g, core, T, topo):
         i = len(ops)
         dep = set(after)
         o = {"q": q, "f": f, "busy": busy, "lat": lat, "dep": dep, "ord": set(after), "sem": sem or own.get(q), "inc": inc, "grp": None, "first": first}
-        tag = (q,) + tuple((r[0].rstrip("0123") if r[0][0] in "QC" else r[0],) + r[1:] for r in rg(outs)[:1] + rg(ins)[:1])
+        tag = (q,) + tuple((r[0].rstrip("0123") if r[0][0] in "QCR" else r[0],) + r[1:] for r in rg(outs)[:1] + rg(ins)[:1])
         seen[tag] = seen.get(tag, 0) + 1
         o["tag"] = tag + (seen[tag],)
         ops.append(o)
@@ -221,6 +328,10 @@ def rank_program(g, core, T, topo):
                     if b["q"] != q:
                         b["q"], b["prev"], b["run"] = q, b["run"], []
                     dep.update(b["prev"])
+                    if q != "t":
+                        L = log.setdefault(r[0], [])
+                        dep.update(j for (r2, w2, j) in L if j in b["run"] and (isw or w2) and hit(r, r2))
+                        L.append((r, isw, i))
                     if q == "t":
                         if start:
                             dep.update(b["run"])
@@ -241,17 +352,24 @@ def rank_program(g, core, T, topo):
                     if (isw or w2) and hit(r, r2):
                         dep.add(j)
                 if isw:
-                    L[:] = [e for e in L if not (e[0][1] >= r[1] and e[0][2] <= r[2] and (r[3] == 1 or e[0] == r) and e[0][4] >= r[4] and e[0][5] <= r[5])]
+                    L[:] = [e for e in L if not (e[0][1] >= r[1] and e[0][2] <= r[2] and ((r[3] == 1 and r[6] == 1) or e[0] == r) and e[0][4] >= r[4] and e[0][5] <= r[5])]
                 L.append((r, isw, i))
         dep.discard(i)
         return i
+
+    mark = {}
+
+    def behind(name, bit):
+        if HINT & bit:
+            ops[-1]["dep"].add(mark[name])
+            ops[-1]["ord"].add(mark[name])
 
     def cost(o, xs, per=None, fixed=0.05):
         xs = [x for x in xs if isinstance(x, tuple)]
         if xs[0][4] == "ix":
             return fixed + xs[0][2] * GA * CY
         if per is None:
-            per = 0.5 if o[3] in ("bfloat16", "uint16") and xs[0][3] in ("bfloat16", "uint16") else 1.0
+            per = 0.5 if all(x[3] in ("bfloat16", "uint16", "float16") for x in [o] + xs) else 1.0
         return max(64, xs[0][2] * per) * CY
 
     V, SE, PE = g.vector, g.scalar, g.tensor
@@ -272,7 +390,10 @@ def rank_program(g, core, T, topo):
             add("v", [o], [a, s1, s2], lambda s: V.tensor_scalar(ap(o), ap(a), ap(s1), ap(s2), op0, op1), cost(o, [a]))
 
     def scan(o, a, b, init, op0, op1):
-        add("v", [o], [a, b, init], lambda s: V.tensor_tensor_scan(ap(o), ap(a), ap(b), ap(init), op0, op1), cost(o, [a], 1.0))
+        add("v", [o], [a, b, init], lambda s: V.tensor_tensor_scan(ap(o), ap(a), ap(b), ap(init), op0, op1), cost(o, [a, b]))
+
+    def red(o, i, op, negate=False):
+        add("v", [o], [i], lambda s: V.tensor_reduce(ap(o), ap(i), AxisListType.X, op, negate=negate), cost(o, [i], 1.0))
 
     def ms(o, c):
         add("v", [o], [], lambda s: V.memset(ap(o), c), cost(o, [o]))
@@ -288,18 +409,29 @@ def rank_program(g, core, T, topo):
     def mm(o, l, r, start=True):
         add("t", [o], [l, r], lambda s: PE.matmul(ap(o), ap(l), ap(r), start, s), max(min(64, l[2]), r[2]) * PE_CY * (4 if l[3] == "float32" else 1), start=start)
 
-    def iota(o, pat, base, ch, small=True):
-        kw = {"allow_small_or_imprecise_dtypes": True} if small else {}
-        add("g", [o], [], lambda s: g.iota(ap(o), pat, base, ch, **kw), 0.13 + 2 * o[2] * CY, first=1000.0 if o[2] < 1000 else 0.0)
+    def iota(o, pat, base, ch):
+        kw = {} if o[3] == "int32" else {"allow_small_or_imprecise_dtypes": True}
+        add("g", [o], [], lambda s: g.iota(ap(o), pat, base, ch, **kw), 0.13 + 2 * o[2] * CY)
 
-    def sel(o, i, pat, op, base, ch):
-        add("g", [o], [i], lambda s: g.affine_select(ap(o), ap(i), pat, op, 0.0, base, ch), 0.17 + 2 * o[2] * CY, first=1000.0)
+    def fill(o, c):
+        if o[2] <= FILLV:
+            ms(o, int(c) if o[3] == "int32" else float(c))
+        else:
+            iota(o, [[0, o[2]]], int(c), 0)
+
+    def sel(o, i, pat, op, base, ch, other=0.0):
+        add("g", [o], [i], lambda s: g.affine_select(ap(o), ap(i), pat, op, other, base, ch), 0.17 + 2 * o[2] * CY)
+
+    def own_group(o, i, n, other):
+        add_ = [[0, n]] if n > 1 else []
+        sel(o, i, add_ + [[-16, 8], [0, 16]], O.is_ge, 0, 1, other)
+        sel(o, o, add_ + [[16, 8], [0, 16]], O.is_ge, 15, -1, other)
 
     nd = [0]
 
-    def dma(o, i, t=0.3, after=()):
+    def dma(o, i, t=0.3, after=(), behind=()):
         nd[0] += 1
-        return add("y", [o], [i], lambda s: g.sync.dma_start(ap(o), ap(i)), 0.05, DMA_T + t, sem="d%d" % (nd[0] - 1), inc=16, after=after)
+        return add("y", [o], [i] + list(behind), lambda s: g.sync.dma_start(ap(o), ap(i)), 0.05, DMA_T + t, sem="d%d" % (nd[0] - 1), inc=16, after=after)
 
     def hbm(x):
         return (x, [], 0, "", "dram")
@@ -327,206 +459,220 @@ def rank_program(g, core, T, topo):
     d = [dma(A("G0"), hbm(T.gd[:, :]))]
     d.append(dma(A("wti"), hbm(T.wt[:, :]), after=d[-1:]))
     d.append(dma(A("kmi"), hbm(T.km[:, :]), after=d[-1:]))
-    d.append(dma(A("x0c"), hbm(T.xs[0:128:16, :]), after=d[-1:]))
     d.append(dma(A("X", 0, 8192), hbm(T.xs[:, :]), X_T, after=d[-1:]))
-    dma(A("thi"), hbm(T.th[:, :]), X_T + 3.0, after=d[-1:])
+    d.append(dma(A("x0c"), hbm(T.xs[0:128:16, :]), X_T + 0.6, after=d[-1:]))
+    dma(A("thi"), hbm(T.th[:, :]), X_T + 0.6, after=d[-1:])
     o128 = A("oneb", 0, 128)
+    W = 512 // NZ
+    MW = 1.5 * 2.0 ** 23 * W
+    nv = 32 - NSC
 
     def consts():
         ms(A("oneb"), 1.0)
         ms(A("onef"), 1.0)
         ms(A("c255"), 255.0)
-        ms(A("X", 8192, 8208), 255.0)
+        ms(A("X", 8192, 8272), 255.0)
         ms(A("Lw"), 0.0)
-        ms(A("VZ"), 0.0)
-        sel(A("BM"), o128, [[-16, 8], [0, 16]], O.is_ge, 0, 1)
-        sel(A("BM"), A("BM"), [[16, 8], [0, 16]], O.is_ge, 15, -1)
-        iota(A("pi"), [[0, 1]], 0, 1, False)
+        ms(A("rsK"), 0.0)
+        dma(A("VZ"), A("rsK", 0, 1040))
+        own_group(A("BM"), o128, 1, 0.0)
+        iota(A("pi"), [[0, 1]], 0, 1)
         iota(A("iM"), [[64, 16]], 0, 0)
         cp(A("wf"), A("wti"))
-        ts(A("nwf"), A("wti"), -1.0, O.mult)
         cp(A("BMgf"), A("BM", 0, 128, 16))
         act(A("BMf"), A("BM"), F.Copy)
         for b in range(4):
             act(A("BMg4", 8 * b, 8 * b + 8), A("BM", 0, 128, 16), F.Copy)
         cp(A("kf"), A("kmi"))
-        ts(A("Q0", QG, QG + 512), A("G0"), -1.0, O.mult, 255.0, O.add)
+        ts(A("Q0", QG, QG + 512), A("G0"), -255.0, O.add)
         ts(A("pj"), A("pi"), 15, O.bitwise_and)
         cp(A("rcol"), A("pj"))
         ts(A("b512"), A("pj"), 512.0, O.mult)
         ts(A("r32"), A("pj"), 32.0, O.add)
         ts(A("r0m"), A("pj"), 0.0, O.is_equal)
         ts(A("r1m"), A("pj"), 1.0, O.is_equal)
-        ms(A("rsK"), 0.0)
-        for (a, b) in KB:
-            ms(A("rsK", 64 * a, 64 * b, b - a), BIG)
+        ms(A("KM"), 0.0)
+        ms(A("KMm"), 0.0)
+        for k in range(len(KB)):
+            fill(A("rsK", 64 * KO[k], 64 * KO[k + 1], KW[k]), BIG / 2)
         for n, c in (("O16", 1024.0), ("O16n", -1024.0), ("O16d", 2048.0)):
             act(A(n, 0, 16, 2), A("BMgf"), F.Copy, None, c)
             act(A(n, 1, 16, 2), A("BMgf"), F.Copy, None, c)
         ts(A("kA"), A("kmi"), 6, O.logical_shift_right)
         ts(A("kB"), A("kmi"), 63, O.bitwise_and)
-        for (a, b) in KB:
+        for j, (a, b) in enumerate(KB):
             for k, n in enumerate(("kA", "kB")):
-                c = 2 * a + k * (b - a)
+                c = 2 * KO[j] + k * KW[j]
                 ts(A("KM", c, c + b - a), A(n, a, b), A("r0m"), O.mult)
                 act(A("KMm", c, c + b - a), A("iM", a, b), F.Copy, None, A("r1m"))
         tt(A("KM"), A("KM"), A("KMm"), O.add)
-        for (a, b) in KB:
-            w, o = 2 * (b - a), 64 * a
+        for j in range(len(KB)):
+            w, o = 2 * KW[j], 64 * KO[j]
             for q in range(8):
-                act(A("Pat", o + q * w, o + q * w + w), A("KM", 2 * a, 2 * b), F.Copy, None, A("BMgf", q, q + 1))
+                act(A("Pat", o + q * w, o + q * w + w), A("KM", 2 * KO[j], 2 * KO[j + 1]), F.Copy, None, A("BMgf", q, q + 1))
             act(A("Pat", o + 8 * w, o + 16 * w), A("Pat", o, o + 8 * w), F.Copy)
             act(A("Pat", o + 16 * w, o + 32 * w), A("Pat", o, o + 16 * w), F.Copy)
         sel(A("idf"), A("onef"), [[-1, 128]], O.is_equal, 0, 1)
         act(A("idb"), A("idf"), F.Copy)
         act(A("nidb"), A("idf"), F.Copy, None, -1.0)
         act(A("i8k"), A("idf"), F.Copy, None, 8192.0)
-        if EQS:
-            act(A("i22"), A("idf"), F.Copy, None, 4194304.0)
-            ms(A("c8256"), 8256.0)
+        act(A("i22"), A("idf"), F.Copy, None, 4194304.0)
+        fill(A("c8256"), 8256)
         iota(A("j255"), [[1, 512]], -255, 0)
-        cp(A("IO", 0, 512, 1, 0, 32), A("j255", 0, 512, 1, 0, 32))
-        ms(A("IO", 0, 512, 1, 32, 64), 255.0)
-        ms(A("IO", 0, 512, 1, 64, 96), 16384.0)
-        ms(A("o32"), 1.0 / 32)
-        ms(A("zb"), 0.0)
-        ms(A("half"), 0.5)
-        sel(A("tri"), o128, [[1, 128]], O.is_ge, 0, -1)
-        sel(A("tB"), o128, [[1, 128]], O.is_gt, 0, -1)
-        tt(A("tB"), A("tB"), A("BM"), O.mult)
-        act(A("tA"), A("tB"), F.Copy, None, 2.0)
-        tt(A("TriB"), A("tA"), A("idb"), O.add)
-        iota(A("i65"), [[1, 66]], 1, 0)
-        act(A("n65"), A("i65"), F.Identity, 0.5, -1.0)
-        ts(A("cm", 0, 16), A("i65", 0, 16), -1.0, O.add)
-        ts(A("cb", 0, 16), A("cm", 0, 16), A("rcol"), O.is_le, 32768.0, O.mult)
-        ms(A("cb", 16, 17), 8192.0)
-        iota(A("slS"), [[128, 4], [0, 8]], 0, 1, False)
-        ms(A("bA"), 191.5)
-        ms(A("bB"), -256.0)
-        ms(A("neg1"), -1.0)
-        ms(A("n1k"), -1024.0)
-        act(A("SG", 2048, 2560), A("x0c"), F.Sign, A("bA"), -1.0)
-        tt(A("id2"), A("idf", 0, 64), A("idf", 64, 128), O.add)
-        tt(A("t32"), A("id2", 0, 32), A("id2", 32, 64), O.add)
-        tt(A("mW", 0, 16), A("t32", 0, 16), A("t32", 16, 32), O.add)
+        ts(A("jh", 0, W), A("j255", 0, W), 255.5 - W // 2, O.add)
+        fill(A("nK"), -KK)
+        act(A("bC"), A("b512"), F.Identity, 16384.0)
+        act(A("d512"), A("idf"), F.Copy, None, A("bC"))
+        act(A("iB"), A("idf"), F.Copy, None, -2.0 ** 28)
+        ts(A("bM"), A("b512"), -1.0, O.mult, 0.5, O.add)
+        ts(A("ini"), A("b512"), -KK, O.mult, 1.5 * KK - 2.0 ** 28, O.add)
+        act(A("kc"), A("onef", 0, 64), F.Copy, None, A("ini"))
+        iota(A("HA", 0, 128, 2), [[0, 32], [1, 2]], 0, 0)
+        fill(A("HA", 1, 128, 4), 64)
+        fill(A("HB", 1, 128, 4), 0)
+        ms(A("GA", 0, 128, 4), 0.0)
+        ms(A("GA", 2, 128, 4), 1.0 / 32)
+        ms(A("GA", 3, 128, 4), 1.0)
+        ms(A("GB", 1, 128, 4), -12)
+        ms(A("GB", 2, 128, 4), int(M1))
+        act(A("o128"), o128, F.Copy, None, 1.0 / 128)
+        act(A("o255"), o128, F.Copy, None, 255.0 / 128)
+        fill(A("zb"), 0)
+        sel(A("triP"), o128, [[1, 128]], O.is_gt, 0, -1)
+        sel(A("triP"), A("triP"), [[1, 128]], O.not_equal, 0, -1, -127.0)
+        act(A("triN"), A("triP"), F.Copy, None, -1.0)
+        fill(A("nob"), -1)
+        fill(A("pm", 0, nv), 128)
+        fill(A("pm", nv, 32), -128)
+        sel(A("tB"), A("BM"), [[1, 128]], O.is_gt, 0, -1)
+        iota(A("i65"), [[1, 66]], 0, 0)
+        act(A("rp", 0, 66), A("i65"), F.Identity, 0.5)
+        ts(A("cb", 0, 16), A("i65", 0, 16), A("rcol"), O.is_le, 32768.0, O.mult)
+        fill(A("cb", 16, 17), 8192)
+        fill(A("neg1"), -1)
+        fill(A("n1k"), 1024)
+        act(A("SG", 2048, 2560), A("x0c"), F.Sign, 191.5, -1.0)
+        ts(A("mW", 0, 16), A("i65", 0, 16), A("rcol"), O.is_equal)
         act(A("mB", 0, 16), A("mW", 0, 16), F.Identity, BIG / 2, -BIG / 2)
         for k in (16, 32):
             act(A("mB", k, 2 * k), A("mB", 0, k), F.Copy)
         act(A("mB", 64, 128), A("mB", 0, 64), F.Copy)
         ts(A("mC0"), A("mB", 0, 64), 8256.0, O.max)
-        ms(A("c16f"), 0.0625)
-        ms(A("rs16"), -BIG)
-        ms(A("rs16", 0, 128, 16), BIG)
-        if RSEL:
-            act(A("k1024"), A("idf"), F.Copy, None, 1024.0)
-            ms(A("n1024"), -1024.0)
-        ms(A("rs64"), -BIG)
-        ms(A("rs64", 0, 256, 64), BIG)
-        act(A("rself"), A("BM"), F.Copy, None, A("r0m"))
+        act(A("c16f"), o128, F.Copy, None, 0.0625)
+        fill(A("rs16"), -BIG / 2)
+        fill(A("rs16", 0, 192, 16), BIG / 2)
+        fill(A("rs64"), -BIG / 2)
+        fill(A("rs64", 0, 256, 64), BIG / 2)
+        wv = [A("wv", k, k + 1) for k in range(14)]
+        ts(A("r2m"), A("pj"), 2.0, O.is_equal, A("r0m"), O.add)
+        tt(A("r2m"), A("r2m"), A("r1m"), O.subtract)
+        act(A("rself"), A("BM"), F.Copy, None, A("r2m"))
+        act(A("rK"), A("rself"), F.Copy, None, KK)
         act(A("rselb"), A("BM"), F.Copy, None, A("r0m"))
-        wv = [A("wv", k, k + 1) for k in range(11)]
         ts(wv[10], A("pj"), 15.0, O.is_equal, 0.5, O.mult)
         act(A("sel15"), A("BM"), F.Copy, None, wv[10])
         act(A("nBMh"), A("BM"), F.Copy, None, -0.5)
-        act(A("tC"), A("BM"), F.Identity, -4096.0, 4096.0)
-        iota(A("Bp"), [[0, 8], [512, 16]], 0, 0)
-        tt(A("Bp"), A("Bp"), A("BM"), O.mult)
-        tt(A("Bp"), A("Bp"), A("tC"), O.add)
+        iota(A("Bp", 0, 128 * NZ), [[W, NZ], [0, 8], [512, 16]], W, 0)
+        own_group(A("Bp", 0, 128 * NZ), A("Bp", 0, 128 * NZ), NZ, -4096.0)
         iota(A("Rp"), [[0, 8], [1, 16]], -8, 0)
-        tt(A("Rp"), A("Rp"), A("BM"), O.mult)
-        tt(A("Rp"), A("Rp"), A("tC"), O.add)
+        own_group(A("Rp"), A("Rp"), 1, -4096.0)
+        if LLS:
+            act(A("Rh"), A("Rp"), F.Identity, 0.5)
         iota(A("B16"), [[16, 32]], 0, 0)
         act(A("nB16"), A("B16"), F.Identity, 0.5, -1.0)
         iota(A("iW"), [[-64, 3], [16, 32]], -64, 0)
         ts(A("iW"), A("iW"), A("rcol"), O.add)
-        ts(A("slL"), A("slS"), 63, O.bitwise_and)
-        cp(A("VZ", 21, 1040, 32), A("slL"))
-        tt(A("VZ", 20, 1040, 32), A("slS"), A("slL"), O.subtract)
-        ms(A("VZ", 22, 1040, 32), 1.0)
-        ms(A("VZ", 23, 1040, 32), 1.0)
+        iota(A("VZ", 20, 1040, 32), [[128, 4], [0, 8]], 0, 0)
+        iota(A("VZ", 21, 1040, 32), [[0, 32]], 0, 1)
+        fill(A("VZ", 22, 1040, 32), 1)
+        fill(A("VZ", 23, 1040, 32), 1)
         ts(A("ph"), A("pj"), 1, O.logical_shift_right)
-        ts(wv[0], A("ph"), 0.0, O.is_equal, 0.5, O.mult)
-        ts(wv[1], A("ph"), 1.0, O.is_equal, 256.0, O.mult)
-        ts(wv[2], A("ph"), 2.0, O.is_equal, 0.5, O.mult)
-        ts(wv[3], A("pj"), 6.0, O.is_equal)
-        ts(wv[4], A("pj"), 7.0, O.is_equal, -0.25, O.mult)
-        ts(wv[5], wv[3], -4128.0, O.mult, wv[0], O.add)
-        ts(wv[6], wv[3], 92.0, O.mult, wv[2], O.add)
-        ts(wv[7], wv[3], -2097152.0, O.mult, wv[2], O.add)
-        ts(wv[8], wv[7], wv[1], O.add)
-        ts(wv[9], wv[7], wv[1], O.add, wv[4], O.add)
+        for (k, n, c) in ((0, "ph", 0.0), (1, "ph", 1.0), (2, "ph", 2.0), (3, "pj", 6.0), (4, "pj", 7.0)):
+            ts(wv[k], A(n), c, O.is_equal, 0.5, O.mult)
+        for (k, a, c, b) in ((5, 3, -8256.0, 0), (6, 3, -10.0, 2), (7, 3, -4194304.0, 2), (8, 1, 512.0, 7), (9, 4, -0.5, 8)):
+            act(wv[k], wv[a], F.Identity, wv[b], c)
         for n, k in (("Cc", 5), ("Cs", 6), ("Cq", 8), ("Ck", 9)):
             act(A(n), A("BM"), F.Copy, None, wv[k])
+        fill(A("n194"), -2 if TWO else -194)
         ts(A("Jf", 4, 8), A("B16", 0, 4), A("rcol"), O.add, 128.0, O.add)
-        ts(A("Jf", 0, 4), A("Jf", 4, 8), 8.0, O.mult)
-        cp(A("Jc", 0, 4), A("Jf", 0, 4))
-        ms(A("Jc", 4, 5), -64.0)
+        act(A("Jf", 0, 4), A("Jf", 4, 8), F.Copy, None, 8.0)
+        act(A("Jc", 0, 4), A("Jf", 4, 8), F.Copy, None, 8.0)
+        fill(A("Jc", 4, 5), -64)
         for k in range(4):
             act(A("Mk", 128 * k, 128 * k + 128), A("nidb"), F.Copy, None, A("Jf", k, k + 1))
-        ms(A("cvec", 3, 4), 0.0)
-        ms(A("cvec", 0, 1), 1.0)
-        ms(A("cvec", 1, 2), -1.0)
-        ms(A("cvec", 2, 3), 2.0)
-        ms(A("mP", 0, 64), 0.0)
-        ms(A("mT", 0, 128), 0.0)
+        iota(A("cvec", 0, 2), [[-2, 2]], 1, 0)
+        iota(A("cvec", 2, 4), [[-2, 2]], 2, 0)
+        fill(A("mP", 0, 128), 0)
+        fill(A("mT", 0, 128), 0)
         for t in range(RO):
-            ms(A("Q%d" % t, QG + 512, QW), 0.0)
+            fill(A("Q%d" % t, QG + 512, QW), 0)
         cp(A("thr"), A("thi"))
         ts(A("tE"), A("BMg4"), A("thr"), O.mult)
         mm(A("B5", 0, 32), A("c16f"), A("tE"))
         cp(A("thS"), A("B5", 0, 32))
-        ms(A("Urep", 8192, 8288), 8192.0)
-        for k in range(8):
-            iota(A("Urep", 1024 * k, 1024 * k + 1024), [[0, 1024]], 0, 0)
+        fill(A("Urep", 8192, 8288), 8192)
+        fill(A("Urep", 8192, 8194), 0)
+        for k in range(16):
+            u = A("Urep", 512 * k, 512 * k + 512)
+            if k < UG_:
+                fill(u, 0)
+            elif k < UG_ + UV_:
+                ms(u, 0.0)
+        if UG_ + UV_ < 16:
+            c = 512 * (UG_ + UV_)
+            dma(A("Urep", c, 8192), A("Urep", 0, 8192 - c), X_T * 1.5 * (8192 - c) / 4096, behind=[A("thi")])
 
     def weights(t):
-        w, nw = A("wf", t, t + 1), A("nwf", t, t + 1)
-        act(A("Lw", 15, 143, 16), A("BMgf"), F.Copy, None, nw)
+        w = A("wf", t, t + 1)
+        act(A("Lw", 15, 143, 16), A("BMgf"), F.Copy, None, w)
         act(A("Wp"), A("BMg4"), F.Copy, None, w)
         act(A("BMw"), A("BM"), F.Copy, None, w)
 
     def lists(t):
         Q = "Q%d" % t
         mm(A("B4", 0, 32), A("BMw"), A("c255", 0, 32), True)
-        bs = "B1" if USPLIT else "B4"
-        mm(A(bs, 32, 64), A("c255"), A("Wp"), USPLIT == 1)
+        mm(A("B1", 32, 64), A("c255"), A("Wp"), True)
         for r in range(16):
             mm(A("B4", 0, 32), A("Lw", 15 - r, 143 - r), A(Q, QG + r, QG + 512, 16), False)
         for b in range(4):
-            mm(A(bs, 32 + 8 * b, 40 + 8 * b), A(Q, QG + 128 * b, QG + 128 * b + 128), A("Lw", 15, 143, 16), False)
-        for (a, b, n) in ((0, 32, "B4"), (32, 64, bs)) if USPLIT else ((0, 64, "B4"),):
-            cp(A("ui", a, b), A(n, a, b))
-            ts(A("U", a, b), A("ui", a, b), 4095, O.bitwise_and)
-            cp(A("UF", a, b), A("U", a, b))
-        tt(A("sq", 0, 32), A("U", 0, 32), A("U", 0, 32), O.mult)
-        ts(A("Fi", 0, 32), A("sq", 0, 32), 5, O.logical_shift_right)
-        tt(A("sq", 32, 64), A("U", 32, 64), A("U", 32, 64), O.mult)
-        ts(A("Fi", 32, 64), A("sq", 32, 64), 5, O.logical_shift_right)
+            mm(A("B1", 32 + 8 * b, 40 + 8 * b), A(Q, QG + 128 * b, QG + 128 * b + 128), A("Lw", 15, 143, 16), False)
+        u, uf = A("GB", 0, 128, 4), A("GA", 1, 128, 4)
+        cp(A("ui", 0, 32), A("B4", 0, 32))
+        ts(u, A("ui", 0, 32), 4095, O.bitwise_and)
+        cp(uf, u)
+        ts(A("GB", 3, 128, 4), u, A("kf", 0, 1), O.mult, -M1, O.add)
+        scan(A("GT"), A("GA"), A("GB"), 0.0, O.mult, O.add)
         for j, (a, b) in enumerate(LCUT):
-            for m in range(a, b):
+            for m in range(max(a, 1), b):
                 ku = A("Tf", 32 * m, 32 * m + 32)
                 if m in VMUL:
-                    ts(ku, A("U", 0, 32), A("kf", m, m + 1), O.mult)
+                    ts(ku, u, A("kf", m, m + 1), O.mult, -M1, O.add)
                 else:
-                    act(ku, A("UF", 0, 32), F.Copy, None, A("kf", m, m + 1))
-                tt(A("T", 32 * m, 32 * m + 32), ku, A("Fi", 0, 32), O.add)
-            ts(A("T", 32 * a, 32 * b), A("T", 32 * a, 32 * b), 8191, O.bitwise_and)
+                    act(ku, uf, F.Identity, -M1, A("kf", m, m + 1))
+                tt(A("T", 32 * m, 32 * m + 32), ku, A("GT", 2, 128, 4), O.add)
+            ts(A("T", 32 * a, 32 * b), A("T", 32 * a, 32 * b) if a else A("GT", 3, 128, 4), 8191, O.bitwise_and)
             cp(A("OT", 32 * a, 32 * b), A("T", 32 * a, 32 * b))
             ops[-1]["lat"] = LURGE[j]
-        act(A("UU", 0, 64, 2), A("UF", 32, 64), F.Copy, None, 64.0)
-        act(A("UU", 1, 64, 2), A("UF", 32, 64), F.Copy)
+        cp(A("ui", 32, 64), A("B1", 32, 64))
+        ts(A("U"), A("ui", 32, 64), 4095, O.bitwise_and)
+        cp(A("HA", 3, 128, 4), A("U"))
+        tt(A("sq"), A("U"), A("U"), O.mult)
+        ts(A("HB", 3, 128, 4), A("sq"), 5, O.logical_shift_right)
 
     def gathers(t):
-        Q, n3 = "Q%d" % t, 0
-        for k, (a, b) in enumerate(KB):
-            mm(A("B%d" % k, 0, 64 * (b - a)), o128, A("Pat", 64 * a, 64 * b), True)
+        Q, n3, last = "Q%d" % t, 0, len(KB) - 1
+        PATH = PATHS[min(t, 1)]
+        for k in range(len(KB)):
+            mm(A("B%d" % k, 0, 64 * KW[k]), o128, A("Pat", 64 * KO[k], 64 * KO[k + 1]), True)
         for m in range(16):
             k = [i for i, (a, b) in enumerate(KB) if a <= m < b][0]
             a, b = KB[k]
             cuts = ((0, 256), (256, 512)) if m in HALVED else ((0, 512),)
             for (lo, hi) in cuts:
                 o = 512 * m
+                PATH = list(PATHS[min(t, 1)])
+                if lo and m in TURN:
+                    PATH[m] = 4 - PATH[m]
                 src, h = IX(A("X"), A("OT", 32 * m + lo // 16, 32 * m + hi // 16)), A(Q, QG + lo, QG + hi)
                 a0, ab = A("A0", o + lo, o + hi), A("Ab", o + lo, o + hi)
                 if PATH[m] == 3:
@@ -536,123 +682,147 @@ def rank_program(g, core, T, topo):
                         act(A("A0", o, o + 1024), IX(A("X"), A("OT", 32 * m, 32 * m + 64)), F.Copy)
                     elif m - 1 not in PAIR:
                         act(x, src, F.Copy)
-                    mm(bank, A("nidb"), h, True)
+                    mm(bank, A("idb"), h, True)
                     mm(bank, A("idb"), x, False)
                     act(ab, bank, F.Abs)
                 else:
-                    tt(a0, src, h, O.subtract)
+                    if PATH[m] == 4:
+                        act(a0, src, F.Copy)
+                        add("g", [a0], [a0, h], lambda s, a0=a0, h=h: g.dma_start(ap(a0), ap(h), accum_op=O.add), ADD_Q, ADD_T, sem="e%d" % m, inc=16)
+                    else:
+                        tt(a0, src, h, O.add)
                     if PATH[m] == 2:
                         act(ab, a0, F.Abs)
                     else:
                         ts(ab, a0, 0.0, O.max)
                 for c in range(lo // 128, hi // 128):
-                    w = b - a
+                    w = KW[k]
                     out = A("B%d" % k, c * 16 * w + m - a, (c + 1) * 16 * w, w)
-                    if PATH[m] == 1:
+                    if PATH[m] in (1, 4):
                         mm(out, A("A0", o + 128 * c, o + 128 * c + 128), A("O16n"), False)
                     mm(out, A("Ab", o + 128 * c, o + 128 * c + 128), A("O16" if PATH[m] in (2, 3) else "O16d"), False)
             if m == b - 1:
-                scan(A("KS", 64 * a, 64 * b), A("rsK", 64 * a, 64 * b), A("B%d" % k, 0, 64 * (b - a)), 0.0, O.max, O.min)
-        low = [A("KS", 64 * a + b - a - 1, 64 * b, b - a) for (a, b) in KB]
-        if len(low) == 3:
-            tt(A("KAB"), low[0], low[1], O.min)
-        tt(A("Ki"), A("KAB") if len(low) == 3 else low[0], low[-1], O.min)
+                lo, hi, w = 64 * KO[k], 64 * KO[k + 1], KW[k]
+                if k == last:
+                    low = [A("KS", 64 * KO[j] + KW[j] - 1, 64 * KO[j + 1], KW[j]) for j in range(last)]
+                    if last == 2:
+                        tt(A("KAB"), low[0], low[1], O.min)
+                    mm(A("B%d" % k, w - 1, 64 * w, w), A("idf"), A("KAB") if last == 2 else low[0], False)
+                scan(A("KI", 0, hi - lo) if k == last else A("KS", lo, hi), A("rsK", lo, hi), A("B%d" % k, 0, hi - lo), 0.0, O.max, O.min)
 
     def utable(t):
         k = (t - 1) % 5 if t else 4
-        mm(A("B7"), A("o32", 0, 128, 1, 0, 96), A("IO", 0, 512, 1, 0, 96), True)
+        mm(A("B7"), A("o128"), A("j255"), True)
+        mm(A("B7"), A("o255"), A("oneb"), False)
+        mm(A("B7"), A("d512"), A("oneb"), False)
         mm(A("B7"), A("i8k"), A("SG", 2048, 2560), False)
         mm(A("B7"), A("i8k"), A("SG", 512 * k, 512 * k + 512), False)
         scan(back("oks"), back("B7"), A("oneb"), 32768.0, O.min, O.mult)
-        act(A("tot"), A("oks", 0, 1), F.Identity, A("b512"))
-        act(A("dg"), A("mW", 0, 16), F.Copy, None, A("tot"))
+        dma(A("Urep", 2, 8194, 1, 0, 128, 16), A("oks"), 0.6)
+        act(A("dg"), A("mW", 0, 16), F.Copy, None, A("oks", 0, 1))
         mm(A("B6", 0, 17), A("idb"), A("cb", 0, 17), True)
         mm(A("B6", 0, 16), A("BMf"), A("dg"), False)
         mm(A("B6", 16, 17), A("sel15"), A("neg1"), False)
         mm(A("B6", 16, 17), A("sel15"), A("SG", t * 512 - 1, t * 512) if t else A("neg1"), False)
-        add("v", [A("cry")], [A("B6", 0, 17)], lambda s: V.tensor_reduce(A("cry")[0], A("B6", 0, 17)[0], AxisListType.X, O.min), 64 * CY)
-        ts(A("Ut"), A("oks"), A("b512"), O.add, A("cry"), O.min)
-        dma(A("Urep", 0, 8192, 1, 0, 128, 16), A("Ut"), 0.6)
+        red(A("cry"), A("B6", 0, 17), O.min, True)
+        act(A("Rr"), A("oks"), F.Relu, A("cry"))
+        dma(A("Urep", 2, 8194, 1, 1, 128, 16), A("Rr"), 0.6)
 
     def choose():
-        ts(A("kp"), A("Ki"), 63, O.bitwise_and)
-        ts(A("DI"), A("Ki", 0, 64, 2), 10, O.logical_shift_right)
-        tt(A("pr"), A("kp"), A("UU"), O.mult)
+        w = KW[-1]
+        ts(A("HB", 0, 128, 2), A("KI", w - 1, 64 * w, w), 63, O.bitwise_and)
+        ts(A("DI"), A("KI", w - 1, 64 * w, 2 * w), 10, O.logical_shift_right)
+        scan(A("tc"), A("HA"), A("HB"), 0.0, O.mult, O.add)
         tt(A("f1"), A("DI"), A("thS"), O.is_lt)
-        tt(A("tf"), A("pr", 0, 64, 2), A("pr", 1, 64, 2), O.add)
         ts(A("lim"), A("f1"), 8096.0, O.mult)
-        tt(A("tc"), A("tf"), A("Fi", 32, 64), O.add)
-        ts(A("cI"), A("tc"), 8191, O.bitwise_and)
+        ts(A("cI"), A("tc", 3, 128, 4), 8191, O.bitwise_and)
         tt(A("fit"), A("cI"), A("lim"), O.is_lt)
-        for bank in ("B3", "B1")[:1 + RSEL]:
-            if RSEL:
-                mm(A(bank, 0, 32), A("idb"), A("n1024"), True)
-                mm(A(bank, 0, 32), A("k1024"), A("fit"), False)
-            mm(A(bank, 0, 32), A("tri"), A("fit"), not RSEL)
-            mm(A(bank, 8, 32), o128, A("fit", 0, 24), False)
-            mm(A(bank, 16, 32), o128, A("fit", 0, 16), False)
-            mm(A(bank, 24, 32), o128, A("fit", 0, 8), False)
+        for (bank, a, b, tri, one) in (("B3", 0, nv, "triP", o128), ("B1", nv, 32, "triN", A("nob"))):
+            mm(A(bank, a, b), A("idb"), A("pm", a, b), True)
+            mm(A(bank, a, b), A(tri), A("fit", a, b), False)
+            for s in (8, 16, 24):
+                if max(a, s) < b:
+                    mm(A(bank, max(a, s), b), one, A("fit", max(a, s) - s, b - s), False)
         for v, n in ((16, "cI"), (18, "DI")):
             cp(A("VZ", v, 1040, 32), A(n))
             tt(A("VZ", v + 1, 1040, 32), A(n), A("VZ", v, 1040, 32), O.subtract)
-        if RSEL:
-            act(A("rsel"), A("B1", 0, 32), F.Copy)
-        else:
-            tt(A("rsel"), A("B3", 0, 32), A("fit"), O.mult)
+        act(A("rsel", nv, 32), A("B1", nv, 32), F.Copy)
         mm(A("B4", 0, 65), A("zb"), A("i65", 0, 65), True)
         for c in range(32):
             st = A("ST", c * 66, c * 66 + 65)
-            if c in SSEL:
-                act(st, A("n65", 0, 65), F.Sign, A("rsel", c, c + 1))
+            if c < nv:
+                ts(st, A("i65", 0, 65), A("B3", c, c + 1), O.is_ge, 2.0, O.mult)
             else:
-                ts(st, A("i65", 0, 65), A("B3" if RSEL else "rsel", c, c + 1), O.is_le, 2.0, O.mult)
+                act(st, A("rp", 0, 65), F.Sign, A("rsel", c, c + 1))
             w, p = 16 + 32 * c - 16 * (c % 2), 32 * (c % 8 // 2)
             mm(A("B4", 0, 65, 1, p, p + 32), A("VZ", w, w + 32), st, False)
-        cp(A("Pc"), A("B4", 1, 65))
-        tt(A("Pd"), A("B4", 0, 64), A("Pc"), O.subtract)
+        cp(A("Pc", 0, 64), A("B4", 0, 64))
+        tt(A("Pd"), A("B4", 1, 65), A("Pc", 0, 64), O.subtract)
         mm(A("B0", 0, 64), A("idb"), A("mC0"), True)
-        mm(A("B0", 64, 128), A("idb"), A("mB", 0, 64), False)
+        mm(A("B0", 64, 192), A("idb"), A("mB"), False)
         mm(A("B0", 0, 64), A("Cc"), A("Pd"), False)
-        mm(A("B0", 64, 128), A("Ck"), A("Pd"), False)
-        mm(A("B3", 384, 448), A("idb"), A("mB", 0, 64), True)
-        mm(A("B3", 64, 128), A("Cc"), A("Pd"), False)
+        mm(A("B0", 64, 128), A("Cs"), A("Pd"), False)
+        mm(A("B0", 128, 192), A("Ck"), A("Pd"), False)
+        if EQS < 4:
+            mm(A("B3", 64, 128), A("Cc"), A("Pd"), True)
         for k in range(4 - EQS):
             mm(A("B3", 128 + 64 * k, 192 + 64 * k), A("Cq"), A("Pd"), False)
-        mm(A("B3", 384, 448), A("Cs"), A("Pd"), False)
 
     def wrap(b, src):
         n = src[2]
         scan(A(b, 0, n), A("rs16", 0, n), src, 0.0, O.max, O.min)
         return A(b, 15, n, 16)
 
-    def marks(k, c):
-        ts(A("hs", k, k + 4), A("ts_", k, k + 4), M512, O.add, M512, O.subtract)
-        if [i for i in range(k, k + 4) if i not in VSTEP]:
-            tt(A("nb", k, k + 4), A("hs", k, k + 4), A("ts_", k, k + 4), O.subtract)
-        if [i for i in range(k, k + 4) if i in VSTEP]:
-            tt(A("nb2", k, k + 4), A("ts_", k, k + 4), A("hs", k, k + 4), O.subtract)
-        for i in range(k, k + 4):
-            hh = A("HH", 128 * i, 128 * i + 128)
-            if i in VSTEP:
-                ts(A("sgn", 512 * i, 512 * i + 512), A("j255"), A("nb2", i, i + 1), O.is_gt, 0.5, O.subtract)
-            else:
-                act(A("sgn", 512 * i, 512 * i + 512), A("j255"), F.Sign, A("nb", i, i + 1))
-            ts(hh, A("Bp"), A("hs", i, i + 1), O.is_equal, 2 * c if i in VSTEP else c, O.mult)
-            mm(A("B5"), hh, A("sgn", 512 * i, 512 * i + 512), i == 0)
+    def consume(t, cW, r2):
+        act(A("ts_"), cW, F.Identity, W // 2 + 0.5)
+        act(A("cmh"), cW, F.Identity, -0.5)
+        ts(A("hs"), A("ts_"), MW, O.add, MW, O.subtract)
+        tt(A("nb"), A("ts_"), A("hs"), O.subtract)
+        tt(A("hsm"), A("hs"), A("win"), O.mult)
+        first = [(A("idb"), A("x0c"))] if t < RO - 1 else []
+        if t:
+            first += [(A("i8k"), A("oneb")), (A("i8k"), A("SG", t * 512 - 512, t * 512))]
+        for i, (l, r) in enumerate(first):
+            mm(A("B5"), l, r, i == 0)
+        mm(A("B6", 64, 128), A("idf"), A("kc"), True)
+        mm(A("B6", 64, 128), A("iB"), A("mk"), False)
+        mm(A("B6", 64, 128), A("rK"), A("UG", 64, 128), False)
+        red(A("ini"), A("B6", 64, 128), O.max)
+        tt(A("val"), r2, A("cmh"), O.subtract)
+        for i in range(4):
+            oh, o = A("OH", W * i, W * i + W), 128 * NZ * i
+            ts(oh, A("jh", 0, W), A("nb", i, i + 1), O.is_equal, KK, O.mult)
+            ts(A("HH", o, o + 128 * NZ), A("Bp", 0, 128 * NZ), A("hsm", i, i + 1), O.is_equal, A("val", i, i + 1), O.mult)
+            mark["HH"] = len(ops) - 1
+            for z in range(NZ):
+                mm(A("B5", W * z, W * z + W), A("HH", o + 128 * z, o + 128 * z + 128), oh, False)
+        if t < RO - 1:
+            scan(A("xc"), A("nK"), A("B5"), A("ini"), O.add, O.max)
+            mark["xc"] = len(ops) - 1
+            dma(A("X", 0, 8192, 1, 0, 128, 16), A("xc"), XLAT)
+            act(A("SG", t * 512, t * 512 + 512), A("xc"), F.Sign, -256.0)
+        else:
+            scan(A("B0"), A("nK"), A("B5"), A("ini"), O.add, O.max)
+            tt(A("Yt"), A("Z4"), A("B0"), O.min)
+            dma(hbm(T.yc[:, :]), A("Yt"), 0.6)
 
     def give(t):
         Q, C = "Q%d" % t, "C%d" % t
-        wrap("tmB", A("B0", 0, 128))
-        cW = A("tmB", 15, 64, 16)
+        if WSPLIT:
+            scan(A("tmB", 0, WSPLIT), A("rs16", 0, WSPLIT), A("B0", 0, WSPLIT), 0.0, O.max, O.min)
+        scan(A("tmB", WSPLIT, 192), A("rs16", WSPLIT, 192), A("B0", WSPLIT, 192), 0.0, O.max, O.min)
+        cW, sW = A("tmB", 15, 64, 16), A("tmB", 79, 128, 16)
+        ts(A("OF"), A("tmB", 15, 128, 16), 10.0, O.add)
         n = 256 - 64 * EQS
         for k in range(4 - EQS):
             ts(A("EQ", 64 * k, 64 * k + 64), A("B3", 64, 128), 8256.0, O.add, A("tmB", 15 + 16 * k, 16 + 16 * k), O.is_equal)
-        tt(A("EQ", 0, n), A("EQ", 0, n), A("B3", 128, 128 + n), O.mult)
-        sW = wrap("tsB", A("B3", 384, 448))
-        scan(A("SC", 0, n), A("rs64", 0, n), A("EQ", 0, n), 0.0, O.max, O.min)
+        if n:
+            tt(A("EQ", 0, n), A("EQ", 0, n), A("B3", 128, 128 + n), O.mult)
+            scan(A("SC", 0, n), A("rs64", 0, n), A("EQ", 0, n), 0.0, O.max, O.min)
+        mm(A("B1", 0, 64), A("idb"), A("c8256"), True)
+        mm(A("B1", 0, 64), A("Cc"), A("Pd"), False)
+        act(A("mk"), A("B1", 0, 64), F.Sign, A("bM"))
         if EQS:
-            mm(A("B1", 0, 64), A("idb"), A("c8256"), True)
-            mm(A("B1", 0, 64), A("Cc"), A("Pd"), False)
             for k in range(EQS):
                 mm(A("B2", 64 * k, 64 * k + 64), A("Cq"), A("Pd"), k == 0)
             for k in range(EQS):
@@ -660,8 +830,9 @@ def rank_program(g, core, T, topo):
                 act(A("AD", 64 * k, 64 * k + 64), A("B1", 0, 64), F.Abs, A("tmB", c, c + 1), -1.0)
                 mm(A("B2", 64 * k, 64 * k + 64), A("i22"), A("AD", 64 * k, 64 * k + 64), False)
             scan(A("SC", n, 256), A("rs64", n, 256), A("B2", 0, 256 - n), 0.0, O.max, O.min)
-        tt(A("win"), A("SC", 63, 256, 64), A("tmB", 79, 128, 16), O.is_gt)
+        tt(A("win"), A("SC", 63, 256, 64), A("tmB", 143, 192, 16), O.is_gt)
         mm(A("B1", 0, 4), A("idb"), A("Jc", 0, 4), True)
+        mm(A("B1", 0, 4), A("idb"), A("n194"), False)
         mm(A("B1", 0, 4), A("tB"), A("win"), False)
         mm(A("B4", 0, 1), A("idb"), A("Jc", 4, 5), True)
         for k in range(4):
@@ -671,82 +842,96 @@ def rank_program(g, core, T, topo):
             mm(A("B4", 0, 1), A("BM"), A("win", k, k + 1), False)
         ts(A("mC"), A("cvec"), A("B4", 0, 1), O.mult)
         remote("lC%d" % t, [(rank ^ 1, eP, A("mC"), A(C, 0, 4), "cP%d" % t), (rank ^ 4, eT, A("mC"), A(C, 4, 8), "cT%d" % t)])
-        cp(A("pos"), A("B1", 0, 4))
+        ts(A("pos"), A("B1", 0, 4), 2.0 if TWO else 194.0, O.add)
         tt(A("t0"), sW, A("B1", 0, 4), O.subtract)
-        ts(A("OFU"), cW, 16.0, O.add)
-        act(A("UG", 0, 64), IX(A("Urep"), A("OFU")), F.Copy)
+        act(A("UG", 0, 64), IX(A("Urep", 8), A("OF", 0, 4)), F.Copy)
         mm(A("B6", 0, 64), A("idb"), A("mB", 0, 64), True)
         mm(A("B6", 0, 64), A("rself"), A("UG", 0, 64), False)
         r1 = wrap("u1B", A("B6", 0, 64))
-        ts(A("OF2"), r1, 8.0, O.add, 8191.0, O.min)
+        ts(A("OF2"), r1, 10.0, O.add, 8193.0, O.min)
         act(A("UG", 64, 128), IX(A("Urep"), A("OF2")), F.Copy)
         mm(A("B7", 0, 64), A("idb"), A("mB", 0, 64), True)
         mm(A("B7", 0, 64), A("rself"), A("UG", 64, 128), False)
         r2 = wrap("u2B", A("B7", 0, 64))
         cp(A("OFX", 0, 4), r1)
         cp(A("OFX", 4, 8), r2)
-        act(A("XG", 64, 128), IX(A("X"), A("OFX", 0, 4)), F.Copy)
-        act(A("XG", 128, 192), IX(A("X"), A("OFX", 4, 8)), F.Copy)
-        ts(A("OFP"), cW, 10.0, O.add, 8192.0, O.min)
-        act(A("XG", 0, 64), IX(A("X"), A("OFP")), F.Copy)
+        act(A("XG", 64, 128), IX(A("X"), A("OFX", 0, 4)), F.Copy, None, -1.0)
+        act(A("XG", 128, 192), IX(A("X"), A("OFX", 4, 8)), F.Copy, None, -1.0)
+        act(A("XG", 0, 64), IX(A("X"), A("OF", 0, 4)), F.Copy, None, -1.0)
         mm(A("B2", 0, 64), A("idb"), A("n1k"), True)
         mm(A("B2", 0, 64), A("rselb"), A("XG", 0, 64), False)
-        tt(A("XP"), A("XG", 0, 64), A("B2", 0, 64), O.max)
-        ts(A("OFC"), sW, -184.0, O.add, 0.0, O.max)
-        act(A("XG", 192, 256), IX(A(Q, QG, QG + 512), A("OFC")), F.Copy)
-        ts(A("XP"), A("XP"), 255.0, O.min)
+        tt(A("XP"), A("XG", 0, 64), A("B2", 0, 64), O.min)
+        act(A("XG", 192, 256), IX(A(Q, QG, QG + 512), A("OF", 4, 8)), F.Copy)
+        ts(A("XP"), A("XP"), -255.0, O.max)
         sct(A("mT", 0, 1600), A("pos"), A("XG", 64, 128))
         sct(A("mT", 64, 1664), A("pos"), A("XG", 128, 192))
-        remote("lT%d" % t, [(rank ^ 4, eT, A("mT", 0, 128), A(Q, 64, 192), "aT%d" % t)])
-        sct(A("mP"), A("pos"), A("XP"))
-        remote("lP%d" % t, [(rank ^ 1, eP, A("mP", 0, 64), A(Q, 0, 64), "aP%d" % t)])
-        sct(A(Q, QG + 512, QG + 512 + 1600), A("pos"), A("XG", 192, 256))
-        ts(A("ts_", 0, 4), cW, -255.5, O.add)
-        marks(0, 4096.0)
-        ts(A("ts_", 4, 8), r2, -254.5, O.add)
-        marks(4, -4096.0)
-        for i in range(8):
-            mm(A("B2", 64, 65), A("HH", 128 * i, 128 * i + 128), A("half") if i in VSTEP else A("oneb", 0, 1), i == 0)
-        ts(A("TBc"), A("TriB"), A("B2", 64, 65), O.mult)
-        mm(A("B5"), A("TBc"), A("oneb"), False)
-        if t < RO - 1:
-            tt(A("x0c"), A("x0c"), A("B5"), O.max)
-            dma(A("X", 0, 8192, 1, 0, 128, 16), A("x0c"))
-            act(A("SG", t * 512, t * 512 + 512), A("x0c"), F.Sign, A("bB"))
+        R = "R%d" % t if TWO else Q
+        if FUSE:
+            sct(A("mP", 64), A("pos"), A("XP"))
+            remote("lT%d" % t, [(rank ^ 4, eT, A("mT", 0, 128), A(R, 128, 256), "aT%d" % t), (rank ^ 1, eP, A("mP", 0, 128), A(R, 0, 128), "aP%d" % t)])
         else:
-            mm(A("B5"), A("idb"), A("Rb"), False)
-            tt(A("Yt"), A("Z4"), A("B5"), O.min)
-            dma(hbm(T.yc[:, :]), A("Yt"), 0.6)
+            remote("lT%d" % t, [(rank ^ 4, eT, A("mT", 0, 128), A(R, 128, 256), "aT%d" % t)])
+            sct(A("mP", 64), A("pos"), A("XP"))
+            remote("lP%d" % t, [(rank ^ 1, eP, A("mP", 64, 128), A(R, 64, 128), "aP%d" % t)])
+        consume(t, cW, r2)
+        sct(A(Q, QG + 512, QG + 512 + 1600), A("pos"), A("XG", 192, 256))
+        behind("HH", 1)
 
     def merge(t):
         Q, C = "Q%d" % t, "C%d" % t
         nP, dP, nT, dT, n2 = A(C, 0, 1), A(C, 1, 2), A(C, 4, 5), A(C, 5, 6), A(C, 6, 7)
-        ts(A("t1"), A("t0"), nP, O.add, n2, O.add)
-        ts(A("h16"), A("t1"), M16, O.add, M16, O.subtract)
-        ts(A("S1", 0, 32), A("iW", 0, 32), nP, O.is_ge, dP, O.mult)
-        ts(A("S1", 32, 64), A("iW", 32, 64), nP, O.subtract, nT, O.is_ge)
-        ts(A("S1", 64, 96), A("iW", 64, 96), nP, O.subtract, n2, O.is_ge)
-        act(A("dT"), A("idb"), F.Copy, None, dT)
+        R = "R%d" % t if TWO else Q
+        t1 = "t0" if TWO else "t1"
+        if not TWO:
+            ts(A("t1"), A("t0"), nP, O.add, n2, O.add)
+        ts(A("h16"), A(t1), M16, O.add, M16, O.subtract)
+        if LLS:
+            tt(A("dl"), A("h16"), A(t1), O.subtract)
         out = A("B3", 0, 32)
         mm(out, A("idb"), A("B16"), True)
+        for k in range(4):
+            h, ll, ee = A("h16", k, k + 1), A("LL", 128 * k, 128 * k + 128), A("EE", 32 * k, 32 * k + 32)
+            act(A("SS", 32 * k, 32 * k + 32), A("nB16"), F.Sign, h)
+            mm(out, A("nBMh"), A("SS", 32 * k, 32 * k + 32), False)
+            if k in LLS:
+                act(ll, A("Rh"), F.Sign, A("dl", k, k + 1))
+                ts(ee, A("B16"), h, O.is_equal, 0.5, O.mult)
+                mm(out, o128, ee, False)
+            else:
+                ts(ll, A("Rp"), h, O.add, A(t1, k, k + 1), O.is_ge)
+                ts(ee, A("B16"), h, O.is_equal)
+            mm(out, ll, ee, False)
+        if TWO:
+            ts(A("MJ"), out, A("r32"), O.add, A("mC", 0, 1), O.add)
+            if OV:
+                cp(A(R, 256, 256 + 16 * OV), IX(A(Q, QG, QW), A("MJ", 0, OV)))
+            act(A(R, 256 + 16 * OV, 768), IX(A(Q, QG, QW), A("MJ", OV, 32)), F.Copy)
+            out = A("B4", 32, 64)
+            mm(out, A("idb"), A("B16"), True)
+        ts(A("S1", 0, 32), A("iW", 0, 32), nP, O.is_ge, dP, O.mult)
+        behind("HH", 2)
+        ts(A("S1", 32, 64), A("iW", 32, 64), nP, O.subtract, nT, O.is_ge)
+        behind("HH", 2)
+        ts(A("S1", 64, 96), A("iW", 64, 96), nP, O.subtract, n2, O.is_ge)
+        behind("HH", 2)
+        act(A("dT"), A("idb"), F.Copy, None, dT)
         mm(out, A("idb"), A("S1", 0, 32), False)
         mm(out, A("dT"), A("S1", 32, 64), False)
         mm(out, A("dT"), A("S1", 64, 96), False)
-        for k in range(4):
-            h = A("h16", k, k + 1)
-            act(A("SS", 32 * k, 32 * k + 32), A("nB16"), F.Sign, h)
-            mm(out, A("nBMh"), A("SS", 32 * k, 32 * k + 32), False)
-            ts(A("LL", 128 * k, 128 * k + 128), A("Rp"), h, O.add, A("t1", k, k + 1), O.is_ge)
-            ts(A("EE", 32 * k, 32 * k + 32), A("B16"), h, O.is_equal)
-            mm(out, A("LL", 128 * k, 128 * k + 128), A("EE", 32 * k, 32 * k + 32), False)
-        ts(A("MI"), out, A("r32"), O.add, A("mC", 0, 1), O.add)
-        a, b = IX(A(Q, 0, QW), A("MI", 0, 16)), IX(A(Q, 0, QW), A("MI", 16, 32))
-        if t < RO - 1:
-            cp(A("Q%d" % (t + 1), QG, QG + 256), a)
-            act(A("Q%d" % (t + 1), QG + 256, QG + 512), b, F.Copy)
+        if TWO:
+            ts(A("MI"), out, A("rcol"), O.add)
         else:
-            ts(A("Gn", 0, 256), a, -1.0, O.mult, 255.0, O.add)
-            act(A("Gn", 256, 512), b, F.Identity, 255.0, -1.0)
+            ts(A("MI"), out, A("r32"), O.add, A("mC", 0, 1), O.add)
+        win = A(R, 64, 768)
+        a, b = IX(win, A("MI", 0, 16)), IX(win, A("MI", 16, 32))
+        if t < RO - 1:
+            if MV:
+                cp(A("Q%d" % (t + 1), QG, QG + 16 * MV), IX(win, A("MI", 0, MV)))
+                behind("xc", 4)
+            act(A("Q%d" % (t + 1), QG + 16 * MV, QG + 512), IX(win, A("MI", MV, 32)), F.Copy)
+        else:
+            ts(A("Gn", 0, 256), a, 255.0, O.add)
+            act(A("Gn", 256, 512), b, F.Identity, 255.0)
             dma(hbm(T.yg[:, :]), A("Gn"))
 
     consts()
@@ -759,7 +944,6 @@ def rank_program(g, core, T, topo):
             for k in range(3):
                 mm(A("B7"), A("idb"), A("SG", k * 512, k * 512 + 512), k == 0)
             act(A("Z4"), A("B7"), F.Identity, 2.5, -0.5)
-            act(A("Rb"), A("x0c"), F.Relu, A("bB"))
         gathers(t)
         choose()
         give(t)

from concourse.mybir import AluOpType as O, AxisListType, ActivationFunctionType as F
from concourse.bass import DstId, RemoteDMATransfer

RO = 4
QW = 768
QG = 192
BIG = 16777216.0
M16 = 1.5 * 2.0 ** 27
M512 = 1.5 * 2.0 ** 32
PATH = [3, 1, 3, 1, 3, 1, 3, 3, 1, 3, 1, 1, 1, 1, 3, 3]
PATHS = [PATH, PATH]
HALVED = [13, 15]
LCUT = [(0, 1), (1, 3), (3, 8), (8, 16)]
PAIR = []
NB3, LURGE, EQS = 3, [0.3, 0.3, 0.0, 0.0, 0.0], 3
VMUL = [0]
KUB = []
KB = [(0, 8), (8, 12), (12, 16)]
KW = [b - a + (b == 16) for (a, b) in KB]
KO = [sum(KW[:k]) for k in range(len(KB) + 1)]
NSC = 14
NZ = 2
KK = 32768.0
M1, M64, M128 = 1.5 * 2.0 ** 23, 1.5 * 2.0 ** 29, 1.5 * 2.0 ** 30
TWO = 1
FILLV, UG_, UV_ = 128, 8, 3
FUSE, WSPLIT, MV, XLAT, HINT = 1, 128, 16, 0.3, 0
TURN = []
LLS = [0, 1, 2, 3]
OV = 0

_f = "x0c:512b xc:512b oks:512 Rr:512 SG:2560b Yt:512 Z4:512 G0:512b idf:128 idb:128b nidb:128b BM:128b BMf:128 nBMh:128b BMgf:8 BMg4:32 tri:128b oneb:512b onef:128"
_f += " O16:16b O16n:16b O16d:16b i65:66b rp:132b mW:128 t32:32 id2:64 rsK:1088b rs64:256b ph:1i p7:1i tE:32 Pat:1088b KM:34 KMm:34 thr:1 thS:32 c16f:128"
_f += " Bp:256b Rp:128b Rh:128b B16:32b nB16:32 cm:18 IO:512b sel15:128b neg1:1b pi:1i pj:1i rcol:1 r32:1 r0m:1 r1m:1 r2m:1 b512:1 iW:96 j255:512b jh:512h nK:512b d512:128b"
_f += " rself:128 rK:128 iB:128b kc:64 bM:1 rselb:128b n1k:64b kA:16i kB:16i iM:16 slS:32i slL:32i tB:128b tC:128b X:8272b Urep:8288 i8k:128b mC0:64b A0:8192b Ab:8192b o128:128b o255:128b bC:1 zb:128b"
_f += " wti:4i kmi:16i thi:1i wf:4 nwf:4 kf:16 Lw:144b Wp:32b BMw:128b c255:128b ui:64i U:32i sq:32i GA:128 GB:128i GT:128i t2:4 dl:4 MJ:32u HA:128 HB:128i AD:256b i22:128b c8256:64b mB:128b rs16:192b cb:18b T:512i Tf:512 OT:512u KS:1024 KI:512i"
_f += " triN:128b triP:128b nob:128b pm:32b KAB:64 tc:128i cI:32i DI:32i f1:32 lim:32 fit:32b rsel:32 ST:2112b VZ:1040b Pc:66 P1:66 Pd:64b Cc:128b Ck:128b Cq:128b Cs:128b wv:14 tmB:192"
_f += " EQ:256 SC:256 win:4b Mk:512b Jc:8b n194:4b Jf:8 cvec:4 pos:4u mC:4 t0:4 t1:4 h16:4 OF:8u OF2:4u OFX:8u UG:128 u1B:64 u2B:64 XG:256b XP:64b"
_f += " mP:1664b mT:1664b ts_:4 hs:4 hsm:4 nb:4b cmh:4 val:4 mk:64b ini:1 HH:1024h OH:2048h LL:512b EE:128b SS:128b S1:96b dT:128b MI:32u dg:16 cry:1 Gn:512b bA:1 bB:1"
_dt = {"b": "bfloat16", "i": "int32", "u": "uint16", "h": "float16"}
_pool, _where, SCRATCH = {}, {}, {}
for _x in _f.split():
    _n, _c = _x.split(":")
    _d = _dt.get(_c[-1], "float32")
    _c = int(_c if _d == "float32" else _c[:-1])
    if _c <= 264 and _n not in ("mC", "XG", "XP"):
        _p = "pool_" + _d
        _where[_n] = (_p, _pool.get(_p, 0), _c)
        _pool[_p] = _pool.get(_p, 0) + (_c + 15) // 16 * 16
        SCRATCH[_p] = ("sbuf", [128, _pool[_p]], _d)
    else:
        _where[_n] = (_n, 0, _c)
        SCRATCH[_n] = ("sbuf", [128, _c], _d)
for _t in range(RO):
    SCRATCH["Q%d" % _t] = ("sbuf", [128, QW + 1536], "bfloat16")
    _where["Q%d" % _t] = ("Q%d" % _t, 0, QW + 1536)
    SCRATCH["R%d" % _t] = ("sbuf", [128, 768], "bfloat16")
    _where["R%d" % _t] = ("R%d" % _t, 0, 768)
    SCRATCH["C%d" % _t] = ("sbuf", [128, 8], "float32")
    _where["C%d" % _t] = ("C%d" % _t, 0, 8)
for _t in range(8):
    SCRATCH["B%d" % _t] = ("psum", [128, 512], "float32")
    _where["B%d" % _t] = ("B%d" % _t, 0, 512)
NDMA = 24
SEMAPHORES = ["sv", "ss", "st", "sg"] + ["d%d" % _t for _t in range(NDMA)]
SEMAPHORES += ["e%d" % _t for _t in range(16) if 4 in (PATHS[0][_t], PATHS[1][_t])]
for _t in range(RO):
    SEMAPHORES += ["aP%d" % _t, "aT%d" % _t, "lP%d" % _t, "lT%d" % _t, "cP%d" % _t, "cT%d" % _t, "lC%d" % _t]

CY, PE_CY, GA, SCA, HOP, DMA_T, REM_T, X_T = 0.88e-3, 0.45e-3, 1.56, 3.8, 0.2, 1.6, 2.0, 6.0
ADD_Q, ADD_T = 0.8, 2.8
SLACK, EARLY, WARM = 0.3, 0.3, 0.01
MOVES, SHIFT, SWAPS = 150, 1.5, 9000
PASSES, SEED, SHAKE, CASES = 60, 1, 6.0, ((1.0, 0.22), (1.15, 0.15), (1.3, 0.2))
_order = {}


def _lay_out(ops):
    n = len(ops)
    succ = [[] for _ in range(n)]
    for i, o in enumerate(ops):
        for d in o["dep"]:
            succ[d].append(i)

    def gap(a, b):
        return 0.0 if (ops[a]["q"] == "t" and ops[b]["q"] == "t") or a in ops[b]["ord"] else HOP

    pre = [[(d, 0.0 if d in o["ord"] else ops[d]["lat"] + gap(d, i)) for d in o["dep"]] for i, o in enumerate(ops)]
    post = [[] for _ in range(n)]
    for i in range(n):
        for (d, w) in pre[i]:
            post[d].append((i, w))
    level, first = [0.0] * n, [0.0] * n
    for i in range(n - 1, -1, -1):
        level[i] = ops[i]["busy"] + max([w + level[s] for (s, w) in post[i]] + [ops[i]["lat"]])
        first[i] = max([ops[i]["first"]] + [first[s] for s in succ[i]])

    def lay(order, edges, least):
        start, lanes = [0.0] * n, {}
        for i in order:
            b = ops[i]["busy"]
            t = max([start[d] + ops[d]["busy"] + w for (d, w) in edges[i]] + [least[i]])
            if b > 0:
                lane = lanes.setdefault(ops[i]["q"], [])
                lo, hi = 0, len(lane)
                while lo < hi:
                    mid = (lo + hi) // 2
                    if lane[mid][1] <= t:
                        lo = mid + 1
                    else:
                        hi = mid
                while lo < len(lane) and lane[lo][0] < t + b - 1e-9:
                    t = max(t, lane[lo][1])
                    lo += 1
                lane.insert(lo, (t, t + b))
            start[i] = t
        return start

    def play(order, slow, hop):
        free, done = {}, [0.0] * n
        for i in order:
            o = ops[i]
            t = free.get(o["q"], 0.0) if o["busy"] > 0 else 0.0
            for (d, w) in pre[i]:
                w = done[d] + (w if w == 0.0 else w - HOP + hop)
                if w > t:
                    t = w
            done[i] = t + o["busy"] * slow
            if o["busy"] > 0:
                free[o["q"]] = done[i]
        return max(done[i] + tail[i] for i in range(n))

    zero, tail = [0.0] * n, [o["lat"] for o in ops]
    order = sorted(range(n), key=lambda i: (-level[i] - first[i], i))
    best, seed = None, [SEED]

    def draw():
        seed[0] = (seed[0] * 1103515245 + 12345) % 2147483648
        return seed[0] / 2147483648.0

    for k in range(PASSES):
        start = lay(order, pre, zero)
        at = {i: j for j, i in enumerate(order)}
        issue = sorted(range(n), key=lambda i: (start[i], at[i]))
        span = sum(play(issue, s, h) / s for (s, h) in CASES) / len(CASES)
        if best is None or span < best[0]:
            best = (span, issue, start, order)
        if k % 3 == 2:
            start, order = best[2], best[3]
            at = {i: j for j, i in enumerate(order)}
        back = sorted(range(n), key=lambda i: (-(start[i] + ops[i]["busy"]), -at[i]))
        late = lay(back, post, tail)
        key = [late[i] + ops[i]["busy"] for i in range(n)]
        if k % 3 == 2:
            a = draw() * max(key)
            b, c = a + 1.0 + 6.0 * draw(), SHAKE * draw()
            key = [x + c * draw() if a <= x < b else x for x in key]
            for i in back:
                key[i] = max([key[i]] + [key[s] + 1e-6 for s in succ[i]])
        at = {i: j for j, i in enumerate(back)}
        order = sorted(range(n), key=lambda i: (-key[i], -at[i]))
    at = {i: j for j, i in enumerate(best[3])}
    back = sorted(range(n), key=lambda i: (-(best[2][i] + ops[i]["busy"]), -at[i]))
    key = [-best[2][i] for i in range(n)]
    kin = {}
    for i, o in enumerate(ops):
        kin.setdefault(o["tag"], []).append(i)
    tags = sorted((t for t in kin if len(kin[t]) > 1 and t[0] in "vst"), key=lambda t: best[2][kin[t][1]])
    for k in range(MOVES):
        a, c, new = int(draw() * len(tags)), (draw() - 0.5) * SHIFT, list(key)
        for t in tags[a:a + 1 + int(draw() * draw() * 12)]:
            if t[0] == tags[a][0]:
                for i in kin[t]:
                    new[i] += c
        for i in back:
            new[i] = max([new[i]] + [new[s] + 1e-6 for s in succ[i]])
        order = sorted(range(n), key=lambda i: (-new[i], at[i]))
        start = lay(order, pre, zero)
        now = {i: j for j, i in enumerate(order)}
        issue = sorted(range(n), key=lambda i: (start[i], now[i]))
        span = sum(play(issue, s, h) / s for (s, h) in CASES) / len(CASES)
        if span < best[0] - 1e-9:
            best = (span, issue, start, order)
            key = [-x for x in start]
            at = now
            back = sorted(range(n), key=lambda i: (-(start[i] + ops[i]["busy"]), -at[i]))
    issue, span = list(best[1]), best[0]

    def chain(order, slow, hop):
        free, done, why, last, ready = {}, [0.0] * n, [None] * n, {}, [0.0] * n
        before = [None] * n
        for i in order:
            o, t, y = ops[i], 0.0, None
            for (d, w) in pre[i]:
                w = done[d] + (w if w == 0.0 else w - HOP + hop)
                if w > t:
                    t, y = w, d
            ready[i] = t
            if o["busy"] > 0:
                before[i] = last.get(o["q"])
                if free.get(o["q"], 0.0) > t:
                    t, y = free[o["q"]], before[i]
                free[o["q"]], last[o["q"]] = t + o["busy"] * slow, i
            why[i], done[i] = y, t + o["busy"] * slow
        end = max(done[i] + tail[i] for i in range(n))
        late, links = [end - tail[i] for i in range(n)], []
        for i in reversed(order):
            t = late[i] - ops[i]["busy"] * slow
            for (d, w) in pre[i]:
                late[d] = min(late[d], t - (w if w == 0.0 else w - HOP + hop))
            p = before[i]
            if p is not None:
                late[p] = min(late[p], t)
            while late[i] - done[i] < SLACK and p is not None and done[p] > ready[i] + 0.03 and ops[i]["q"] != ops[p]["tag"][0] + "t":
                links.append((p, i))
                p = before[p]
        return links

    lane = [{"v": 0, "s": 1, "t": 2, "g": 3, "y": 4, "r": 5}[o["q"]] for o in ops]
    busy = [o["busy"] for o in ops]
    (s1, h1), (s2, h2) = CASES[0], CASES[-1]
    pre2 = [[(d, w if w == 0.0 else w - HOP + h1, w if w == 0.0 else w - HOP + h2) for (d, w) in pre[i]] for i in range(n)]

    def both(order):
        f1, f2, d1, d2 = [0.0] * 6, [0.0] * 6, [0.0] * n, [0.0] * n
        for i in order:
            q = lane[i]
            t, u = f1[q], f2[q]
            for (d, w, x) in pre2[i]:
                w += d1[d]
                if w > t:
                    t = w
                x += d2[d]
                if x > u:
                    u = x
            d1[i] = t = t + busy[i] * s1
            d2[i] = u = u + busy[i] * s2
            if q < 5:
                f1[q], f2[q] = t, u
        a = max(d1[i] + tail[i] for i in ends) / s1 + max(d2[i] + tail[i] for i in ends) / s2
        return a / 2 + EARLY * (sum(d1) + sum(d2)) / n

    ends = [i for i in range(n) if not succ[i]]

    def ahead(order, i, p):
        at = {x: j for j, x in enumerate(order)}
        if at[i] < at[p]:
            return order
        need, todo = {i}, [i]
        while todo:
            for (d, w) in pre[todo.pop()]:
                if at[d] >= at[p] and d not in need:
                    if d == p:
                        return order
                    need.add(d)
                    todo.append(d)
        a, b = at[p], at[i] + 1
        return order[:a] + [x for x in order[a:b] if x in need] + [x for x in order[a:b] if x not in need] + order[b:]

    links, span = [], both(issue)
    for k in range(SWAPS):
        if not links or k % 40 == 0:
            links = chain(issue, *CASES[k % len(CASES)])
        p, i = links.pop(int(draw() * len(links)))
        new = issue
        if len(kin[ops[i]["tag"]]) == len(kin[ops[p]["tag"]]) and draw() < 0.6:
            for (x, y) in zip(kin[ops[i]["tag"]], kin[ops[p]["tag"]]):
                new = ahead(new, x, y)
        else:
            new = ahead(new, i, p)
        if new is issue:
            continue
        s = both(new)
        if s < span + WARM * draw() * (1.0 - k / SWAPS):
            issue, span = new, s
    _order["span"] = sum(play(issue, s, h) / s for (s, h) in CASES) / len(CASES)
    return issue


def rank_program(g, core, T, topo):
    rank = T.rank_of(core)
    if rank is None:
        return
    queues = {"v": g.vector, "s": g.scalar, "t": g.tensor, "g": g, "y": g.sync}
    own = {"v": "sv", "s": "ss", "t": "st", "g": "sg"}
    ops, log, banks, seen = [], {}, {}, {}

    def A(n, lo=0, hi=None, st=1, p0=0, p1=128, pst=1):
        p, o, c = _where[n]
        hi = c if hi is None else hi
        k = (hi - lo - 1) // st + 1
        hi = lo + (k - 1) * st + 1
        ap = T[p][p0:p1:pst, o + lo:o + hi:st] if (pst != 1 or st != 1) else T[p][p0:p1, o + lo:o + hi]
        return (ap, [(p, o + lo, o + hi, st, p0, p1, pst)], k, SCRATCH[p][2], SCRATCH[p][0])

    def back(n):
        a = A(n)
        return (T[n][0:128, ::-1],) + a[1:]

    def IX(win, off):
        return (win[0].indirect(off[0]), win[1] + off[1], 16 * off[2], win[3], "ix")

    def hit(a, b):
        if a[1] >= b[2] or b[1] >= a[2] or a[4] >= b[5] or b[4] >= a[5]:
            return False
        if a[6] == b[6] and (a[4] - b[4]) % a[6]:
            return False
        return not (a[3] == b[3] and a[3] > 1 and (a[1] - b[1]) % a[3])

    def rg(xs):
        return [r for x in xs if isinstance(x, tuple) for r in x[1]]

    def ap(x):
        return x[0] if isinstance(x, tuple) else x

    def add(q, outs, ins, f, busy, lat=0.0, start=None, sem=None, inc=1, after=(), first=0.0):
        i = len(ops)
        dep = set(after)
        o = {"q": q, "f": f, "busy": busy, "lat": lat, "dep": dep, "ord": set(after), "sem": sem or own.get(q), "inc": inc, "grp": None, "first": first}
        tag = (q,) + tuple((r[0].rstrip("0123") if r[0][0] in "QCR" else r[0],) + r[1:] for r in rg(outs)[:1] + rg(ins)[:1])
        seen[tag] = seen.get(tag, 0) + 1
        o["tag"] = tag + (seen[tag],)
        ops.append(o)
        for regs, isw in ((rg(ins), False), (rg(outs), True)):
            for r in regs:
                if r[0][0] == "B" and r[0][1:].isdigit():
                    b = banks.setdefault(r[0], {"q": None, "run": [], "prev": [], "grp": None})
                    if b["q"] != q:
                        b["q"], b["prev"], b["run"] = q, b["run"], []
                    dep.update(b["prev"])
                    if q != "t":
                        L = log.setdefault(r[0], [])
                        dep.update(j for (r2, w2, j) in L if j in b["run"] and (isw or w2) and hit(r, r2))
                        L.append((r, isw, i))
                    if q == "t":
                        if start:
                            dep.update(b["run"])
                            b["grp"], b["new"] = [i], [(r, i)]
                        else:
                            dep.add(b["grp"][0])
                            b["grp"].append(i)
                            was = [j for (r2, j) in b["new"] if hit(r, r2)]
                            dep.update(was)
                            if not was:
                                b["new"].append((r, i))
                        o["grp"], o["rows"] = b["grp"], (r[4], r[5])
                    if i not in b["run"]:
                        b["run"].append(i)
                    continue
                L = log.setdefault(r[0], [])
                for (r2, w2, j) in L:
                    if (isw or w2) and hit(r, r2):
                        dep.add(j)
                if isw:
                    L[:] = [e for e in L if not (e[0][1] >= r[1] and e[0][2] <= r[2] and ((r[3] == 1 and r[6] == 1) or e[0] == r) and e[0][4] >= r[4] and e[0][5] <= r[5])]
                L.append((r, isw, i))
        dep.discard(i)
        return i

    mark = {}

    def behind(name, bit):
        if HINT & bit:
            ops[-1]["dep"].add(mark[name])
            ops[-1]["ord"].add(mark[name])

    def cost(o, xs, per=None, fixed=0.05):
        xs = [x for x in xs if isinstance(x, tuple)]
        if xs[0][4] == "ix":
            return fixed + xs[0][2] * GA * CY
        if per is None:
            per = 0.5 if all(x[3] in ("bfloat16", "uint16", "float16") for x in [o] + xs) else 1.0
        return max(64, xs[0][2] * per) * CY

    V, SE, PE = g.vector, g.scalar, g.tensor

    def cp(o, i):
        add("v", [o], [i], lambda s: V.tensor_copy(ap(o), ap(i)), cost(o, [i]))

    def sct(win, off, i):
        add("v", [win], [off, i], lambda s: V.tensor_copy(win[0].indirect(off[0]), ap(i)), 0.05 + i[2] * SCA * CY)

    def tt(o, a, b, op):
        add("v", [o], [a, b], lambda s: V.tensor_tensor(ap(o), ap(a), ap(b), op), cost(o, [a], 1.0 if "psum" in (a[4], b[4]) else 2.0))

    def ts(o, a, s1, op0, s2=None, op1=None):
        if op1 is None:
            add("v", [o], [a, s1], lambda s: V.tensor_scalar(ap(o), ap(a), ap(s1), None, op0), cost(o, [a]))
        else:
            add("v", [o], [a, s1, s2], lambda s: V.tensor_scalar(ap(o), ap(a), ap(s1), ap(s2), op0, op1), cost(o, [a]))

    def scan(o, a, b, init, op0, op1):
        add("v", [o], [a, b, init], lambda s: V.tensor_tensor_scan(ap(o), ap(a), ap(b), ap(init), op0, op1), cost(o, [a, b]))

    def red(o, i, op, negate=False):
        add("v", [o], [i], lambda s: V.tensor_reduce(ap(o), ap(i), AxisListType.X, op, negate=negate), cost(o, [i], 1.0))

    def ms(o, c):
        add("v", [o], [], lambda s: V.memset(ap(o), c), cost(o, [o]))

    def act(o, i, f, bias=None, scale=None):
        kw = {}
        if bias is not None:
            kw["bias"] = ap(bias)
        if scale is not None:
            kw["scale"] = ap(scale)
        add("s", [o], [i, bias, scale], lambda s: SE.activation(ap(o), ap(i), f, **kw), cost(o, [i], 1.0, 0.065))

    def mm(o, l, r, start=True):
        add("t", [o], [l, r], lambda s: PE.matmul(ap(o), ap(l), ap(r), start, s), max(min(64, l[2]), r[2]) * PE_CY * (4 if l[3] == "float32" else 1), start=start)

    def iota(o, pat, base, ch):
        kw = {} if o[3] == "int32" else {"allow_small_or_imprecise_dtypes": True}
        add("g", [o], [], lambda s: g.iota(ap(o), pat, base, ch, **kw), 0.13 + 2 * o[2] * CY)

    def fill(o, c):
        if o[2] <= FILLV:
            ms(o, int(c) if o[3] == "int32" else float(c))
        else:
            iota(o, [[0, o[2]]], int(c), 0)

    def sel(o, i, pat, op, base, ch, other=0.0):
        add("g", [o], [i], lambda s: g.affine_select(ap(o), ap(i), pat, op, other, base, ch), 0.17 + 2 * o[2] * CY)

    def own_group(o, i, n, other):
        add_ = [[0, n]] if n > 1 else []
        sel(o, i, add_ + [[-16, 8], [0, 16]], O.is_ge, 0, 1, other)
        sel(o, o, add_ + [[16, 8], [0, 16]], O.is_ge, 15, -1, other)

    nd = [0]

    def dma(o, i, t=0.3, after=(), behind=()):
        nd[0] += 1
        return add("y", [o], [i] + list(behind), lambda s: g.sync.dma_start(ap(o), ap(i)), 0.05, DMA_T + t, sem="d%d" % (nd[0] - 1), inc=16, after=after)

    def hbm(x):
        return (x, [], 0, "", "dram")

    def remote(local, parts):
        trs = []
        for (r, e, src, land, sem) in parts:
            rid, pid, _ = topo.addr(T.cores[r])
            trs.append((rid, pid, sum(1 << x for x in e), src[0], land[0], T.sem[sem]))

        def f(s):
            if len(trs) == 1:
                rid, pid, m, a, b, sm = trs[0]
                g.remote_dma(out_ap=b, in_ap=a, remote_sem=sm, local_sem=T.sem[local], pid=pid, routing_id=rid, dma_engine_mask=m)
            else:
                g.remote_dma_fused([RemoteDMATransfer(dst_ids=[DstId(rid=rid, pnc=pid)], dma_engine_mask=m, remote_sem=sm, src=a, dst=b) for (rid, pid, m, a, b, sm) in trs],
                                   local_sem=T.sem[local])
        i = add("g", [], [p[2] for p in parts], f, 0.3, REM_T, sem=local, inc=-sum(len(p[1]) for p in parts))
        for (r, e, src, land, sem) in parts:
            add("r", [land], [], None, 0.0, REM_T, sem=sem, inc=-len(e), after=[i])

    eP = topo.engines(core, T.cores[rank ^ 1])[8:16]
    eT = topo.engines(core, T.cores[rank ^ 4])[:8]

    d = [dma(A("G0"), hbm(T.gd[:, :]))]
    d.append(dma(A("wti"), hbm(T.wt[:, :]), after=d[-1:]))
    d.append(dma(A("kmi"), hbm(T.km[:, :]), after=d[-1:]))
    d.append(dma(A("X", 0, 8192), hbm(T.xs[:, :]), X_T, after=d[-1:]))
    d.append(dma(A("x0c"), hbm(T.xs[0:128:16, :]), X_T + 0.6, after=d[-1:]))
    dma(A("thi"), hbm(T.th[:, :]), X_T + 0.6, after=d[-1:])
    o128 = A("oneb", 0, 128)
    W = 512 // NZ
    MW = 1.5 * 2.0 ** 23 * W
    nv = 32 - NSC

    def consts():
        ms(A("oneb"), 1.0)
        ms(A("onef"), 1.0)
        ms(A("c255"), 255.0)
        ms(A("X", 8192, 8272), 255.0)
        ms(A("Lw"), 0.0)
        ms(A("rsK"), 0.0)
        dma(A("VZ"), A("rsK", 0, 1040))
        own_group(A("BM"), o128, 1, 0.0)
        iota(A("pi"), [[0, 1]], 0, 1)
        iota(A("iM"), [[64, 16]], 0, 0)
        cp(A("wf"), A("wti"))
        cp(A("BMgf"), A("BM", 0, 128, 16))
        act(A("BMf"), A("BM"), F.Copy)
        for b in range(4):
            act(A("BMg4", 8 * b, 8 * b + 8), A("BM", 0, 128, 16), F.Copy)
        cp(A("kf"), A("kmi"))
        ts(A("Q0", QG, QG + 512), A("G0"), -255.0, O.add)
        ts(A("pj"), A("pi"), 15, O.bitwise_and)
        cp(A("rcol"), A("pj"))
        ts(A("b512"), A("pj"), 512.0, O.mult)
        ts(A("r32"), A("pj"), 32.0, O.add)
        ts(A("r0m"), A("pj"), 0.0, O.is_equal)
        ts(A("r1m"), A("pj"), 1.0, O.is_equal)
        ms(A("KM"), 0.0)
        ms(A("KMm"), 0.0)
        for k in range(len(KB)):
            fill(A("rsK", 64 * KO[k], 64 * KO[k + 1], KW[k]), BIG / 2)
        for n, c in (("O16", 1024.0), ("O16n", -1024.0), ("O16d", 2048.0)):
            act(A(n, 0, 16, 2), A("BMgf"), F.Copy, None, c)
            act(A(n, 1, 16, 2), A("BMgf"), F.Copy, None, c)
        ts(A("kA"), A("kmi"), 6, O.logical_shift_right)
        ts(A("kB"), A("kmi"), 63, O.bitwise_and)
        for j, (a, b) in enumerate(KB):
            for k, n in enumerate(("kA", "kB")):
                c = 2 * KO[j] + k * KW[j]
                ts(A("KM", c, c + b - a), A(n, a, b), A("r0m"), O.mult)
                act(A("KMm", c, c + b - a), A("iM", a, b), F.Copy, None, A("r1m"))
        tt(A("KM"), A("KM"), A("KMm"), O.add)
        for j in range(len(KB)):
            w, o = 2 * KW[j], 64 * KO[j]
            for q in range(8):
                act(A("Pat", o + q * w, o + q * w + w), A("KM", 2 * KO[j], 2 * KO[j + 1]), F.Copy, None, A("BMgf", q, q + 1))
            act(A("Pat", o + 8 * w, o + 16 * w), A("Pat", o, o + 8 * w), F.Copy)
            act(A("Pat", o + 16 * w, o + 32 * w), A("Pat", o, o + 16 * w), F.Copy)
        sel(A("idf"), A("onef"), [[-1, 128]], O.is_equal, 0, 1)
        act(A("idb"), A("idf"), F.Copy)
        act(A("nidb"), A("idf"), F.Copy, None, -1.0)
        act(A("i8k"), A("idf"), F.Copy, None, 8192.0)
        act(A("i22"), A("idf"), F.Copy, None, 4194304.0)
        fill(A("c8256"), 8256)
        iota(A("j255"), [[1, 512]], -255, 0)
        ts(A("jh", 0, W), A("j255", 0, W), 255.5 - W // 2, O.add)
        fill(A("nK"), -KK)
        act(A("bC"), A("b512"), F.Identity, 16384.0)
        act(A("d512"), A("idf"), F.Copy, None, A("bC"))
        act(A("iB"), A("idf"), F.Copy, None, -2.0 ** 28)
        ts(A("bM"), A("b512"), -1.0, O.mult, 0.5, O.add)
        ts(A("ini"), A("b512"), -KK, O.mult, 1.5 * KK - 2.0 ** 28, O.add)
        act(A("kc"), A("onef", 0, 64), F.Copy, None, A("ini"))
        iota(A("HA", 0, 128, 2), [[0, 32], [1, 2]], 0, 0)
        fill(A("HA", 1, 128, 4), 64)
        fill(A("HB", 1, 128, 4), 0)
        ms(A("GA", 0, 128, 4), 0.0)
        ms(A("GA", 2, 128, 4), 1.0 / 32)
        ms(A("GA", 3, 128, 4), 1.0)
        ms(A("GB", 1, 128, 4), -12)
        ms(A("GB", 2, 128, 4), int(M1))
        act(A("o128"), o128, F.Copy, None, 1.0 / 128)
        act(A("o255"), o128, F.Copy, None, 255.0 / 128)
        fill(A("zb"), 0)
        sel(A("triP"), o128, [[1, 128]], O.is_gt, 0, -1)
        sel(A("triP"), A("triP"), [[1, 128]], O.not_equal, 0, -1, -127.0)
        act(A("triN"), A("triP"), F.Copy, None, -1.0)
        fill(A("nob"), -1)
        fill(A("pm", 0, nv), 128)
        fill(A("pm", nv, 32), -128)
        sel(A("tB"), A("BM"), [[1, 128]], O.is_gt, 0, -1)
        iota(A("i65"), [[1, 66]], 0, 0)
        act(A("rp", 0, 66), A("i65"), F.Identity, 0.5)
        ts(A("cb", 0, 16), A("i65", 0, 16), A("rcol"), O.is_le, 32768.0, O.mult)
        fill(A("cb", 16, 17), 8192)
        fill(A("neg1"), -1)
        fill(A("n1k"), 1024)
        act(A("SG", 2048, 2560), A("x0c"), F.Sign, 191.5, -1.0)
        ts(A("mW", 0, 16), A("i65", 0, 16), A("rcol"), O.is_equal)
        act(A("mB", 0, 16), A("mW", 0, 16), F.Identity, BIG / 2, -BIG / 2)
        for k in (16, 32):
            act(A("mB", k, 2 * k), A("mB", 0, k), F.Copy)
        act(A("mB", 64, 128), A("mB", 0, 64), F.Copy)
        ts(A("mC0"), A("mB", 0, 64), 8256.0, O.max)
        act(A("c16f"), o128, F.Copy, None, 0.0625)
        fill(A("rs16"), -BIG / 2)
        fill(A("rs16", 0, 192, 16), BIG / 2)
        fill(A("rs64"), -BIG / 2)
        fill(A("rs64", 0, 256, 64), BIG / 2)
        wv = [A("wv", k, k + 1) for k in range(14)]
        ts(A("r2m"), A("pj"), 2.0, O.is_equal, A("r0m"), O.add)
        tt(A("r2m"), A("r2m"), A("r1m"), O.subtract)
        act(A("rself"), A("BM"), F.Copy, None, A("r2m"))
        act(A("rK"), A("rself"), F.Copy, None, KK)
        act(A("rselb"), A("BM"), F.Copy, None, A("r0m"))
        ts(wv[10], A("pj"), 15.0, O.is_equal, 0.5, O.mult)
        act(A("sel15"), A("BM"), F.Copy, None, wv[10])
        act(A("nBMh"), A("BM"), F.Copy, None, -0.5)
        iota(A("Bp", 0, 128 * NZ), [[W, NZ], [0, 8], [512, 16]], W, 0)
        own_group(A("Bp", 0, 128 * NZ), A("Bp", 0, 128 * NZ), NZ, -4096.0)
        iota(A("Rp"), [[0, 8], [1, 16]], -8, 0)
        own_group(A("Rp"), A("Rp"), 1, -4096.0)
        if LLS:
            act(A("Rh"), A("Rp"), F.Identity, 0.5)
        iota(A("B16"), [[16, 32]], 0, 0)
        act(A("nB16"), A("B16"), F.Identity, 0.5, -1.0)
        iota(A("iW"), [[-64, 3], [16, 32]], -64, 0)
        ts(A("iW"), A("iW"), A("rcol"), O.add)
        iota(A("VZ", 20, 1040, 32), [[128, 4], [0, 8]], 0, 0)
        iota(A("VZ", 21, 1040, 32), [[0, 32]], 0, 1)
        fill(A("VZ", 22, 1040, 32), 1)
        fill(A("VZ", 23, 1040, 32), 1)
        ts(A("ph"), A("pj"), 1, O.logical_shift_right)
        for (k, n, c) in ((0, "ph", 0.0), (1, "ph", 1.0), (2, "ph", 2.0), (3, "pj", 6.0), (4, "pj", 7.0)):
            ts(wv[k], A(n), c, O.is_equal, 0.5, O.mult)
        for (k, a, c, b) in ((5, 3, -8256.0, 0), (6, 3, -10.0, 2), (7, 3, -4194304.0, 2), (8, 1, 512.0, 7), (9, 4, -0.5, 8)):
            act(wv[k], wv[a], F.Identity, wv[b], c)
        for n, k in (("Cc", 5), ("Cs", 6), ("Cq", 8), ("Ck", 9)):
            act(A(n), A("BM"), F.Copy, None, wv[k])
        fill(A("n194"), -2 if TWO else -194)
        ts(A("Jf", 4, 8), A("B16", 0, 4), A("rcol"), O.add, 128.0, O.add)
        act(A("Jf", 0, 4), A("Jf", 4, 8), F.Copy, None, 8.0)
        act(A("Jc", 0, 4), A("Jf", 4, 8), F.Copy, None, 8.0)
        fill(A("Jc", 4, 5), -64)
        for k in range(4):
            act(A("Mk", 128 * k, 128 * k + 128), A("nidb"), F.Copy, None, A("Jf", k, k + 1))
        iota(A("cvec", 0, 2), [[-2, 2]], 1, 0)
        iota(A("cvec", 2, 4), [[-2, 2]], 2, 0)
        fill(A("mP", 0, 128), 0)
        fill(A("mT", 0, 128), 0)
        for t in range(RO):
            fill(A("Q%d" % t, QG + 512, QW), 0)
        cp(A("thr"), A("thi"))
        ts(A("tE"), A("BMg4"), A("thr"), O.mult)
        mm(A("B5", 0, 32), A("c16f"), A("tE"))
        cp(A("thS"), A("B5", 0, 32))
        fill(A("Urep", 8192, 8288), 8192)
        fill(A("Urep", 8192, 8194), 0)
        for k in range(16):
            u = A("Urep", 512 * k, 512 * k + 512)
            if k < UG_:
                fill(u, 0)
            elif k < UG_ + UV_:
                ms(u, 0.0)
        if UG_ + UV_ < 16:
            c = 512 * (UG_ + UV_)
            dma(A("Urep", c, 8192), A("Urep", 0, 8192 - c), X_T * 1.5 * (8192 - c) / 4096, behind=[A("thi")])

    def weights(t):
        w = A("wf", t, t + 1)
        act(A("Lw", 15, 143, 16), A("BMgf"), F.Copy, None, w)
        act(A("Wp"), A("BMg4"), F.Copy, None, w)
        act(A("BMw"), A("BM"), F.Copy, None, w)

    def lists(t):
        Q = "Q%d" % t
        mm(A("B4", 0, 32), A("BMw"), A("c255", 0, 32), True)
        mm(A("B1", 32, 64), A("c255"), A("Wp"), True)
        for r in range(16):
            mm(A("B4", 0, 32), A("Lw", 15 - r, 143 - r), A(Q, QG + r, QG + 512, 16), False)
        for b in range(4):
            mm(A("B1", 32 + 8 * b, 40 + 8 * b), A(Q, QG + 128 * b, QG + 128 * b + 128), A("Lw", 15, 143, 16), False)
        u, uf = A("GB", 0, 128, 4), A("GA", 1, 128, 4)
        cp(A("ui", 0, 32), A("B4", 0, 32))
        ts(u, A("ui", 0, 32), 4095, O.bitwise_and)
        cp(uf, u)
        ts(A("GB", 3, 128, 4), u, A("kf", 0, 1), O.mult, -M1, O.add)
        scan(A("GT"), A("GA"), A("GB"), 0.0, O.mult, O.add)
        for j, (a, b) in enumerate(LCUT):
            for m in range(max(a, 1), b):
                ku = A("Tf", 32 * m, 32 * m + 32)
                if m in VMUL:
                    ts(ku, u, A("kf", m, m + 1), O.mult, -M1, O.add)
                else:
                    act(ku, uf, F.Identity, -M1, A("kf", m, m + 1))
                tt(A("T", 32 * m, 32 * m + 32), ku, A("GT", 2, 128, 4), O.add)
            ts(A("T", 32 * a, 32 * b), A("T", 32 * a, 32 * b) if a else A("GT", 3, 128, 4), 8191, O.bitwise_and)
            cp(A("OT", 32 * a, 32 * b), A("T", 32 * a, 32 * b))
            ops[-1]["lat"] = LURGE[j]
        cp(A("ui", 32, 64), A("B1", 32, 64))
        ts(A("U"), A("ui", 32, 64), 4095, O.bitwise_and)
        cp(A("HA", 3, 128, 4), A("U"))
        tt(A("sq"), A("U"), A("U"), O.mult)
        ts(A("HB", 3, 128, 4), A("sq"), 5, O.logical_shift_right)

    def gathers(t):
        Q, n3, last = "Q%d" % t, 0, len(KB) - 1
        PATH = PATHS[min(t, 1)]
        for k in range(len(KB)):
            mm(A("B%d" % k, 0, 64 * KW[k]), o128, A("Pat", 64 * KO[k], 64 * KO[k + 1]), True)
        for m in range(16):
            k = [i for i, (a, b) in enumerate(KB) if a <= m < b][0]
            a, b = KB[k]
            cuts = ((0, 256), (256, 512)) if m in HALVED else ((0, 512),)
            for (lo, hi) in cuts:
                o = 512 * m
                PATH = list(PATHS[min(t, 1)])
                if lo and m in TURN:
                    PATH[m] = 4 - PATH[m]
                src, h = IX(A("X"), A("OT", 32 * m + lo // 16, 32 * m + hi // 16)), A(Q, QG + lo, QG + hi)
                a0, ab = A("A0", o + lo, o + hi), A("Ab", o + lo, o + hi)
                if PATH[m] == 3:
                    bank, x = A("B%d" % (3 + n3 % NB3), 0, hi - lo), a0
                    n3 += 1
                    if m in PAIR:
                        act(A("A0", o, o + 1024), IX(A("X"), A("OT", 32 * m, 32 * m + 64)), F.Copy)
                    elif m - 1 not in PAIR:
                        act(x, src, F.Copy)
                    mm(bank, A("idb"), h, True)
                    mm(bank, A("idb"), x, False)
                    act(ab, bank, F.Abs)
                else:
                    if PATH[m] == 4:
                        act(a0, src, F.Copy)
                        add("g", [a0], [a0, h], lambda s, a0=a0, h=h: g.dma_start(ap(a0), ap(h), accum_op=O.add), ADD_Q, ADD_T, sem="e%d" % m, inc=16)
                    else:
                        tt(a0, src, h, O.add)
                    if PATH[m] == 2:
                        act(ab, a0, F.Abs)
                    else:
                        ts(ab, a0, 0.0, O.max)
                for c in range(lo // 128, hi // 128):
                    w = KW[k]
                    out = A("B%d" % k, c * 16 * w + m - a, (c + 1) * 16 * w, w)
                    if PATH[m] in (1, 4):
                        mm(out, A("A0", o + 128 * c, o + 128 * c + 128), A("O16n"), False)
                    mm(out, A("Ab", o + 128 * c, o + 128 * c + 128), A("O16" if PATH[m] in (2, 3) else "O16d"), False)
            if m == b - 1:
                lo, hi, w = 64 * KO[k], 64 * KO[k + 1], KW[k]
                if k == last:
                    low = [A("KS", 64 * KO[j] + KW[j] - 1, 64 * KO[j + 1], KW[j]) for j in range(last)]
                    if last == 2:
                        tt(A("KAB"), low[0], low[1], O.min)
                    mm(A("B%d" % k, w - 1, 64 * w, w), A("idf"), A("KAB") if last == 2 else low[0], False)
                scan(A("KI", 0, hi - lo) if k == last else A("KS", lo, hi), A("rsK", lo, hi), A("B%d" % k, 0, hi - lo), 0.0, O.max, O.min)

    def utable(t):
        k = (t - 1) % 5 if t else 4
        mm(A("B7"), A("o128"), A("j255"), True)
        mm(A("B7"), A("o255"), A("oneb"), False)
        mm(A("B7"), A("d512"), A("oneb"), False)
        mm(A("B7"), A("i8k"), A("SG", 2048, 2560), False)
        mm(A("B7"), A("i8k"), A("SG", 512 * k, 512 * k + 512), False)
        scan(back("oks"), back("B7"), A("oneb"), 32768.0, O.min, O.mult)
        dma(A("Urep", 2, 8194, 1, 0, 128, 16), A("oks"), 0.6)
        act(A("dg"), A("mW", 0, 16), F.Copy, None, A("oks", 0, 1))
        mm(A("B6", 0, 17), A("idb"), A("cb", 0, 17), True)
        mm(A("B6", 0, 16), A("BMf"), A("dg"), False)
        mm(A("B6", 16, 17), A("sel15"), A("neg1"), False)
        mm(A("B6", 16, 17), A("sel15"), A("SG", t * 512 - 1, t * 512) if t else A("neg1"), False)
        red(A("cry"), A("B6", 0, 17), O.min, True)
        act(A("Rr"), A("oks"), F.Relu, A("cry"))
        dma(A("Urep", 2, 8194, 1, 1, 128, 16), A("Rr"), 0.6)

    def choose():
        w = KW[-1]
        ts(A("HB", 0, 128, 2), A("KI", w - 1, 64 * w, w), 63, O.bitwise_and)
        ts(A("DI"), A("KI", w - 1, 64 * w, 2 * w), 10, O.logical_shift_right)
        scan(A("tc"), A("HA"), A("HB"), 0.0, O.mult, O.add)
        tt(A("f1"), A("DI"), A("thS"), O.is_lt)
        ts(A("lim"), A("f1"), 8096.0, O.mult)
        ts(A("cI"), A("tc", 3, 128, 4), 8191, O.bitwise_and)
        tt(A("fit"), A("cI"), A("lim"), O.is_lt)
        for (bank, a, b, tri, one) in (("B3", 0, nv, "triP", o128), ("B1", nv, 32, "triN", A("nob"))):
            mm(A(bank, a, b), A("idb"), A("pm", a, b), True)
            mm(A(bank, a, b), A(tri), A("fit", a, b), False)
            for s in (8, 16, 24):
                if max(a, s) < b:
                    mm(A(bank, max(a, s), b), one, A("fit", max(a, s) - s, b - s), False)
        for v, n in ((16, "cI"), (18, "DI")):
            cp(A("VZ", v, 1040, 32), A(n))
            tt(A("VZ", v + 1, 1040, 32), A(n), A("VZ", v, 1040, 32), O.subtract)
        act(A("rsel", nv, 32), A("B1", nv, 32), F.Copy)
        mm(A("B4", 0, 65), A("zb"), A("i65", 0, 65), True)
        for c in range(32):
            st = A("ST", c * 66, c * 66 + 65)
            if c < nv:
                ts(st, A("i65", 0, 65), A("B3", c, c + 1), O.is_ge, 2.0, O.mult)
            else:
                act(st, A("rp", 0, 65), F.Sign, A("rsel", c, c + 1))
            w, p = 16 + 32 * c - 16 * (c % 2), 32 * (c % 8 // 2)
            mm(A("B4", 0, 65, 1, p, p + 32), A("VZ", w, w + 32), st, False)
        cp(A("Pc", 0, 64), A("B4", 0, 64))
        tt(A("Pd"), A("B4", 1, 65), A("Pc", 0, 64), O.subtract)
        mm(A("B0", 0, 64), A("idb"), A("mC0"), True)
        mm(A("B0", 64, 192), A("idb"), A("mB"), False)
        mm(A("B0", 0, 64), A("Cc"), A("Pd"), False)
        mm(A("B0", 64, 128), A("Cs"), A("Pd"), False)
        mm(A("B0", 128, 192), A("Ck"), A("Pd"), False)
        if EQS < 4:
            mm(A("B3", 64, 128), A("Cc"), A("Pd"), True)
        for k in range(4 - EQS):
            mm(A("B3", 128 + 64 * k, 192 + 64 * k), A("Cq"), A("Pd"), False)

    def wrap(b, src):
        n = src[2]
        scan(A(b, 0, n), A("rs16", 0, n), src, 0.0, O.max, O.min)
        return A(b, 15, n, 16)

    def consume(t, cW, r2):
        act(A("ts_"), cW, F.Identity, W // 2 + 0.5)
        act(A("cmh"), cW, F.Identity, -0.5)
        ts(A("hs"), A("ts_"), MW, O.add, MW, O.subtract)
        tt(A("nb"), A("ts_"), A("hs"), O.subtract)
        tt(A("hsm"), A("hs"), A("win"), O.mult)
        first = [(A("idb"), A("x0c"))] if t < RO - 1 else []
        if t:
            first += [(A("i8k"), A("oneb")), (A("i8k"), A("SG", t * 512 - 512, t * 512))]
        for i, (l, r) in enumerate(first):
            mm(A("B5"), l, r, i == 0)
        mm(A("B6", 64, 128), A("idf"), A("kc"), True)
        mm(A("B6", 64, 128), A("iB"), A("mk"), False)
        mm(A("B6", 64, 128), A("rK"), A("UG", 64, 128), False)
        red(A("ini"), A("B6", 64, 128), O.max)
        tt(A("val"), r2, A("cmh"), O.subtract)
        for i in range(4):
            oh, o = A("OH", W * i, W * i + W), 128 * NZ * i
            ts(oh, A("jh", 0, W), A("nb", i, i + 1), O.is_equal, KK, O.mult)
            ts(A("HH", o, o + 128 * NZ), A("Bp", 0, 128 * NZ), A("hsm", i, i + 1), O.is_equal, A("val", i, i + 1), O.mult)
            mark["HH"] = len(ops) - 1
            for z in range(NZ):
                mm(A("B5", W * z, W * z + W), A("HH", o + 128 * z, o + 128 * z + 128), oh, False)
        if t < RO - 1:
            scan(A("xc"), A("nK"), A("B5"), A("ini"), O.add, O.max)
            mark["xc"] = len(ops) - 1
            dma(A("X", 0, 8192, 1, 0, 128, 16), A("xc"), XLAT)
            act(A("SG", t * 512, t * 512 + 512), A("xc"), F.Sign, -256.0)
        else:
            scan(A("B0"), A("nK"), A("B5"), A("ini"), O.add, O.max)
            tt(A("Yt"), A("Z4"), A("B0"), O.min)
            dma(hbm(T.yc[:, :]), A("Yt"), 0.6)

    def give(t):
        Q, C = "Q%d" % t, "C%d" % t
        if WSPLIT:
            scan(A("tmB", 0, WSPLIT), A("rs16", 0, WSPLIT), A("B0", 0, WSPLIT), 0.0, O.max, O.min)
        scan(A("tmB", WSPLIT, 192), A("rs16", WSPLIT, 192), A("B0", WSPLIT, 192), 0.0, O.max, O.min)
        cW, sW = A("tmB", 15, 64, 16), A("tmB", 79, 128, 16)
        ts(A("OF"), A("tmB", 15, 128, 16), 10.0, O.add)
        n = 256 - 64 * EQS
        for k in range(4 - EQS):
            ts(A("EQ", 64 * k, 64 * k + 64), A("B3", 64, 128), 8256.0, O.add, A("tmB", 15 + 16 * k, 16 + 16 * k), O.is_equal)
        if n:
            tt(A("EQ", 0, n), A("EQ", 0, n), A("B3", 128, 128 + n), O.mult)
            scan(A("SC", 0, n), A("rs64", 0, n), A("EQ", 0, n), 0.0, O.max, O.min)
        mm(A("B1", 0, 64), A("idb"), A("c8256"), True)
        mm(A("B1", 0, 64), A("Cc"), A("Pd"), False)
        act(A("mk"), A("B1", 0, 64), F.Sign, A("bM"))
        if EQS:
            for k in range(EQS):
                mm(A("B2", 64 * k, 64 * k + 64), A("Cq"), A("Pd"), k == 0)
            for k in range(EQS):
                c = 15 + 16 * (4 - EQS + k)
                act(A("AD", 64 * k, 64 * k + 64), A("B1", 0, 64), F.Abs, A("tmB", c, c + 1), -1.0)
                mm(A("B2", 64 * k, 64 * k + 64), A("i22"), A("AD", 64 * k, 64 * k + 64), False)
            scan(A("SC", n, 256), A("rs64", n, 256), A("B2", 0, 256 - n), 0.0, O.max, O.min)
        tt(A("win"), A("SC", 63, 256, 64), A("tmB", 143, 192, 16), O.is_gt)
        mm(A("B1", 0, 4), A("idb"), A("Jc", 0, 4), True)
        mm(A("B1", 0, 4), A("idb"), A("n194"), False)
        mm(A("B1", 0, 4), A("tB"), A("win"), False)
        mm(A("B4", 0, 1), A("idb"), A("Jc", 4, 5), True)
        for k in range(4):
            mm(A("B1", k, k + 1), A("Mk", 128 * k, 128 * k + 128), A("win", k, k + 1), False)
            if k:
                mm(A("B1", k, 4), A("BM"), A("win", 0, 4 - k), False)
            mm(A("B4", 0, 1), A("BM"), A("win", k, k + 1), False)
        ts(A("mC"), A("cvec"), A("B4", 0, 1), O.mult)
        remote("lC%d" % t, [(rank ^ 1, eP, A("mC"), A(C, 0, 4), "cP%d" % t), (rank ^ 4, eT, A("mC"), A(C, 4, 8), "cT%d" % t)])
        ts(A("pos"), A("B1", 0, 4), 2.0 if TWO else 194.0, O.add)
        tt(A("t0"), sW, A("B1", 0, 4), O.subtract)
        act(A("UG", 0, 64), IX(A("Urep", 8), A("OF", 0, 4)), F.Copy)
        mm(A("B6", 0, 64), A("idb"), A("mB", 0, 64), True)
        mm(A("B6", 0, 64), A("rself"), A("UG", 0, 64), False)
        r1 = wrap("u1B", A("B6", 0, 64))
        ts(A("OF2"), r1, 10.0, O.add, 8193.0, O.min)
        act(A("UG", 64, 128), IX(A("Urep"), A("OF2")), F.Copy)
        mm(A("B7", 0, 64), A("idb"), A("mB", 0, 64), True)
        mm(A("B7", 0, 64), A("rself"), A("UG", 64, 128), False)
        r2 = wrap("u2B", A("B7", 0, 64))
        cp(A("OFX", 0, 4), r1)
        cp(A("OFX", 4, 8), r2)
        act(A("XG", 64, 128), IX(A("X"), A("OFX", 0, 4)), F.Copy, None, -1.0)
        act(A("XG", 128, 192), IX(A("X"), A("OFX", 4, 8)), F.Copy, None, -1.0)
        act(A("XG", 0, 64), IX(A("X"), A("OF", 0, 4)), F.Copy, None, -1.0)
        mm(A("B2", 0, 64), A("idb"), A("n1k"), True)
        mm(A("B2", 0, 64), A("rselb"), A("XG", 0, 64), False)
        tt(A("XP"), A("XG", 0, 64), A("B2", 0, 64), O.min)
        act(A("XG", 192, 256), IX(A(Q, QG, QG + 512), A("OF", 4, 8)), F.Copy)
        ts(A("XP"), A("XP"), -255.0, O.max)
        sct(A("mT", 0, 1600), A("pos"), A("XG", 64, 128))
        sct(A("mT", 64, 1664), A("pos"), A("XG", 128, 192))
        R = "R%d" % t if TWO else Q
        if FUSE:
            sct(A("mP", 64), A("pos"), A("XP"))
            remote("lT%d" % t, [(rank ^ 4, eT, A("mT", 0, 128), A(R, 128, 256), "aT%d" % t), (rank ^ 1, eP, A("mP", 0, 128), A(R, 0, 128), "aP%d" % t)])
        else:
            remote("lT%d" % t, [(rank ^ 4, eT, A("mT", 0, 128), A(R, 128, 256), "aT%d" % t)])
            sct(A("mP", 64), A("pos"), A("XP"))
            remote("lP%d" % t, [(rank ^ 1, eP, A("mP", 64, 128), A(R, 64, 128), "aP%d" % t)])
        consume(t, cW, r2)
        sct(A(Q, QG + 512, QG + 512 + 1600), A("pos"), A("XG", 192, 256))
        behind("HH", 1)

    def merge(t):
        Q, C = "Q%d" % t, "C%d" % t
        nP, dP, nT, dT, n2 = A(C, 0, 1), A(C, 1, 2), A(C, 4, 5), A(C, 5, 6), A(C, 6, 7)
        R = "R%d" % t if TWO else Q
        t1 = "t0" if TWO else "t1"
        if not TWO:
            ts(A("t1"), A("t0"), nP, O.add, n2, O.add)
        ts(A("h16"), A(t1), M16, O.add, M16, O.subtract)
        if LLS:
            tt(A("dl"), A("h16"), A(t1), O.subtract)
        out = A("B3", 0, 32)
        mm(out, A("idb"), A("B16"), True)
        for k in range(4):
            h, ll, ee = A("h16", k, k + 1), A("LL", 128 * k, 128 * k + 128), A("EE", 32 * k, 32 * k + 32)
            act(A("SS", 32 * k, 32 * k + 32), A("nB16"), F.Sign, h)
            mm(out, A("nBMh"), A("SS", 32 * k, 32 * k + 32), False)
            if k in LLS:
                act(ll, A("Rh"), F.Sign, A("dl", k, k + 1))
                ts(ee, A("B16"), h, O.is_equal, 0.5, O.mult)
                mm(out, o128, ee, False)
            else:
                ts(ll, A("Rp"), h, O.add, A(t1, k, k + 1), O.is_ge)
                ts(ee, A("B16"), h, O.is_equal)
            mm(out, ll, ee, False)
        if TWO:
            ts(A("MJ"), out, A("r32"), O.add, A("mC", 0, 1), O.add)
            if OV:
                cp(A(R, 256, 256 + 16 * OV), IX(A(Q, QG, QW), A("MJ", 0, OV)))
            act(A(R, 256 + 16 * OV, 768), IX(A(Q, QG, QW), A("MJ", OV, 32)), F.Copy)
            out = A("B4", 32, 64)
            mm(out, A("idb"), A("B16"), True)
        ts(A("S1", 0, 32), A("iW", 0, 32), nP, O.is_ge, dP, O.mult)
        behind("HH", 2)
        ts(A("S1", 32, 64), A("iW", 32, 64), nP, O.subtract, nT, O.is_ge)
        behind("HH", 2)
        ts(A("S1", 64, 96), A("iW", 64, 96), nP, O.subtract, n2, O.is_ge)
        behind("HH", 2)
        act(A("dT"), A("idb"), F.Copy, None, dT)
        mm(out, A("idb"), A("S1", 0, 32), False)
        mm(out, A("dT"), A("S1", 32, 64), False)
        mm(out, A("dT"), A("S1", 64, 96), False)
        if TWO:
            ts(A("MI"), out, A("rcol"), O.add)
        else:
            ts(A("MI"), out, A("r32"), O.add, A("mC", 0, 1), O.add)
        win = A(R, 64, 768)
        a, b = IX(win, A("MI", 0, 16)), IX(win, A("MI", 16, 32))
        if t < RO - 1:
            if MV:
                cp(A("Q%d" % (t + 1), QG, QG + 16 * MV), IX(win, A("MI", 0, MV)))
                behind("xc", 4)
            act(A("Q%d" % (t + 1), QG + 16 * MV, QG + 512), IX(win, A("MI", MV, 32)), F.Copy)
        else:
            ts(A("Gn", 0, 256), a, 255.0, O.add)
            act(A("Gn", 256, 512), b, F.Identity, 255.0)
            dma(hbm(T.yg[:, :]), A("Gn"))

    consts()
    for t in range(RO):
        seen.clear()
        weights(t)
        lists(t)
        utable(t)
        if t == RO - 1:
            for k in range(3):
                mm(A("B7"), A("idb"), A("SG", k * 512, k * 512 + 512), k == 0)
            act(A("Z4"), A("B7"), F.Identity, 2.5, -0.5)
        gathers(t)
        choose()
        give(t)
        merge(t)

    if "order" not in _order:
        _order["order"] = _lay_out(ops)
    order = _order["order"]
    place = {i: k for k, i in enumerate(order)}
    count, done = {}, {}
    known = {q: {} for q in queues}
    for i in order:
        o = ops[i]
        q = o["q"]
        if q == "r":
            count[o["sem"]] = -o["inc"]
            done[i] = (o["sem"], -o["inc"], {})
            continue
        w = {}
        for j in o["dep"]:
            if j in o["ord"] or (q == "t" and ops[j]["q"] == "t"):
                continue
            sem, n, snap = done[j]
            if known[q].get(sem, 0) < n and w.get(sem, (0,))[0] < n:
                w[sem] = (n, snap)
        for sem in sorted(w, key=lambda s: -len(w[s][1])):
            n, snap = w[sem]
            if known[q].get(sem, 0) >= n:
                continue
            queues[q].wait_ge(T.sem[sem], n)
            for k in snap:
                known[q][k] = max(snap[k], known[q].get(k, 0))
            known[q][sem] = n
        s = o["sem"]
        r = o["f"](o["grp"] is not None and place[i] == max(place[j] for j in o["grp"] if ops[j]["rows"][0] < o["rows"][1] and o["rows"][0] < ops[j]["rows"][1]))
        if o["inc"] > 0:
            r.then_inc(T.sem[s], o["inc"])
        count[s] = count.get(s, 0) + abs(o["inc"])
        done[i] = (s, count[s], dict(known[q]))
    for s in count:
        if known["g"].get(s, 0) < count[s]:
            g.wait_ge(T.sem[s], count[s])
